import numpy as np
import ml_dtypes


def mxq(x, axis, fmt="e4m3"):
    dtype, down = {"e4m3": (ml_dtypes.float8_e4m3fn, 7), "e5m2": (ml_dtypes.float8_e5m2, 14)}[fmt]
    v = np.moveaxis(np.asarray(x, np.float32).astype(ml_dtypes.bfloat16).astype(np.float64), axis, -1)
    blocks = v.reshape(v.shape[:-1] + (-1, 32))
    amax = np.abs(blocks).max(-1, keepdims=True)
    byte = np.maximum(np.where(amax > 0, np.frexp(amax)[1] - 1 + 127, 0) - down, 1)
    scale = np.exp2(byte - 127.0)
    codes = (blocks / scale).astype(np.float32).astype(dtype).astype(np.float64)
    return np.moveaxis((codes * scale).reshape(v.shape), -1, axis)


WIDE = False


def mx_kscale(k):
    if not WIDE:
        return np.ones(k)
    levels = np.array([10, -10, 5, -5, 0])
    if k % 512:
        return np.exp2(np.random.permutation(np.resize(levels, k // 32))).repeat(32)
    a = np.empty((k // 512, 16))
    for p in range(k // 512):
        a[p, :8] = np.random.permutation(np.resize(levels, 8))
        for g in range(8):
            far = levels[np.abs(levels - a[p, g]) >= 10]
            a[p, g + 8] = far[np.random.randint(len(far))]
    return np.exp2(a.ravel()).repeat(32)


def f64(x):
    return np.asarray(x).astype(np.float64)


def striped(idx):
    return np.tile(idx.reshape(-1, 16).T, (8, 1)).astype(np.uint16)


def unstriped(offs):
    return offs[:16].T.reshape(-1).astype(np.int64)


def striped8(idx):
    return np.concatenate([x.reshape(-1, 16).T for x in idx]).astype(np.uint16)


def runs(offs, k):
    lists = np.stack([offs[16 * r : 16 * r + 16].T.reshape(-1) for r in range(8)]).astype(np.int64)
    return lists[np.arange(k) % 512 // 64]


def pack_weight(w):
    k, n = w.shape
    w = f64(np.asarray(w, np.float32).astype(ml_dtypes.bfloat16)).reshape(k // 32, 32, n)
    amax = np.abs(w).max(1)
    byte = np.clip(np.where(amax > 0, np.frexp(amax)[1] - 1 + 127 - 7, 1), 1, 254)
    scaled = (w * np.exp2(127.0 - byte)[:, None, :]).reshape(k, n).astype(np.float32)
    words = np.ascontiguousarray(scaled.reshape(k // 512, 128, 4, n).transpose(0, 1, 3, 2)).astype(ml_dtypes.float8_e4m3fn).view(np.uint8)
    return words, np.ascontiguousarray(byte.astype(np.uint8).reshape(k // 512, 16, n))


def unpack_weight(words, scales):
    g, p, n, _ = words.shape
    vals = np.ascontiguousarray(words).view(ml_dtypes.float8_e4m3fn).astype(np.float64) * np.repeat(np.exp2(scales.astype(np.float64) - 127.0), 8, axis=1)[..., None]
    return vals.transpose(0, 1, 3, 2).reshape(g * 512, n)


E2M1 = np.array([0.0, 0.5, 1.0, 1.5, 2.0, 3.0, 4.0, 6.0, -0.0, -0.5, -1.0, -1.5, -2.0, -3.0, -4.0, -6.0])


def pack_fp4(w):
    k, n = w.shape
    w = f64(np.asarray(w, np.float32).astype(ml_dtypes.bfloat16)).reshape(k // 32, 32, n)
    amax = np.abs(w).max(1)
    mant, ex = np.frexp(amax / 6.0)
    byte = np.clip(np.where(amax > 0, np.where(mant > 0.5, ex, ex - 1) + 127, 1), 1, 254)
    scaled = (w * np.exp2(127.0 - byte)[:, None, :]).reshape(k, n).astype(np.float32)
    c = np.ascontiguousarray(scaled.reshape(k // 512, 128, 4, n).transpose(0, 1, 3, 2)).astype(ml_dtypes.float4_e2m1fn).view(np.uint8) & 0xF
    words = (c[..., 0::2] | (c[..., 1::2] << 4)).reshape(k // 512, 128, 2 * n)
    return np.ascontiguousarray(words), np.ascontiguousarray(byte.astype(np.uint8).reshape(k // 512, 16, n))


def unpack_fp4(words, scales):
    g, _, n = scales.shape
    words = np.ascontiguousarray(words).reshape(g, 128, n, 2)
    nib = np.empty((g, 128, n, 4), np.uint8)
    nib[..., 0::2] = words & 0xF
    nib[..., 1::2] = words >> 4
    vals = E2M1[nib] * np.repeat(np.exp2(scales.astype(np.float64) - 127.0), 8, axis=1)[..., None]
    return vals.transpose(0, 1, 3, 2).reshape(g * 512, n)


def planes(y):
    n, m = y.shape
    v = y.astype(np.float32).astype(ml_dtypes.bfloat16).astype(np.float64).reshape(n // 32, 32, m)
    top = np.abs(v).max(1)
    byte = np.clip(np.where(top > 0, np.frexp(top)[1] - 1 + 127 - 7, 1), 1, 254)
    codes = (v * np.exp2(127.0 - byte)[:, None, :]).reshape(n, m).astype(np.float32).astype(ml_dtypes.float8_e4m3fn).view(np.uint8)
    words = codes.reshape(n // 512, 128, 4, m).transpose(0, 1, 3, 2)
    return np.ascontiguousarray(words), np.ascontiguousarray(byte.astype(np.uint8).reshape(n // 512, 16, m))


K, T, S, N, H = 512, 2048, 512, 512, 512
P = 2 ** 7


def setup_inputs():
    n = np.random.standard_normal
    s = mx_kscale(K)[:, None]
    u = mx_kscale(H)
    packed_xT = pack_weight(n((K, T)) * s)
    packed_w1 = pack_fp4(n((K, H)) / np.sqrt(K) / s)
    packed_w4 = pack_fp4(n((H, N)) / np.sqrt(H) / u[:, None])
    return {
        "x_words": packed_xT[0],
        "x_scales": packed_xT[1],
        "w1_words": packed_w1[0],
        "w1_scales": packed_w1[1],
        "w2": (n((K, H)) / np.sqrt(K) / s * u).astype(np.float32),
        "w3": (n((K, H)) / np.sqrt(K) / s * u).astype(np.float32),
        "dir1": np.tile(np.random.uniform(-1, 1, S), (P, 1)).astype(np.float32),
        "dir2": np.tile(np.random.uniform(-1, 1, S), (P, 1)).astype(np.float32),
        "w4_words": packed_w4[0],
        "w4_scales": packed_w4[1],
        "offs": striped(np.random.permutation(T)[:S]),
        "p1": striped8(np.stack([np.random.permutation(S) for _ in range(8)])),
        "p2": striped8(np.stack([np.random.permutation(S) for _ in range(8)])),
    }


def reference(x_words, x_scales, w1_words, w1_scales, w2, w3, dir1, dir2, w4_words, w4_scales, offs, p1, p2):
    xq = unpack_weight(x_words, x_scales)[:, unstriped(offs)]
    y = unpack_fp4(w1_words, w1_scales).T @ xq
    e = mxq(f64(w2), 0, "e4m3").T @ xq
    q = mxq(f64(w3), 0, "e4m3").T @ xq
    z = (y[np.arange(H)[:, None], runs(p1, H)]) * (e[np.arange(H)[:, None], runs(p1, H)]) + (q[np.arange(H)[:, None], runs(p1, H)]) * f64(dir1)[:1] + (y[np.arange(H)[:, None], runs(p2, H)]) * (e[np.arange(H)[:, None], runs(p2, H)]) + (q[np.arange(H)[:, None], runs(p2, H)]) * f64(dir2)[:1]
    out_0 = unpack_fp4(w4_words, w4_scales).T @ mxq(z, 0, "e4m3")
    return (out_0,) + planes(out_0)

@@ -1,0 +1,217 @@
+from contextlib import ExitStack
+
+import concourse.mybir as mybir
+
+K, T, S, H, N = 512, 2048, 512, 512, 512
+FLOPS = 4 * 2 * 512 * 512 * 512
+
+F32 = mybir.dt.float32
+BF16 = mybir.dt.bfloat16
+I32 = mybir.dt.int32
+U32 = mybir.dt.uint32
+U16 = mybir.dt.uint16
+U8 = mybir.dt.uint8
+FP8X4 = mybir.dt.float8_e4m3fn_x4
+FP4X4 = mybir.dt.float4_e2m1fn_x4
+MULT = mybir.AluOpType.mult
+ADD = mybir.AluOpType.add
+
+P = 128
+PACK = 4
+HALF = 256
+SLICES = ((0, 256), (256, 128), (384, 128))
+
+
+def tile_picked_painn8_none_po_kernel(
+    tc, x_words, x_scales, w1_words, w1_scales, w2, w3, dir1, dir2, w4_words, w4_scales, offs, p1, p2, out_0, out_1, out_2
+):
+    nc = tc.nc
+    with ExitStack() as ctx:
+        keep = ctx.enter_context(tc.tile_pool(name="keep", bufs=1))
+        first = ctx.enter_context(tc.psum_pool(name="first", bufs=6))
+        last = ctx.enter_context(tc.psum_pool(name="last", bufs=2))
+
+        def sb(shape, dtype, name, tag=None):
+            return keep.tile(shape, dtype, name=name, tag=tag or name, align_bytes=64)
+
+        def load_scale_rows(queue, plane, rows):
+            for r in range(4):
+                queue.dma_start(out=plane[r:P:32, :].bitcast(I32), in_=rows[0, r:16:4, :].bitcast(I32))
+
+        offs_sb = keep.tile([P, S // 16], U16, name="offs_sb")
+        p1_sb = keep.tile([P, S // 16], U16, name="p1_sb")
+        p2_sb = keep.tile([P, S // 16], U16, name="p2_sb")
+        xw = sb([P, T], I32, "xw")
+        xs = sb([P, T], U8, "xs")
+        w1w = sb([P, 2 * H], U8, "w1w")
+        w4w = sb([P, 2 * N], U8, "w4w")
+        w1s = sb([P, H], U8, "w1s")
+        w4s = sb([P, N], U8, "w4s")
+        o_scales = sb([P, S], U8, "o_scales")
+        o_codes = sb([P, S], I32, "o_codes")
+        d1 = sb([P, S], F32, "d1")
+        d2 = sb([P, S], F32, "d2")
+        w3_raw = [sb([P, PACK, HALF], F32, "w3_raw%d" % h) for h in range(2)]
+        w2_raw = sb([P, PACK, H], F32, "w2_raw")
+
+        nc.vector.memset(xs[:].bitcast(I32), 0)
+        nc.gpsimd.memset(w1s[:].bitcast(I32), 0)
+        nc.gpsimd.memset(w4s[:].bitcast(I32), 0)
+        nc.vector.memset(o_scales[:].bitcast(I32), 0)
+
+        nc.sync.dma_start(offs_sb[:], offs)
+        nc.sync.dma_start(out=w1w[:].bitcast(I32), in_=w1_words[0].bitcast(I32))
+        load_scale_rows(nc.sync, xs, x_scales)
+        nc.sync.dma_start(out=w4w[:].bitcast(I32), in_=w4_words[0].bitcast(I32))
+        nc.sync.dma_start(out=xw[:], in_=x_words[0].rearrange("p n t -> p (n t)").bitcast(I32))
+        w3_rows = w3.rearrange("(p j) c -> p j c", j=PACK)
+        for h in range(2):
+            nc.sync.dma_start(out=w3_raw[h][:], in_=w3_rows[:, :, h * HALF : (h + 1) * HALF])
+        nc.sync.dma_start(p1_sb[:], p1)
+        nc.sync.dma_start(out=d1[:], in_=dir1)
+        nc.sync.dma_start(p2_sb[:], p2)
+        nc.sync.dma_start(out=d2[:], in_=dir2)
+        nc.sync.dma_start(out=w2_raw[:], in_=w2.rearrange("(p j) c -> p j c", j=PACK))
+        load_scale_rows(nc.gpsimd, w1s, w1_scales)
+        load_scale_rows(nc.gpsimd, w4s, w4_scales)
+
+        def deal_words(words, name):
+            dealt = sb([P, 2 * H], U8, name)
+            nc.vector.tensor_copy(
+                out=dealt[:].rearrange("p (t m b) -> p t m b", t=PACK, b=2),
+                in_=words[:].rearrange("p (m t b) -> p t m b", t=PACK, b=2),
+            )
+            return dealt
+
+        def deal_scales(plane, name):
+            dealt = sb([P, H], U8, name)
+            nc.vector.tensor_copy(
+                out=dealt[:].rearrange("p (t m) -> p t m", t=PACK),
+                in_=plane[:].rearrange("p (m t) -> p t m", t=PACK),
+            )
+            return dealt
+
+        xq_s = sb([P, S], U8, "xq_s")
+        xq = sb([P, S], U32, "xq")
+        w1w_d = deal_words(w1w, "w1w_d")
+        nc.vector.tensor_copy(xq_s[:], xs[:].indirect(offs_sb[:]))
+        nc.vector.tensor_copy(xq[:], xw[:].bitcast(U32).indirect(offs_sb[:]))
+        w4w_d = deal_words(w4w, "w4w_d")
+        w1s_d = deal_scales(w1s, "w1s_d")
+
+        def round_and_deal(copy, grouped, raw, m0, m1):
+            copy(
+                out=grouped[:].rearrange("p (t m j) -> p m t j", t=PACK, j=PACK)[:, m0:m1],
+                in_=raw.rearrange("p j (m t) -> p m t j", t=PACK),
+            )
+
+        w3_b = sb([P, PACK * H], BF16, "w3_b")
+        round_and_deal(nc.scalar.copy, w3_b, w3_raw[0][:], 0, 64)
+        round_and_deal(nc.vector.tensor_copy, w3_b, w3_raw[1][:], 64, 128)
+        w3_c = sb([P, H], U32, "w3_c")
+        w3_s = sb([P, H], U8, "w3_s")
+        for t in range(PACK):
+            cols = slice(t * P, (t + 1) * P)
+            nc.vector.quantize_mx(
+                out=w3_c[:, cols].bitcast(FP8X4), scales=w3_s[:, cols], in_=w3_b[:, t * PACK * P : (t + 1) * PACK * P]
+            )
+        w4s_d = deal_scales(w4s, "w4s_d")
+
+        def product(lhsT, lhsT_scale, name):
+            acc = first.tile([P, S], F32, name=name, tag="first")
+            nc.tensor.matmul_mx(
+                out=acc[:], lhsT=lhsT, lhsT_scale=lhsT_scale, rhs=xq[:].bitcast(FP8X4), rhs_scale=xq_s[:], start=True, stop=True
+            )
+            return acc
+
+        q_sb = []
+        for t in range(PACK):
+            cols = slice(t * P, (t + 1) * P)
+            acc = product(w3_c[:, cols].bitcast(FP8X4), w3_s[:, cols], "q%d" % t)
+            q_t = sb([P, S], F32, "q_sb%d" % t)
+            nc.scalar.copy(out=q_t[:], in_=acc[:])
+            q_sb.append(q_t)
+        y_sb = []
+        for t in range(PACK):
+            acc = product(w1w_d[:, 2 * t * P : 2 * (t + 1) * P].bitcast(FP4X4), w1s_d[:, t * P : (t + 1) * P], "y%d" % t)
+            y_t = sb([P, S], F32, "y_sb%d" % t)
+            nc.scalar.copy(out=y_t[:], in_=acc[:])
+            y_sb.append(y_t)
+
+        w2_b = sb([P, PACK * H], BF16, "w2_b", tag="hold")
+        for h in range(2):
+            round_and_deal(nc.scalar.copy, w2_b, w2_raw[:, :, h * HALF : (h + 1) * HALF], h * 64, (h + 1) * 64)
+        w2_c = sb([P, H], U32, "w2_c")
+        w2_s = sb([P, H], U8, "w2_s")
+
+        qd = []
+
+        def directed(t):
+            both = sb([P, 2, S], F32, "qd%d" % t, tag="hold" if t == PACK - 1 else None)
+            for h in range(2):
+                cols = slice(h * HALF, (h + 1) * HALF)
+                ent = slice(h * HALF // 16, (h + 1) * HALF // 16)
+                nc.vector.tensor_tensor(both[:, 0, cols], q_sb[t][:].indirect(p1_sb[:, ent]), d1[:, cols], MULT)
+                nc.vector.tensor_tensor(both[:, 1, cols], q_sb[t][:].indirect(p2_sb[:, ent]), d2[:, cols], MULT)
+            qd.append(both)
+
+        for t in range(PACK - 1):
+            directed(t)
+        nc.vector.quantize_mx(out=w2_c[:].bitcast(FP8X4), scales=w2_s[:], in_=w2_b[:])
+        directed(PACK - 1)
+
+        ye = []
+        for t in range(PACK):
+            cols = slice(t * P, (t + 1) * P)
+            acc = product(w2_c[:, cols].bitcast(FP8X4), w2_s[:, cols], "e%d" % t)
+            ye_t = sb([P, S], F32, "ye%d" % t)
+            nc.vector.tensor_tensor(ye_t[:], acc[:], y_sb[t][:], MULT)
+            ye.append(ye_t)
+
+        out_rows = out_0.rearrange("(p t) j -> p t j", t=PACK)
+        code_rows = out_1[0].rearrange("p n t -> p (n t)").bitcast(I32)
+        for s, (j0, n) in enumerate(SLICES):
+            cols = slice(j0, j0 + n)
+            ent = slice(j0 // 16, (j0 + n) // 16)
+            m1 = sb([P, PACK, n], F32, "m1_%d" % s)
+            m2 = sb([P, PACK, n], F32, "m2_%d" % s)
+            for t in range(PACK):
+                nc.vector.tensor_tensor(m1[:, t, :], ye[t][:].indirect(p1_sb[:, ent]), qd[t][:, 0, cols], ADD)
+                nc.vector.tensor_tensor(m2[:, t, :], ye[t][:].indirect(p2_sb[:, ent]), qd[t][:, 1, cols], ADD)
+            z_b = sb([P, PACK * n], BF16, "z_b%d" % s)
+            nc.vector.tensor_tensor(
+                z_b[:].rearrange("p (c i t) -> p c t i", i=4, t=PACK),
+                m1[:].rearrange("p t (c i) -> p c t i", i=4),
+                m2[:].rearrange("p t (c i) -> p c t i", i=4),
+                ADD,
+            )
+            z_c = sb([P, n], U32, "z_c%d" % s)
+            z_s = sb([P, n], U8, "z_s%d" % s)
+            nc.vector.quantize_mx(out=z_c[:].bitcast(FP8X4), scales=z_s[:], in_=z_b[:])
+            o_f = sb([P, PACK, n], F32, "o_f%d" % s)
+            for u in range(2):
+                acc = last.tile([P, 2, n], F32, name="o%d_%d" % (s, u), tag="last")
+                for e in range(2):
+                    t = 2 * u + e
+                    nc.tensor.matmul_mx(
+                        out=acc[:, e, :],
+                        lhsT=w4w_d[:, 2 * t * P : 2 * (t + 1) * P].bitcast(FP4X4),
+                        lhsT_scale=w4s_d[:, t * P : (t + 1) * P],
+                        rhs=z_c[:].bitcast(FP8X4),
+                        rhs_scale=z_s[:],
+                        start=True,
+                        stop=True,
+                    )
+                nc.scalar.copy(out=o_f[:, 2 * u : 2 * u + 2, :], in_=acc[:])
+            nc.sync.dma_start(out=out_rows[:, :, cols], in_=o_f[:])
+            o_b = sb([P, PACK * n], BF16, "o_b%d" % s)
+            copy = nc.vector.tensor_copy if s == len(SLICES) - 1 else nc.scalar.copy
+            copy(
+                out=o_b[:].rearrange("p (c i t) -> p c t i", i=4, t=PACK),
+                in_=o_f[:].rearrange("p t (c i) -> p c t i", i=4),
+            )
+            nc.vector.quantize_mx(out=o_codes[:, cols].bitcast(FP8X4), scales=o_scales[:, cols], in_=o_b[:])
+            nc.sync.dma_start(out=code_rows[:, cols], in_=o_codes[:, cols])
+        for r in range(4):
+            queue = nc.scalar if r % 2 else nc.sync
+            queue.dma_start(out=out_2[0, r:16:4, :].bitcast(I32), in_=o_scales[r:P:32, :].bitcast(I32))

@@ -1,6 +1,7 @@
 from contextlib import ExitStack
 
 import concourse.mybir as mybir
+from concourse.masks import make_identity
 
 K, T, S, H, N = 512, 2048, 512, 512, 512
 FLOPS = 4 * 2 * 512 * 512 * 512
@@ -28,8 +29,10 @@ def tile_picked_painn8_none_po_kernel(
     nc = tc.nc
     with ExitStack() as ctx:
         keep = ctx.enter_context(tc.tile_pool(name="keep", bufs=1))
-        first = ctx.enter_context(tc.psum_pool(name="first", bufs=6))
-        last = ctx.enter_context(tc.psum_pool(name="last", bufs=2))
+        psum = ctx.enter_context(tc.psum_pool(name="psum", bufs=1))
+
+        def bank(b, shape, name):
+            return psum.tile(shape, F32, name=name, tag="bank%d" % b)
 
         def sb(shape, dtype, name, tag=None):
             return keep.tile(shape, dtype, name=name, tag=tag or name, align_bytes=64)
@@ -58,22 +61,27 @@ def tile_picked_painn8_none_po_kernel(
         nc.gpsimd.memset(w1s[:].bitcast(I32), 0)
         nc.gpsimd.memset(w4s[:].bitcast(I32), 0)
         nc.vector.memset(o_scales[:].bitcast(I32), 0)
+        q_sb = [sb([P, 2 * S], F32, "q_sb%d" % t) for t in range(PACK)]
+        for t in range(PACK):
+            nc.gpsimd.memset(q_sb[t][:, S:], 0.0)
+        ident = sb([P, P], F32, "ident")
+        make_identity(nc, ident[:])
 
         nc.sync.dma_start(offs_sb[:], offs)
         nc.sync.dma_start(out=w1w[:].bitcast(I32), in_=w1_words[0].bitcast(I32))
         load_scale_rows(nc.sync, xs, x_scales)
-        nc.sync.dma_start(out=w4w[:].bitcast(I32), in_=w4_words[0].bitcast(I32))
         nc.sync.dma_start(out=xw[:], in_=x_words[0].rearrange("p n t -> p (n t)").bitcast(I32))
         w3_rows = w3.rearrange("(p j) c -> p j c", j=PACK)
         for h in range(2):
             nc.sync.dma_start(out=w3_raw[h][:], in_=w3_rows[:, :, h * HALF : (h + 1) * HALF])
+        nc.sync.dma_start(out=w4w[:].bitcast(I32), in_=w4_words[0].bitcast(I32))
+        load_scale_rows(nc.sync, w1s, w1_scales)
         nc.sync.dma_start(p1_sb[:], p1)
         nc.sync.dma_start(out=d1[:], in_=dir1)
         nc.sync.dma_start(p2_sb[:], p2)
         nc.sync.dma_start(out=d2[:], in_=dir2)
+        load_scale_rows(nc.sync, w4s, w4_scales)
         nc.sync.dma_start(out=w2_raw[:], in_=w2.rearrange("(p j) c -> p j c", j=PACK))
-        load_scale_rows(nc.gpsimd, w1s, w1_scales)
-        load_scale_rows(nc.gpsimd, w4s, w4_scales)
 
         def deal_words(words, name):
             dealt = sb([P, 2 * H], U8, name)
@@ -96,18 +104,17 @@ def tile_picked_painn8_none_po_kernel(
         w1w_d = deal_words(w1w, "w1w_d")
         nc.vector.tensor_copy(xq_s[:], xs[:].indirect(offs_sb[:]))
         nc.vector.tensor_copy(xq[:], xw[:].bitcast(U32).indirect(offs_sb[:]))
-        w4w_d = deal_words(w4w, "w4w_d")
-        w1s_d = deal_scales(w1s, "w1s_d")
 
-        def round_and_deal(copy, grouped, raw, m0, m1):
+        def round_and_deal(copy, grouped, raw, m0, m1, t0=0, t1=PACK):
             copy(
-                out=grouped[:].rearrange("p (t m j) -> p m t j", t=PACK, j=PACK)[:, m0:m1],
-                in_=raw.rearrange("p j (m t) -> p m t j", t=PACK),
+                out=grouped[:].rearrange("p (t m j) -> p m t j", t=PACK, j=PACK)[:, m0:m1, t0:t1],
+                in_=raw.rearrange("p j (m t) -> p m t j", t=PACK)[:, :, t0:t1],
             )
 
         w3_b = sb([P, PACK * H], BF16, "w3_b")
         round_and_deal(nc.scalar.copy, w3_b, w3_raw[0][:], 0, 64)
-        round_and_deal(nc.vector.tensor_copy, w3_b, w3_raw[1][:], 64, 128)
+        round_and_deal(nc.vector.tensor_copy, w3_b, w3_raw[1][:], 64, 128, 0, 1)
+        round_and_deal(nc.scalar.copy, w3_b, w3_raw[1][:], 64, 128, 1, PACK)
         w3_c = sb([P, H], U32, "w3_c")
         w3_s = sb([P, H], U8, "w3_s")
         for t in range(PACK):
@@ -115,25 +122,31 @@ def tile_picked_painn8_none_po_kernel(
             nc.vector.quantize_mx(
                 out=w3_c[:, cols].bitcast(FP8X4), scales=w3_s[:, cols], in_=w3_b[:, t * PACK * P : (t + 1) * PACK * P]
             )
+        w4w_d = deal_words(w4w, "w4w_d")
+        w1s_d = deal_scales(w1s, "w1s_d")
         w4s_d = deal_scales(w4s, "w4s_d")
 
-        def product(lhsT, lhsT_scale, name):
-            acc = first.tile([P, S], F32, name=name, tag="first")
+        def product(lhsT, lhsT_scale, name, b):
+            acc = bank(b, [P, S], name)
             nc.tensor.matmul_mx(
                 out=acc[:], lhsT=lhsT, lhsT_scale=lhsT_scale, rhs=xq[:].bitcast(FP8X4), rhs_scale=xq_s[:], start=True, stop=True
             )
             return acc
 
-        q_sb = []
-        for t in range(PACK):
+        for h in range(2):
+            cols = slice(h * HALF, (h + 1) * HALF)
+            acc = bank(PACK * h, [P, HALF], "q0_%d" % h)
+            nc.tensor.matmul_mx(
+                out=acc[:], lhsT=w3_c[:, :P].bitcast(FP8X4), lhsT_scale=w3_s[:, :P], rhs=xq[:, cols].bitcast(FP8X4), rhs_scale=xq_s[:, cols], start=True, stop=True
+            )
+            nc.scalar.copy(out=q_sb[0][:, cols], in_=acc[:])
+        for t in range(1, PACK):
             cols = slice(t * P, (t + 1) * P)
-            acc = product(w3_c[:, cols].bitcast(FP8X4), w3_s[:, cols], "q%d" % t)
-            q_t = sb([P, S], F32, "q_sb%d" % t)
-            nc.scalar.copy(out=q_t[:], in_=acc[:])
-            q_sb.append(q_t)
+            acc = product(w3_c[:, cols].bitcast(FP8X4), w3_s[:, cols], "q%d" % t, t)
+            nc.scalar.copy(out=q_sb[t][:, :S], in_=acc[:])
         y_sb = []
         for t in range(PACK):
-            acc = product(w1w_d[:, 2 * t * P : 2 * (t + 1) * P].bitcast(FP4X4), w1s_d[:, t * P : (t + 1) * P], "y%d" % t)
+            acc = product(w1w_d[:, 2 * t * P : 2 * (t + 1) * P].bitcast(FP4X4), w1s_d[:, t * P : (t + 1) * P], "y%d" % t, PACK + t)
             y_t = sb([P, S], F32, "y_sb%d" % t)
             nc.scalar.copy(out=y_t[:], in_=acc[:])
             y_sb.append(y_t)
@@ -148,11 +161,8 @@ def tile_picked_painn8_none_po_kernel(
 
         def directed(t):
             both = sb([P, 2, S], F32, "qd%d" % t, tag="hold" if t == PACK - 1 else None)
-            for h in range(2):
-                cols = slice(h * HALF, (h + 1) * HALF)
-                ent = slice(h * HALF // 16, (h + 1) * HALF // 16)
-                nc.vector.tensor_tensor(both[:, 0, cols], q_sb[t][:].indirect(p1_sb[:, ent]), d1[:, cols], MULT)
-                nc.vector.tensor_tensor(both[:, 1, cols], q_sb[t][:].indirect(p2_sb[:, ent]), d2[:, cols], MULT)
+            nc.vector.tensor_tensor(both[:, 0, :], q_sb[t][:].indirect(p1_sb[:]), d1[:], MULT)
+            nc.vector.tensor_tensor(both[:, 1, :], q_sb[t][:].indirect(p2_sb[:]), d2[:], MULT)
             qd.append(both)
 
         for t in range(PACK - 1):
@@ -163,7 +173,7 @@ def tile_picked_painn8_none_po_kernel(
         ye = []
         for t in range(PACK):
             cols = slice(t * P, (t + 1) * P)
-            acc = product(w2_c[:, cols].bitcast(FP8X4), w2_s[:, cols], "e%d" % t)
+            acc = product(w2_c[:, cols].bitcast(FP8X4), w2_s[:, cols], "e%d" % t, t)
             ye_t = sb([P, S], F32, "ye%d" % t)
             nc.vector.tensor_tensor(ye_t[:], acc[:], y_sb[t][:], MULT)
             ye.append(ye_t)
@@ -174,23 +184,44 @@ def tile_picked_painn8_none_po_kernel(
             cols = slice(j0, j0 + n)
             ent = slice(j0 // 16, (j0 + n) // 16)
             m1 = sb([P, PACK, n], F32, "m1_%d" % s)
-            m2 = sb([P, PACK, n], F32, "m2_%d" % s)
+            m2 = sb([P, PACK, n], F32, "m2_%d" % s, tag="z_first" if s == 2 else None)
             for t in range(PACK):
                 nc.vector.tensor_tensor(m1[:, t, :], ye[t][:].indirect(p1_sb[:, ent]), qd[t][:, 0, cols], ADD)
                 nc.vector.tensor_tensor(m2[:, t, :], ye[t][:].indirect(p2_sb[:, ent]), qd[t][:, 1, cols], ADD)
-            z_b = sb([P, PACK * n], BF16, "z_b%d" % s)
-            nc.vector.tensor_tensor(
-                z_b[:].rearrange("p (c i t) -> p c t i", i=4, t=PACK),
-                m1[:].rearrange("p t (c i) -> p c t i", i=4),
-                m2[:].rearrange("p t (c i) -> p c t i", i=4),
-                ADD,
-            )
+            z_b = sb([P, PACK * n], BF16, "z_b%d" % s, tag="z_first" if s == 0 else "z_later")
+            if s == len(SLICES) - 1:
+                nc.vector.tensor_tensor(
+                    z_b[:].rearrange("p (c i t) -> p c t i", i=4, t=PACK),
+                    m1[:].rearrange("p t (c i) -> p c t i", i=4),
+                    m2[:].rearrange("p t (c i) -> p c t i", i=4),
+                    ADD,
+                )
+            else:
+                turned = [bank(4 + b + s, [P, PACK, P], "turned%d_%d" % (s, b)) for b in range(n // P)]
+                for t in range(PACK):
+                    for b in range(n // P):
+                        atoms = slice(b * P, (b + 1) * P)
+                        nc.tensor.matmul(turned[b][:, t, :], m1[:, t, atoms], ident[:], start=True, stop=False, is_transpose=True)
+                        nc.tensor.matmul(turned[b][:, t, :], m2[:, t, atoms], ident[:], start=False, stop=True, is_transpose=True)
+                for b in range(n // P):
+                    pairs = sb([P, 2 * P * 2], BF16, "pairs%d_%d" % (s, b))
+                    nc.scalar.copy(
+                        out=pairs[:].rearrange("a (u p e) -> a u p e", u=2, e=2),
+                        in_=turned[b][:].rearrange("a (u e) p -> a u p e", e=2),
+                    )
+                    back = bank(6 + b - 2 * s, [P, 2, P], "back%d_%d" % (s, b))
+                    for u in range(2):
+                        nc.tensor.transpose(back[:, u, :], pairs[:].bitcast(F32)[:, u * P : (u + 1) * P], ident[:])
+                    nc.scalar.copy(
+                        out=z_b[:].bitcast(F32)[:, 2 * b * P : 2 * (b + 1) * P].rearrange("p (a u) -> p a u", u=2),
+                        in_=back[:].rearrange("p u a -> p a u"),
+                    )
             z_c = sb([P, n], U32, "z_c%d" % s)
             z_s = sb([P, n], U8, "z_s%d" % s)
             nc.vector.quantize_mx(out=z_c[:].bitcast(FP8X4), scales=z_s[:], in_=z_b[:])
             o_f = sb([P, PACK, n], F32, "o_f%d" % s)
             for u in range(2):
-                acc = last.tile([P, 2, n], F32, name="o%d_%d" % (s, u), tag="last")
+                acc = bank((0, 2, 6)[s] + u, [P, 2, n], "o%d_%d" % (s, u))
                 for e in range(2):
                     t = 2 * u + e
                     nc.tensor.matmul_mx(
@@ -205,7 +236,7 @@ def tile_picked_painn8_none_po_kernel(
                 nc.scalar.copy(out=o_f[:, 2 * u : 2 * u + 2, :], in_=acc[:])
             nc.sync.dma_start(out=out_rows[:, :, cols], in_=o_f[:])
             o_b = sb([P, PACK * n], BF16, "o_b%d" % s)
-            copy = nc.vector.tensor_copy if s == len(SLICES) - 1 else nc.scalar.copy
+            copy = nc.vector.tensor_copy if s > 0 else nc.scalar.copy
             copy(
                 out=o_b[:].rearrange("p (c i t) -> p c t i", i=4, t=PACK),
                 in_=o_f[:].rearrange("p t (c i) -> p c t i", i=4),

@@ -135,7 +135,7 @@ def tile_picked_painn8_none_po_kernel(
 
         for h in range(2):
             cols = slice(h * HALF, (h + 1) * HALF)
-            acc = bank(PACK * h, [P, HALF], "q0_%d" % h)
+            acc = bank(7 * h, [P, HALF], "q0_%d" % h)
             nc.tensor.matmul_mx(
                 out=acc[:], lhsT=w3_c[:, :P].bitcast(FP8X4), lhsT_scale=w3_s[:, :P], rhs=xq[:, cols].bitcast(FP8X4), rhs_scale=xq_s[:, cols], start=True, stop=True
             )
@@ -146,7 +146,7 @@ def tile_picked_painn8_none_po_kernel(
             nc.scalar.copy(out=q_sb[t][:, :S], in_=acc[:])
         y_sb = []
         for t in range(PACK):
-            acc = product(w1w_d[:, 2 * t * P : 2 * (t + 1) * P].bitcast(FP4X4), w1s_d[:, t * P : (t + 1) * P], "y%d" % t, PACK + t)
+            acc = product(w1w_d[:, 2 * t * P : 2 * (t + 1) * P].bitcast(FP4X4), w1s_d[:, t * P : (t + 1) * P], "y%d" % t, t)
             y_t = sb([P, S], F32, "y_sb%d" % t)
             nc.scalar.copy(out=y_t[:], in_=acc[:])
             y_sb.append(y_t)
@@ -158,12 +158,18 @@ def tile_picked_painn8_none_po_kernel(
         w2_s = sb([P, H], U8, "w2_s")
 
         qd = []
+        turned = [bank(4 + b, [P, PACK, P], "turned%d" % b) for b in range(3)]
 
         def directed(t):
             both = sb([P, 2, S], F32, "qd%d" % t, tag="hold" if t == PACK - 1 else None)
             nc.vector.tensor_tensor(both[:, 0, :], q_sb[t][:].indirect(p1_sb[:]), d1[:], MULT)
             nc.vector.tensor_tensor(both[:, 1, :], q_sb[t][:].indirect(p2_sb[:]), d2[:], MULT)
             qd.append(both)
+            for b in range(3):
+                for i in range(2):
+                    nc.tensor.matmul(
+                        turned[b][:, t, :], both[:, i, b * P : (b + 1) * P], ident[:], start=t == 0 and i == 0, stop=False, is_transpose=True
+                    )
 
         for t in range(PACK - 1):
             directed(t)
@@ -186,8 +192,12 @@ def tile_picked_painn8_none_po_kernel(
             m1 = sb([P, PACK, n], F32, "m1_%d" % s)
             m2 = sb([P, PACK, n], F32, "m2_%d" % s, tag="z_first" if s == 2 else None)
             for t in range(PACK):
-                nc.vector.tensor_tensor(m1[:, t, :], ye[t][:].indirect(p1_sb[:, ent]), qd[t][:, 0, cols], ADD)
-                nc.vector.tensor_tensor(m2[:, t, :], ye[t][:].indirect(p2_sb[:, ent]), qd[t][:, 1, cols], ADD)
+                if s == len(SLICES) - 1:
+                    nc.vector.tensor_tensor(m1[:, t, :], ye[t][:].indirect(p1_sb[:, ent]), qd[t][:, 0, cols], ADD)
+                    nc.vector.tensor_tensor(m2[:, t, :], ye[t][:].indirect(p2_sb[:, ent]), qd[t][:, 1, cols], ADD)
+                else:
+                    nc.vector.tensor_copy(m1[:, t, :], ye[t][:].indirect(p1_sb[:, ent]))
+                    nc.vector.tensor_copy(m2[:, t, :], ye[t][:].indirect(p2_sb[:, ent]))
             z_b = sb([P, PACK * n], BF16, "z_b%d" % s, tag="z_first" if s == 0 else "z_later")
             if s == len(SLICES) - 1:
                 nc.vector.tensor_tensor(
@@ -197,19 +207,20 @@ def tile_picked_painn8_none_po_kernel(
                     ADD,
                 )
             else:
-                turned = [bank(4 + b + s, [P, PACK, P], "turned%d_%d" % (s, b)) for b in range(n // P)]
                 for t in range(PACK):
                     for b in range(n // P):
                         atoms = slice(b * P, (b + 1) * P)
-                        nc.tensor.matmul(turned[b][:, t, :], m1[:, t, atoms], ident[:], start=True, stop=False, is_transpose=True)
-                        nc.tensor.matmul(turned[b][:, t, :], m2[:, t, atoms], ident[:], start=False, stop=True, is_transpose=True)
+                        for i, term in enumerate((m1, m2)):
+                            nc.tensor.matmul(
+                                turned[j0 // P + b][:, t, :], term[:, t, atoms], ident[:], start=False, stop=t == 3 and i == 1, is_transpose=True
+                            )
                 for b in range(n // P):
                     pairs = sb([P, 2 * P * 2], BF16, "pairs%d_%d" % (s, b))
                     nc.scalar.copy(
                         out=pairs[:].rearrange("a (u p e) -> a u p e", u=2, e=2),
-                        in_=turned[b][:].rearrange("a (u e) p -> a u p e", e=2),
+                        in_=turned[j0 // P + b][:].rearrange("a (u e) p -> a u p e", e=2),
                     )
-                    back = bank(6 + b - 2 * s, [P, 2, P], "back%d_%d" % (s, b))
+                    back = bank((7, 3, 4)[j0 // P + b], [P, 2, P], "back%d_%d" % (s, b))
                     for u in range(2):
                         nc.tensor.transpose(back[:, u, :], pairs[:].bitcast(F32)[:, u * P : (u + 1) * P], ident[:])
                     nc.scalar.copy(
@@ -221,7 +232,7 @@ def tile_picked_painn8_none_po_kernel(
             nc.vector.quantize_mx(out=z_c[:].bitcast(FP8X4), scales=z_s[:], in_=z_b[:])
             o_f = sb([P, PACK, n], F32, "o_f%d" % s)
             for u in range(2):
-                acc = bank((0, 2, 6)[s] + u, [P, 2, n], "o%d_%d" % (s, u))
+                acc = bank((0, 2, 5)[s] + u, [P, 2, n], "o%d_%d" % (s, u))
                 for e in range(2):
                     t = 2 * u + e
                     nc.tensor.matmul_mx(

@@ -20,7 +20,6 @@ ADD = mybir.AluOpType.add
 P = 128
 PACK = 4
 HALF = 256
-SLICES = ((0, 256), (256, 128), (384, 128))
 
 
 def tile_picked_painn8_none_po_kernel(
@@ -67,21 +66,21 @@ def tile_picked_painn8_none_po_kernel(
         ident = sb([P, P], F32, "ident")
         make_identity(nc, ident[:])
 
-        nc.sync.dma_start(offs_sb[:], offs)
-        nc.sync.dma_start(out=w1w[:].bitcast(I32), in_=w1_words[0].bitcast(I32))
-        load_scale_rows(nc.sync, xs, x_scales)
-        nc.sync.dma_start(out=xw[:], in_=x_words[0].rearrange("p n t -> p (n t)").bitcast(I32))
         w3_rows = w3.rearrange("(p j) c -> p j c", j=PACK)
-        for h in range(2):
-            nc.sync.dma_start(out=w3_raw[h][:], in_=w3_rows[:, :, h * HALF : (h + 1) * HALF])
-        nc.sync.dma_start(out=w4w[:].bitcast(I32), in_=w4_words[0].bitcast(I32))
-        load_scale_rows(nc.sync, w1s, w1_scales)
+        nc.sync.dma_start(offs_sb[:], offs)
+        nc.sync.dma_start(out=w3_raw[0][:], in_=w3_rows[:, :, :HALF])
+        load_scale_rows(nc.sync, xs, x_scales)
+        nc.sync.dma_start(out=w1w[:].bitcast(I32), in_=w1_words[0].bitcast(I32))
+        nc.sync.dma_start(out=xw[:], in_=x_words[0].rearrange("p n t -> p (n t)").bitcast(I32))
+        nc.sync.dma_start(out=w3_raw[1][:], in_=w3_rows[:, :, HALF:])
         nc.sync.dma_start(p1_sb[:], p1)
         nc.sync.dma_start(out=d1[:], in_=dir1)
+        nc.sync.dma_start(out=w4w[:].bitcast(I32), in_=w4_words[0].bitcast(I32))
+        load_scale_rows(nc.sync, w1s, w1_scales)
         nc.sync.dma_start(p2_sb[:], p2)
         nc.sync.dma_start(out=d2[:], in_=dir2)
-        load_scale_rows(nc.sync, w4s, w4_scales)
         nc.sync.dma_start(out=w2_raw[:], in_=w2.rearrange("(p j) c -> p j c", j=PACK))
+        load_scale_rows(nc.sync, w4s, w4_scales)
 
         def deal_words(words, name):
             dealt = sb([P, 2 * H], U8, name)
@@ -101,8 +100,8 @@ def tile_picked_painn8_none_po_kernel(
 
         xq_s = sb([P, S], U8, "xq_s")
         xq = sb([P, S], U32, "xq")
-        w1w_d = deal_words(w1w, "w1w_d")
         nc.vector.tensor_copy(xq_s[:], xs[:].indirect(offs_sb[:]))
+        w1w_d = deal_words(w1w, "w1w_d")
         nc.vector.tensor_copy(xq[:], xw[:].bitcast(U32).indirect(offs_sb[:]))
 
         def round_and_deal(copy, grouped, raw, m0, m1, t0=0, t1=PACK):
@@ -124,7 +123,6 @@ def tile_picked_painn8_none_po_kernel(
             )
         w4w_d = deal_words(w4w, "w4w_d")
         w1s_d = deal_scales(w1s, "w1s_d")
-        w4s_d = deal_scales(w4s, "w4s_d")
 
         def product(lhsT, lhsT_scale, name, b):
             acc = bank(b, [P, S], name)
@@ -135,7 +133,7 @@ def tile_picked_painn8_none_po_kernel(
 
         for h in range(2):
             cols = slice(h * HALF, (h + 1) * HALF)
-            acc = bank(7 * h, [P, HALF], "q0_%d" % h)
+            acc = bank(h, [P, HALF], "q0_%d" % h)
             nc.tensor.matmul_mx(
                 out=acc[:], lhsT=w3_c[:, :P].bitcast(FP8X4), lhsT_scale=w3_s[:, :P], rhs=xq[:, cols].bitcast(FP8X4), rhs_scale=xq_s[:, cols], start=True, stop=True
             )
@@ -144,36 +142,36 @@ def tile_picked_painn8_none_po_kernel(
             cols = slice(t * P, (t + 1) * P)
             acc = product(w3_c[:, cols].bitcast(FP8X4), w3_s[:, cols], "q%d" % t, t)
             nc.scalar.copy(out=q_sb[t][:, :S], in_=acc[:])
-        y_sb = []
-        for t in range(PACK):
-            acc = product(w1w_d[:, 2 * t * P : 2 * (t + 1) * P].bitcast(FP4X4), w1s_d[:, t * P : (t + 1) * P], "y%d" % t, t)
-            y_t = sb([P, S], F32, "y_sb%d" % t)
-            nc.scalar.copy(out=y_t[:], in_=acc[:])
-            y_sb.append(y_t)
-
         w2_b = sb([P, PACK * H], BF16, "w2_b", tag="hold")
         for h in range(2):
             round_and_deal(nc.scalar.copy, w2_b, w2_raw[:, :, h * HALF : (h + 1) * HALF], h * 64, (h + 1) * 64)
+        y_sb = sb([P, PACK, S], F32, "y_sb", tag="w2_raw")
+        for t in range(PACK):
+            acc = product(w1w_d[:, 2 * t * P : 2 * (t + 1) * P].bitcast(FP4X4), w1s_d[:, t * P : (t + 1) * P], "y%d" % t, t)
+            nc.scalar.copy(out=y_sb[:, t, :], in_=acc[:])
         w2_c = sb([P, H], U32, "w2_c")
         w2_s = sb([P, H], U8, "w2_s")
 
-        qd = []
-        turned = [bank(4 + b, [P, PACK, P], "turned%d" % b) for b in range(3)]
+        turned = [bank(4 + u, [P, 2, 2, P], "turned%d" % u) for u in range(2)]
+        late = [bank(6 + b, [P, PACK, P], "late%d" % b) for b in range(2)]
+
+        def turn(dst, src, start, stop):
+            nc.tensor.matmul(dst, src, ident[:], start=start, stop=stop, is_transpose=True)
 
         def directed(t):
             both = sb([P, 2, S], F32, "qd%d" % t, tag="hold" if t == PACK - 1 else None)
             nc.vector.tensor_tensor(both[:, 0, :], q_sb[t][:].indirect(p1_sb[:]), d1[:], MULT)
             nc.vector.tensor_tensor(both[:, 1, :], q_sb[t][:].indirect(p2_sb[:]), d2[:], MULT)
-            qd.append(both)
-            for b in range(3):
-                for i in range(2):
-                    nc.tensor.matmul(
-                        turned[b][:, t, :], both[:, i, b * P : (b + 1) * P], ident[:], start=t == 0 and i == 0, stop=False, is_transpose=True
-                    )
+            for i in range(2):
+                for b in range(2):
+                    turn(late[b][:, t, :], both[:, i, (2 + b) * P : (3 + b) * P], t == 0 and i == 0, t == 3 and i == 1)
+                for b in range(2):
+                    turn(turned[t // 2][:, b, t % 2, :], both[:, i, b * P : (b + 1) * P], t % 2 == 0 and i == 0 and b == 0, False)
 
         for t in range(PACK - 1):
             directed(t)
         nc.vector.quantize_mx(out=w2_c[:].bitcast(FP8X4), scales=w2_s[:], in_=w2_b[:])
+        w4s_d = deal_scales(w4s, "w4s_d")
         directed(PACK - 1)
 
         ye = []
@@ -181,58 +179,29 @@ def tile_picked_painn8_none_po_kernel(
             cols = slice(t * P, (t + 1) * P)
             acc = product(w2_c[:, cols].bitcast(FP8X4), w2_s[:, cols], "e%d" % t, t)
             ye_t = sb([P, S], F32, "ye%d" % t)
-            nc.vector.tensor_tensor(ye_t[:], acc[:], y_sb[t][:], MULT)
+            nc.vector.tensor_tensor(ye_t[:], acc[:], y_sb[:, t, :], MULT)
             ye.append(ye_t)
+
+        qd_late = sb([P, PACK, HALF], F32, "qd_late")
+        for b in range(2):
+            flat = sb([P, PACK, P], F32, "flat%d" % b, tag="flat_early" if b == 0 else None)
+            nc.scalar.copy(out=flat[:], in_=late[b][:])
+            again = bank(6 + b, [P, PACK, P], "again%d" % b)
+            for t in range(PACK):
+                nc.tensor.transpose(again[:, t, :], flat[:, t, :], ident[:])
+            nc.scalar.copy(out=qd_late[:, :, b * P : (b + 1) * P], in_=again[:])
 
         out_rows = out_0.rearrange("(p t) j -> p t j", t=PACK)
         code_rows = out_1[0].rearrange("p n t -> p (n t)").bitcast(I32)
-        for s, (j0, n) in enumerate(SLICES):
+
+        def finish(s, j0, n, z_b, banks, interleave):
             cols = slice(j0, j0 + n)
-            ent = slice(j0 // 16, (j0 + n) // 16)
-            m1 = sb([P, PACK, n], F32, "m1_%d" % s)
-            m2 = sb([P, PACK, n], F32, "m2_%d" % s, tag="z_first" if s == 2 else None)
-            for t in range(PACK):
-                if s == len(SLICES) - 1:
-                    nc.vector.tensor_tensor(m1[:, t, :], ye[t][:].indirect(p1_sb[:, ent]), qd[t][:, 0, cols], ADD)
-                    nc.vector.tensor_tensor(m2[:, t, :], ye[t][:].indirect(p2_sb[:, ent]), qd[t][:, 1, cols], ADD)
-                else:
-                    nc.vector.tensor_copy(m1[:, t, :], ye[t][:].indirect(p1_sb[:, ent]))
-                    nc.vector.tensor_copy(m2[:, t, :], ye[t][:].indirect(p2_sb[:, ent]))
-            z_b = sb([P, PACK * n], BF16, "z_b%d" % s, tag="z_first" if s == 0 else "z_later")
-            if s == len(SLICES) - 1:
-                nc.vector.tensor_tensor(
-                    z_b[:].rearrange("p (c i t) -> p c t i", i=4, t=PACK),
-                    m1[:].rearrange("p t (c i) -> p c t i", i=4),
-                    m2[:].rearrange("p t (c i) -> p c t i", i=4),
-                    ADD,
-                )
-            else:
-                for t in range(PACK):
-                    for b in range(n // P):
-                        atoms = slice(b * P, (b + 1) * P)
-                        for i, term in enumerate((m1, m2)):
-                            nc.tensor.matmul(
-                                turned[j0 // P + b][:, t, :], term[:, t, atoms], ident[:], start=False, stop=t == 3 and i == 1, is_transpose=True
-                            )
-                for b in range(n // P):
-                    pairs = sb([P, 2 * P * 2], BF16, "pairs%d_%d" % (s, b))
-                    nc.scalar.copy(
-                        out=pairs[:].rearrange("a (u p e) -> a u p e", u=2, e=2),
-                        in_=turned[j0 // P + b][:].rearrange("a (u e) p -> a u p e", e=2),
-                    )
-                    back = bank((7, 3, 4)[j0 // P + b], [P, 2, P], "back%d_%d" % (s, b))
-                    for u in range(2):
-                        nc.tensor.transpose(back[:, u, :], pairs[:].bitcast(F32)[:, u * P : (u + 1) * P], ident[:])
-                    nc.scalar.copy(
-                        out=z_b[:].bitcast(F32)[:, 2 * b * P : 2 * (b + 1) * P].rearrange("p (a u) -> p a u", u=2),
-                        in_=back[:].rearrange("p u a -> p a u"),
-                    )
             z_c = sb([P, n], U32, "z_c%d" % s)
             z_s = sb([P, n], U8, "z_s%d" % s)
             nc.vector.quantize_mx(out=z_c[:].bitcast(FP8X4), scales=z_s[:], in_=z_b[:])
             o_f = sb([P, PACK, n], F32, "o_f%d" % s)
             for u in range(2):
-                acc = bank((0, 2, 5)[s] + u, [P, 2, n], "o%d_%d" % (s, u))
+                acc = bank(banks + u, [P, 2, n], "o%d_%d" % (s, u))
                 for e in range(2):
                     t = 2 * u + e
                     nc.tensor.matmul_mx(
@@ -247,13 +216,51 @@ def tile_picked_painn8_none_po_kernel(
                 nc.scalar.copy(out=o_f[:, 2 * u : 2 * u + 2, :], in_=acc[:])
             nc.sync.dma_start(out=out_rows[:, :, cols], in_=o_f[:])
             o_b = sb([P, PACK * n], BF16, "o_b%d" % s)
-            copy = nc.vector.tensor_copy if s > 0 else nc.scalar.copy
-            copy(
+            interleave(
                 out=o_b[:].rearrange("p (c i t) -> p c t i", i=4, t=PACK),
                 in_=o_f[:].rearrange("p t (c i) -> p c t i", i=4),
             )
             nc.vector.quantize_mx(out=o_codes[:, cols].bitcast(FP8X4), scales=o_scales[:, cols], in_=o_b[:])
             nc.sync.dma_start(out=code_rows[:, cols], in_=o_codes[:, cols])
+
+        early = sb([P, PACK, 2, HALF], F32, "early", tag="flat_early")
+        back = [bank(3 * b, [P, 2, P], "back%d" % b) for b in range(2)]
+        for t in range(PACK):
+            for i, lists in enumerate((p1_sb, p2_sb)):
+                nc.vector.tensor_copy(early[:, t, i, :], ye[t][:].indirect(lists[:, : HALF // 16]))
+                for b in range(2):
+                    turn(turned[t // 2][:, b, t % 2, :], early[:, t, i, b * P : (b + 1) * P], False, t % 2 == 1 and i == 1 and b == 1)
+            if t % 2 == 1:
+                u = t // 2
+                for b in range(2):
+                    pairs = sb([P, 2 * P], BF16, "pairs%d_%d" % (u, b))
+                    nc.scalar.copy(out=pairs[:].rearrange("a (p e) -> a p e", e=2), in_=turned[u][:, b].rearrange("a e p -> a p e"))
+                    nc.tensor.transpose(back[b][:, u, :], pairs[:].bitcast(F32), ident[:])
+        z_early = sb([P, PACK * HALF], BF16, "z_early", tag="z_first")
+        for b in range(2):
+            nc.scalar.copy(
+                out=z_early[:].bitcast(F32)[:, 2 * b * P : 2 * (b + 1) * P].rearrange("p (a u) -> p a u", u=2),
+                in_=back[b][:].rearrange("p u a -> p a u"),
+            )
+        finish(0, 0, HALF, z_early, 1, nc.scalar.copy)
+
+        m1 = sb([P, PACK, HALF], F32, "m1")
+        for t in range(PACK):
+            nc.vector.tensor_tensor(m1[:, t, :], ye[t][:].indirect(p1_sb[:, HALF // 16 :]), qd_late[:, t, :], ADD)
+        z_late = sb([P, 2, PACK, P], F32, "z_late", tag="z_first")
+        for b in range(2):
+            j0 = HALF + b * P
+            z_f = z_late[:, b]
+            for t in range(PACK):
+                nc.vector.tensor_tensor(
+                    z_f[:, t, :], ye[t][:].indirect(p2_sb[:, j0 // 16 : (j0 + P) // 16]), m1[:, t, b * P : (b + 1) * P], ADD
+                )
+            z_b = sb([P, PACK * P], BF16, "z_b%d" % b)
+            nc.vector.tensor_copy(
+                out=z_b[:].rearrange("p (c i t) -> p c t i", i=4, t=PACK),
+                in_=z_f.rearrange("p t (c i) -> p c t i", i=4),
+            )
+            finish(1 + b, j0, P, z_b, 4 + 2 * b, nc.vector.tensor_copy)
         for r in range(4):
             queue = nc.scalar if r % 2 else nc.sync
             queue.dma_start(out=out_2[0, r:16:4, :].bitcast(I32), in_=o_scales[r:P:32, :].bitcast(I32))

@@ -4,7 +4,7 @@ import concourse.mybir as mybir
 from concourse.masks import make_identity
 
 K, T, S, H, N = 512, 2048, 512, 512, 512
-FLOPS = 4 * 2 * 512 * 512 * 512
+FLOPS = 3 * 2 * K * H * S + 2 * H * N * S
 
 F32 = mybir.dt.float32
 BF16 = mybir.dt.bfloat16
@@ -20,6 +20,9 @@ ADD = mybir.AluOpType.add
 P = 128
 PACK = 4
 HALF = 256
+PER_COLUMN = 16
+QUADRANT = 32
+BLOCKS = K // 32
 
 
 def tile_picked_painn8_none_po_kernel(
@@ -30,19 +33,19 @@ def tile_picked_painn8_none_po_kernel(
         keep = ctx.enter_context(tc.tile_pool(name="keep", bufs=1))
         psum = ctx.enter_context(tc.psum_pool(name="psum", bufs=1))
 
-        def bank(b, shape, name):
-            return psum.tile(shape, F32, name=name, tag="bank%d" % b)
+        def bank(number, shape, name):
+            return psum.tile(shape, F32, name=name, tag="bank%d" % number)
 
         def sb(shape, dtype, name, tag=None):
             return keep.tile(shape, dtype, name=name, tag=tag or name, align_bytes=64)
 
-        def load_scale_rows(queue, plane, rows):
-            for r in range(4):
-                queue.dma_start(out=plane[r:P:32, :].bitcast(I32), in_=rows[0, r:16:4, :].bitcast(I32))
+        def load_scale_rows(plane, rows):
+            for r in range(PACK):
+                nc.sync.dma_start(out=plane[r:P:QUADRANT, :].bitcast(I32), in_=rows[0, r:BLOCKS:PACK, :].bitcast(I32))
 
-        offs_sb = keep.tile([P, S // 16], U16, name="offs_sb")
-        p1_sb = keep.tile([P, S // 16], U16, name="p1_sb")
-        p2_sb = keep.tile([P, S // 16], U16, name="p2_sb")
+        offs_sb = keep.tile([P, S // PER_COLUMN], U16, name="offs_sb")
+        p1_sb = keep.tile([P, S // PER_COLUMN], U16, name="p1_sb")
+        p2_sb = keep.tile([P, S // PER_COLUMN], U16, name="p2_sb")
         xw = sb([P, T], I32, "xw")
         xs = sb([P, T], U8, "xs")
         w1w = sb([P, 2 * H], U8, "w1w")
@@ -59,7 +62,6 @@ def tile_picked_painn8_none_po_kernel(
         nc.vector.memset(xs[:].bitcast(I32), 0)
         nc.gpsimd.memset(w1s[:].bitcast(I32), 0)
         nc.gpsimd.memset(w4s[:].bitcast(I32), 0)
-        nc.vector.memset(o_scales[:].bitcast(I32), 0)
         q_sb = [sb([P, 2 * S], F32, "q_sb%d" % t) for t in range(PACK)]
         for t in range(PACK):
             nc.gpsimd.memset(q_sb[t][:, S:], 0.0)
@@ -69,24 +71,24 @@ def tile_picked_painn8_none_po_kernel(
         w3_rows = w3.rearrange("(p j) c -> p j c", j=PACK)
         nc.sync.dma_start(offs_sb[:], offs)
         nc.sync.dma_start(out=w3_raw[0][:], in_=w3_rows[:, :, :HALF])
-        load_scale_rows(nc.sync, xs, x_scales)
+        load_scale_rows(xs, x_scales)
         nc.sync.dma_start(out=w1w[:].bitcast(I32), in_=w1_words[0].bitcast(I32))
         nc.sync.dma_start(out=xw[:], in_=x_words[0].rearrange("p n t -> p (n t)").bitcast(I32))
         nc.sync.dma_start(out=w3_raw[1][:], in_=w3_rows[:, :, HALF:])
         nc.sync.dma_start(p1_sb[:], p1)
         nc.sync.dma_start(out=d1[:], in_=dir1)
         nc.sync.dma_start(out=w4w[:].bitcast(I32), in_=w4_words[0].bitcast(I32))
-        load_scale_rows(nc.sync, w1s, w1_scales)
+        load_scale_rows(w1s, w1_scales)
         nc.sync.dma_start(p2_sb[:], p2)
         nc.sync.dma_start(out=d2[:], in_=dir2)
         nc.sync.dma_start(out=w2_raw[:], in_=w2.rearrange("(p j) c -> p j c", j=PACK))
-        load_scale_rows(nc.sync, w4s, w4_scales)
+        load_scale_rows(w4s, w4_scales)
 
         def deal_words(words, name):
             dealt = sb([P, 2 * H], U8, name)
             nc.vector.tensor_copy(
-                out=dealt[:].rearrange("p (t m b) -> p t m b", t=PACK, b=2),
-                in_=words[:].rearrange("p (m t b) -> p t m b", t=PACK, b=2),
+                out=dealt[:].rearrange("p (t m byte) -> p t m byte", t=PACK, byte=2),
+                in_=words[:].rearrange("p (m t byte) -> p t m byte", t=PACK, byte=2),
             )
             return dealt
 
@@ -104,16 +106,16 @@ def tile_picked_painn8_none_po_kernel(
         w1w_d = deal_words(w1w, "w1w_d")
         nc.vector.tensor_copy(xq[:], xw[:].bitcast(U32).indirect(offs_sb[:]))
 
-        def round_and_deal(copy, grouped, raw, m0, m1, t0=0, t1=PACK):
+        def round_and_deal(copy, grouped, raw, h, t0=0, t1=PACK):
             copy(
-                out=grouped[:].rearrange("p (t m j) -> p m t j", t=PACK, j=PACK)[:, m0:m1, t0:t1],
+                out=grouped[:].rearrange("p (t m j) -> p m t j", t=PACK, j=PACK)[:, h * P // 2 : (h + 1) * P // 2, t0:t1],
                 in_=raw.rearrange("p j (m t) -> p m t j", t=PACK)[:, :, t0:t1],
             )
 
         w3_b = sb([P, PACK * H], BF16, "w3_b")
-        round_and_deal(nc.scalar.copy, w3_b, w3_raw[0][:], 0, 64)
-        round_and_deal(nc.vector.tensor_copy, w3_b, w3_raw[1][:], 64, 128, 0, 1)
-        round_and_deal(nc.scalar.copy, w3_b, w3_raw[1][:], 64, 128, 1, PACK)
+        round_and_deal(nc.scalar.copy, w3_b, w3_raw[0][:], 0)
+        round_and_deal(nc.vector.tensor_copy, w3_b, w3_raw[1][:], 1, 0, 1)
+        round_and_deal(nc.scalar.copy, w3_b, w3_raw[1][:], 1, 1, PACK)
         w3_c = sb([P, H], U32, "w3_c")
         w3_s = sb([P, H], U8, "w3_s")
         for t in range(PACK):
@@ -124,8 +126,8 @@ def tile_picked_painn8_none_po_kernel(
         w4w_d = deal_words(w4w, "w4w_d")
         w1s_d = deal_scales(w1s, "w1s_d")
 
-        def product(lhsT, lhsT_scale, name, b):
-            acc = bank(b, [P, S], name)
+        def product(lhsT, lhsT_scale, name, number):
+            acc = bank(number, [P, S], name)
             nc.tensor.matmul_mx(
                 out=acc[:], lhsT=lhsT, lhsT_scale=lhsT_scale, rhs=xq[:].bitcast(FP8X4), rhs_scale=xq_s[:], start=True, stop=True
             )
@@ -135,16 +137,22 @@ def tile_picked_painn8_none_po_kernel(
             cols = slice(h * HALF, (h + 1) * HALF)
             acc = bank(h, [P, HALF], "q0_%d" % h)
             nc.tensor.matmul_mx(
-                out=acc[:], lhsT=w3_c[:, :P].bitcast(FP8X4), lhsT_scale=w3_s[:, :P], rhs=xq[:, cols].bitcast(FP8X4), rhs_scale=xq_s[:, cols], start=True, stop=True
+                out=acc[:],
+                lhsT=w3_c[:, :P].bitcast(FP8X4),
+                lhsT_scale=w3_s[:, :P],
+                rhs=xq[:, cols].bitcast(FP8X4),
+                rhs_scale=xq_s[:, cols],
+                start=True,
+                stop=True,
             )
             nc.scalar.copy(out=q_sb[0][:, cols], in_=acc[:])
         for t in range(1, PACK):
             cols = slice(t * P, (t + 1) * P)
             acc = product(w3_c[:, cols].bitcast(FP8X4), w3_s[:, cols], "q%d" % t, t)
             nc.scalar.copy(out=q_sb[t][:, :S], in_=acc[:])
-        w2_b = sb([P, PACK * H], BF16, "w2_b", tag="hold")
+        w2_b = sb([P, PACK * H], BF16, "w2_b")
         for h in range(2):
-            round_and_deal(nc.scalar.copy, w2_b, w2_raw[:, :, h * HALF : (h + 1) * HALF], h * 64, (h + 1) * 64)
+            round_and_deal(nc.scalar.copy, w2_b, w2_raw[:, :, h * HALF : (h + 1) * HALF], h)
         y_sb = sb([P, PACK, S], F32, "y_sb", tag="w2_raw")
         for t in range(PACK):
             acc = product(w1w_d[:, 2 * t * P : 2 * (t + 1) * P].bitcast(FP4X4), w1s_d[:, t * P : (t + 1) * P], "y%d" % t, t)
@@ -159,12 +167,12 @@ def tile_picked_painn8_none_po_kernel(
             nc.tensor.matmul(dst, src, ident[:], start=start, stop=stop, is_transpose=True)
 
         def directed(t):
-            both = sb([P, 2, S], F32, "qd%d" % t, tag="hold" if t == PACK - 1 else None)
+            both = sb([P, 2, S], F32, "qd%d" % t, tag="w2_b" if t == PACK - 1 else None)
             nc.vector.tensor_tensor(both[:, 0, :], q_sb[t][:].indirect(p1_sb[:]), d1[:], MULT)
             nc.vector.tensor_tensor(both[:, 1, :], q_sb[t][:].indirect(p2_sb[:]), d2[:], MULT)
             for i in range(2):
                 for b in range(2):
-                    turn(late[b][:, t, :], both[:, i, (2 + b) * P : (3 + b) * P], t == 0 and i == 0, t == 3 and i == 1)
+                    turn(late[b][:, t, :], both[:, i, (2 + b) * P : (3 + b) * P], t == 0 and i == 0, t == PACK - 1 and i == 1)
                 for b in range(2):
                     turn(turned[t // 2][:, b, t % 2, :], both[:, i, b * P : (b + 1) * P], t % 2 == 0 and i == 0 and b == 0, False)
 
@@ -178,13 +186,18 @@ def tile_picked_painn8_none_po_kernel(
         for t in range(PACK):
             cols = slice(t * P, (t + 1) * P)
             acc = product(w2_c[:, cols].bitcast(FP8X4), w2_s[:, cols], "e%d" % t, t)
-            ye_t = sb([P, S], F32, "ye%d" % t)
-            nc.vector.tensor_tensor(ye_t[:], acc[:], y_sb[:, t, :], MULT)
+            ye_t = sb([P, S], F32, "ye%d" % t, tag="q_sb3" if t == 1 else None)
+            if t == 0:
+                nc.vector.tensor_tensor(ye_t[:], acc[:], y_sb[:, t, :], MULT)
+            else:
+                e_t = sb([P, S], F32, "e_sb%d" % t)
+                nc.scalar.copy(out=e_t[:], in_=acc[:])
+                nc.gpsimd.tensor_tensor(ye_t[:], e_t[:], y_sb[:, t, :], MULT)
             ye.append(ye_t)
 
         qd_late = sb([P, PACK, HALF], F32, "qd_late")
         for b in range(2):
-            flat = sb([P, PACK, P], F32, "flat%d" % b, tag="flat_early" if b == 0 else None)
+            flat = sb([P, PACK, P], F32, "flat%d" % b)
             nc.scalar.copy(out=flat[:], in_=late[b][:])
             again = bank(6 + b, [P, PACK, P], "again%d" % b)
             for t in range(PACK):
@@ -194,18 +207,18 @@ def tile_picked_painn8_none_po_kernel(
         out_rows = out_0.rearrange("(p t) j -> p t j", t=PACK)
         code_rows = out_1[0].rearrange("p n t -> p (n t)").bitcast(I32)
 
-        def finish(s, j0, n, z_b, banks, interleave):
+        def finish(j0, n, z_b, first_bank, interleave):
             cols = slice(j0, j0 + n)
-            z_c = sb([P, n], U32, "z_c%d" % s)
-            z_s = sb([P, n], U8, "z_s%d" % s)
+            z_c = sb([P, n], U32, "z_c%d" % j0)
+            z_s = sb([P, n], U8, "z_s%d" % j0)
             nc.vector.quantize_mx(out=z_c[:].bitcast(FP8X4), scales=z_s[:], in_=z_b[:])
-            o_f = sb([P, PACK, n], F32, "o_f%d" % s)
+            o_f = sb([P, PACK, n], F32, "o_f%d" % j0)
             for u in range(2):
-                acc = bank(banks + u, [P, 2, n], "o%d_%d" % (s, u))
-                for e in range(2):
-                    t = 2 * u + e
+                acc = bank(first_bank + u, [P, 2, n], "o%d_%d" % (j0, u))
+                for odd in range(2):
+                    t = 2 * u + odd
                     nc.tensor.matmul_mx(
-                        out=acc[:, e, :],
+                        out=acc[:, odd, :],
                         lhsT=w4w_d[:, 2 * t * P : 2 * (t + 1) * P].bitcast(FP4X4),
                         lhsT_scale=w4s_d[:, t * P : (t + 1) * P],
                         rhs=z_c[:].bitcast(FP8X4),
@@ -215,52 +228,54 @@ def tile_picked_painn8_none_po_kernel(
                     )
                 nc.scalar.copy(out=o_f[:, 2 * u : 2 * u + 2, :], in_=acc[:])
             nc.sync.dma_start(out=out_rows[:, :, cols], in_=o_f[:])
-            o_b = sb([P, PACK * n], BF16, "o_b%d" % s)
+            o_b = sb([P, PACK * n], BF16, "o_b%d" % j0)
             interleave(
-                out=o_b[:].rearrange("p (c i t) -> p c t i", i=4, t=PACK),
-                in_=o_f[:].rearrange("p t (c i) -> p c t i", i=4),
+                out=o_b[:].rearrange("p (c a t) -> p c t a", a=4, t=PACK),
+                in_=o_f[:].rearrange("p t (c a) -> p c t a", a=4),
             )
             nc.vector.quantize_mx(out=o_codes[:, cols].bitcast(FP8X4), scales=o_scales[:, cols], in_=o_b[:])
             nc.sync.dma_start(out=code_rows[:, cols], in_=o_codes[:, cols])
 
-        early = sb([P, PACK, 2, HALF], F32, "early", tag="flat_early")
-        back = [bank(3 * b, [P, 2, P], "back%d" % b) for b in range(2)]
+        early = sb([P, PACK, 2, HALF], F32, "early")
+        back = [bank(free, [P, 2, P], "back%d" % free) for free in (0, 3)]
         for t in range(PACK):
             for i, lists in enumerate((p1_sb, p2_sb)):
-                nc.vector.tensor_copy(early[:, t, i, :], ye[t][:].indirect(lists[:, : HALF // 16]))
+                nc.vector.tensor_copy(early[:, t, i, :], ye[t][:].indirect(lists[:, : HALF // PER_COLUMN]))
                 for b in range(2):
                     turn(turned[t // 2][:, b, t % 2, :], early[:, t, i, b * P : (b + 1) * P], False, t % 2 == 1 and i == 1 and b == 1)
             if t % 2 == 1:
                 u = t // 2
                 for b in range(2):
                     pairs = sb([P, 2 * P], BF16, "pairs%d_%d" % (u, b))
-                    nc.scalar.copy(out=pairs[:].rearrange("a (p e) -> a p e", e=2), in_=turned[u][:, b].rearrange("a e p -> a p e"))
+                    nc.scalar.copy(
+                        out=pairs[:].rearrange("a (p odd) -> a p odd", odd=2), in_=turned[u][:, b].rearrange("a odd p -> a p odd")
+                    )
                     nc.tensor.transpose(back[b][:, u, :], pairs[:].bitcast(F32), ident[:])
-        z_early = sb([P, PACK * HALF], BF16, "z_early", tag="z_first")
+        z_early = sb([P, PACK * HALF], BF16, "z_early")
         for b in range(2):
             nc.scalar.copy(
                 out=z_early[:].bitcast(F32)[:, 2 * b * P : 2 * (b + 1) * P].rearrange("p (a u) -> p a u", u=2),
                 in_=back[b][:].rearrange("p u a -> p a u"),
             )
-        finish(0, 0, HALF, z_early, 1, nc.scalar.copy)
+        finish(0, HALF, z_early, 1, nc.scalar.copy)
 
-        m1 = sb([P, PACK, HALF], F32, "m1")
+        with_p1 = sb([P, PACK, HALF], F32, "with_p1")
         for t in range(PACK):
-            nc.vector.tensor_tensor(m1[:, t, :], ye[t][:].indirect(p1_sb[:, HALF // 16 :]), qd_late[:, t, :], ADD)
-        z_late = sb([P, 2, PACK, P], F32, "z_late", tag="z_first")
+            nc.vector.tensor_tensor(with_p1[:, t, :], ye[t][:].indirect(p1_sb[:, HALF // PER_COLUMN :]), qd_late[:, t, :], ADD)
+        z_late = sb([P, 2, PACK, P], F32, "z_late", tag="z_early")
         for b in range(2):
             j0 = HALF + b * P
             z_f = z_late[:, b]
             for t in range(PACK):
                 nc.vector.tensor_tensor(
-                    z_f[:, t, :], ye[t][:].indirect(p2_sb[:, j0 // 16 : (j0 + P) // 16]), m1[:, t, b * P : (b + 1) * P], ADD
+                    z_f[:, t, :], ye[t][:].indirect(p2_sb[:, j0 // PER_COLUMN : (j0 + P) // PER_COLUMN]), with_p1[:, t, b * P : (b + 1) * P], ADD
                 )
             z_b = sb([P, PACK * P], BF16, "z_b%d" % b)
             nc.vector.tensor_copy(
-                out=z_b[:].rearrange("p (c i t) -> p c t i", i=4, t=PACK),
-                in_=z_f.rearrange("p t (c i) -> p c t i", i=4),
+                out=z_b[:].rearrange("p (c a t) -> p c t a", a=4, t=PACK),
+                in_=z_f.rearrange("p t (c a) -> p c t a", a=4),
             )
-            finish(1 + b, j0, P, z_b, 4 + 2 * b, nc.vector.tensor_copy)
-        for r in range(4):
+            finish(j0, P, z_b, 4 + 2 * b, nc.vector.tensor_copy)
+        for r in range(PACK):
             queue = nc.scalar if r % 2 else nc.sync
-            queue.dma_start(out=out_2[0, r:16:4, :].bitcast(I32), in_=o_scales[r:P:32, :].bitcast(I32))
+            queue.dma_start(out=out_2[0, r:BLOCKS:PACK, :].bitcast(I32), in_=o_scales[r:P:QUADRANT, :].bitcast(I32))

@@ -16,6 +16,7 @@ FP8X4 = mybir.dt.float8_e4m3fn_x4
 FP4X4 = mybir.dt.float4_e2m1fn_x4
 MULT = mybir.AluOpType.mult
 ADD = mybir.AluOpType.add
+COPY = mybir.ActivationFunctionType.Copy
 
 P = 128
 PACK = 4
@@ -39,9 +40,9 @@ def tile_picked_painn8_none_po_kernel(
         def sb(shape, dtype, name, tag=None):
             return keep.tile(shape, dtype, name=name, tag=tag or name, align_bytes=64)
 
-        def load_scale_rows(plane, rows):
+        def load_scale_rows(plane, rows, first=0):
             for r in range(PACK):
-                nc.sync.dma_start(out=plane[r:P:QUADRANT, :].bitcast(I32), in_=rows[0, r:BLOCKS:PACK, :].bitcast(I32))
+                nc.sync.dma_start(out=plane[first + r : P : QUADRANT, :].bitcast(I32), in_=rows[r:BLOCKS:PACK, :].bitcast(I32))
 
         offs_sb = keep.tile([P, S // PER_COLUMN], U16, name="offs_sb")
         p1_sb = keep.tile([P, S // PER_COLUMN], U16, name="p1_sb")
@@ -50,8 +51,8 @@ def tile_picked_painn8_none_po_kernel(
         xs = sb([P, T], U8, "xs")
         w1w = sb([P, 2 * H], U8, "w1w")
         w4w = sb([P, 2 * N], U8, "w4w")
-        w1s = sb([P, H], U8, "w1s")
-        w4s = sb([P, N], U8, "w4s")
+        ws = sb([P, H], U8, "ws")
+        w4s_d = sb([P, N], U8, "w4s_d")
         o_scales = sb([P, S], U8, "o_scales")
         o_codes = sb([P, S], I32, "o_codes")
         d1 = sb([P, S], F32, "d1")
@@ -60,10 +61,10 @@ def tile_picked_painn8_none_po_kernel(
         w2_raw = sb([P, PACK, H], F32, "w2_raw")
 
         nc.vector.memset(xs[:].bitcast(I32), 0)
-        nc.gpsimd.memset(w1s[:].bitcast(I32), 0)
-        nc.gpsimd.memset(w4s[:].bitcast(I32), 0)
-        q_sb = [sb([P, 2 * S], F32, "q_sb%d" % t) for t in range(PACK)]
-        for t in range(PACK):
+        nc.gpsimd.memset(ws[:].bitcast(I32), 0)
+        nc.gpsimd.memset(w4s_d[:].bitcast(I32), 0)
+        q_sb = [sb([P, 2 * S if t < PACK - 1 else S], F32, "q_sb%d" % t) for t in range(PACK)]
+        for t in range(PACK - 1):
             nc.gpsimd.memset(q_sb[t][:, S:], 0.0)
         ident = sb([P, P], F32, "ident")
         make_identity(nc, ident[:])
@@ -71,24 +72,28 @@ def tile_picked_painn8_none_po_kernel(
         w3_rows = w3.rearrange("(p j) c -> p j c", j=PACK)
         nc.sync.dma_start(offs_sb[:], offs)
         nc.sync.dma_start(out=w3_raw[0][:], in_=w3_rows[:, :, :HALF])
-        load_scale_rows(xs, x_scales)
-        nc.sync.dma_start(out=w1w[:].bitcast(I32), in_=w1_words[0].bitcast(I32))
+        load_scale_rows(xs, x_scales[0])
         nc.sync.dma_start(out=xw[:], in_=x_words[0].rearrange("p n t -> p (n t)").bitcast(I32))
         nc.sync.dma_start(out=w3_raw[1][:], in_=w3_rows[:, :, HALF:])
         nc.sync.dma_start(p1_sb[:], p1)
-        nc.sync.dma_start(out=d1[:], in_=dir1)
+        nc.sync.dma_start(out=w1w[:].bitcast(I32), in_=w1_words[0].bitcast(I32))
         nc.sync.dma_start(out=w4w[:].bitcast(I32), in_=w4_words[0].bitcast(I32))
-        load_scale_rows(w1s, w1_scales)
+        nc.sync.dma_start(out=d1[:], in_=dir1)
+        load_scale_rows(ws, w1_scales[0])
+        load_scale_rows(ws, w4_scales[0], PACK)
         nc.sync.dma_start(p2_sb[:], p2)
         nc.sync.dma_start(out=d2[:], in_=dir2)
         nc.sync.dma_start(out=w2_raw[:], in_=w2.rearrange("(p j) c -> p j c", j=PACK))
-        load_scale_rows(w4s, w4_scales)
+        d_late = [sb([P, 2], F32, "d_late%d" % i) for i in range(2)]
+        with nc.allow_non_contiguous_dma(reason="one direction a partition"):
+            for i, direction in enumerate((dir1, dir2)):
+                nc.sync.dma_start(out=d_late[i][:], in_=direction[0, HALF:].rearrange("(b a) -> a b", a=P))
 
         def deal_words(words, name):
             dealt = sb([P, 2 * H], U8, name)
             nc.vector.tensor_copy(
-                out=dealt[:].rearrange("p (t m byte) -> p t m byte", t=PACK, byte=2),
-                in_=words[:].rearrange("p (m t byte) -> p t m byte", t=PACK, byte=2),
+                out=dealt[:].bitcast(U16).rearrange("p (t m) -> p t m", t=PACK),
+                in_=words[:].bitcast(U16).rearrange("p (m t) -> p t m", t=PACK),
             )
             return dealt
 
@@ -103,7 +108,6 @@ def tile_picked_painn8_none_po_kernel(
         xq_s = sb([P, S], U8, "xq_s")
         xq = sb([P, S], U32, "xq")
         nc.vector.tensor_copy(xq_s[:], xs[:].indirect(offs_sb[:]))
-        w1w_d = deal_words(w1w, "w1w_d")
         nc.vector.tensor_copy(xq[:], xw[:].bitcast(U32).indirect(offs_sb[:]))
 
         def round_and_deal(copy, grouped, raw, h, t0=0, t1=PACK):
@@ -123,8 +127,11 @@ def tile_picked_painn8_none_po_kernel(
             nc.vector.quantize_mx(
                 out=w3_c[:, cols].bitcast(FP8X4), scales=w3_s[:, cols], in_=w3_b[:, t * PACK * P : (t + 1) * PACK * P]
             )
+        w1w_d = deal_words(w1w, "w1w_d")
         w4w_d = deal_words(w4w, "w4w_d")
-        w1s_d = deal_scales(w1s, "w1s_d")
+        w1s_d = deal_scales(ws, "ws_d")
+        for r in range(PACK):
+            nc.sync.dma_start(out=w4s_d[r:P:QUADRANT, :].bitcast(I32), in_=w1s_d[PACK + r : P : QUADRANT, :].bitcast(I32))
 
         def product(lhsT, lhsT_scale, name, number):
             acc = bank(number, [P, S], name)
@@ -153,65 +160,88 @@ def tile_picked_painn8_none_po_kernel(
         w2_b = sb([P, PACK * H], BF16, "w2_b")
         for h in range(2):
             round_and_deal(nc.scalar.copy, w2_b, w2_raw[:, :, h * HALF : (h + 1) * HALF], h)
-        y_sb = sb([P, PACK, S], F32, "y_sb", tag="w2_raw")
+        y_first = sb([P, PACK - 1, S], F32, "y_first", tag="w2_raw")
+        last = sb([P, 2, S], F32, "last")
+        y_sb = [y_first[:, t, :] for t in range(PACK - 1)] + [last[:, 0, :]]
         for t in range(PACK):
             acc = product(w1w_d[:, 2 * t * P : 2 * (t + 1) * P].bitcast(FP4X4), w1s_d[:, t * P : (t + 1) * P], "y%d" % t, t)
-            nc.scalar.copy(out=y_sb[:, t, :], in_=acc[:])
+            nc.scalar.copy(out=y_sb[t], in_=acc[:])
         w2_c = sb([P, H], U32, "w2_c")
         w2_s = sb([P, H], U8, "w2_s")
 
+        def directed(t, n, both):
+            nc.vector.tensor_tensor(both[:, 0, :], q_sb[t][:].indirect(p1_sb[:, : n // PER_COLUMN]), d1[:, :n], MULT)
+            nc.vector.tensor_tensor(both[:, 1, :], q_sb[t][:].indirect(p2_sb[:, : n // PER_COLUMN]), d2[:, :n], MULT)
+            return both
+
         turned = [bank(4 + u, [P, 2, 2, P], "turned%d" % u) for u in range(2)]
-        late = [bank(6 + b, [P, PACK, P], "late%d" % b) for b in range(2)]
+        late = [bank(6 + b, [P, PACK - 1, P], "late%d" % b) for b in range(2)]
 
         def turn(dst, src, start, stop):
             nc.tensor.matmul(dst, src, ident[:], start=start, stop=stop, is_transpose=True)
 
-        def directed(t):
-            both = sb([P, 2, S], F32, "qd%d" % t, tag="w2_b" if t == PACK - 1 else None)
-            nc.vector.tensor_tensor(both[:, 0, :], q_sb[t][:].indirect(p1_sb[:]), d1[:], MULT)
-            nc.vector.tensor_tensor(both[:, 1, :], q_sb[t][:].indirect(p2_sb[:]), d2[:], MULT)
+        for t in range(PACK - 1):
+            both = directed(t, S, sb([P, 2, S], F32, "qd%d" % t))
             for i in range(2):
                 for b in range(2):
-                    turn(late[b][:, t, :], both[:, i, (2 + b) * P : (3 + b) * P], t == 0 and i == 0, t == PACK - 1 and i == 1)
+                    turn(late[b][:, t, :], both[:, i, (2 + b) * P : (3 + b) * P], t == 0 and i == 0, t == PACK - 2 and i == 1)
                 for b in range(2):
                     turn(turned[t // 2][:, b, t % 2, :], both[:, i, b * P : (b + 1) * P], t % 2 == 0 and i == 0 and b == 0, False)
-
-        for t in range(PACK - 1):
-            directed(t)
+        flat = sb([P, 2, PACK + 1, P], F32, "flat")
+        for b in range(2):
+            nc.scalar.copy(out=flat[:, b, : PACK - 1, :], in_=late[b][:])
         nc.vector.quantize_mx(out=w2_c[:].bitcast(FP8X4), scales=w2_s[:], in_=w2_b[:])
-        w4s_d = deal_scales(w4s, "w4s_d")
-        directed(PACK - 1)
-
-        ye = []
+        e_sb = []
         for t in range(PACK):
             cols = slice(t * P, (t + 1) * P)
             acc = product(w2_c[:, cols].bitcast(FP8X4), w2_s[:, cols], "e%d" % t, t)
-            ye_t = sb([P, S], F32, "ye%d" % t, tag="q_sb3" if t == 1 else None)
-            if t == 0:
-                nc.vector.tensor_tensor(ye_t[:], acc[:], y_sb[:, t, :], MULT)
-            else:
-                e_t = sb([P, S], F32, "e_sb%d" % t)
-                nc.scalar.copy(out=e_t[:], in_=acc[:])
-                nc.gpsimd.tensor_tensor(ye_t[:], e_t[:], y_sb[:, t, :], MULT)
+            e_t = sb([P, S], F32, "e_sb%d" % t)[:] if t < PACK - 1 else last[:, 1, :]
+            nc.scalar.copy(out=e_t, in_=acc[:])
+            e_sb.append(e_t)
+        qd3 = sb([P, 2, 2, HALF], F32, "qd3", tag="w2_b")
+        directed(3, HALF, qd3[:, 0])
+        q3_late = qd3[:, 1]
+        for i, lists in enumerate((p1_sb, p2_sb)):
+            nc.vector.tensor_copy(q3_late[:, i, :], q_sb[3][:].indirect(lists[:, HALF // PER_COLUMN :]))
+
+        ye = []
+        for t in range(PACK):
+            ye_t = sb([P, S], F32, "ye%d" % t, tag="d2" if t == 0 else None)
+            nc.gpsimd.tensor_tensor(ye_t[:], e_sb[t], y_sb[t], MULT)
             ye.append(ye_t)
+
+        for i in range(2):
+            for b in range(2):
+                turn(turned[1][:, b, 1, :], qd3[:, 0, i, b * P : (b + 1) * P], False, False)
+        late3 = bank(0, [P, 2, 2, P], "late3")
+        for i in range(2):
+            for b in range(2):
+                nc.tensor.transpose(late3[:, i, b, :], q3_late[:, i, b * P : (b + 1) * P], ident[:])
 
         qd_late = sb([P, PACK, HALF], F32, "qd_late")
         for b in range(2):
-            flat = sb([P, PACK, P], F32, "flat%d" % b)
-            nc.scalar.copy(out=flat[:], in_=late[b][:])
-            again = bank(6 + b, [P, PACK, P], "again%d" % b)
-            for t in range(PACK):
-                nc.tensor.transpose(again[:, t, :], flat[:, t, :], ident[:])
+            for i in range(2):
+                nc.scalar.activation(flat[:, b, PACK - 1 + i, :], late3[:, i, b, :], COPY, scale=d_late[i][:, b : b + 1])
+        for b in range(2):
+            again = bank(3 - 3 * b, [P, PACK, P], "again%d" % b)
+            for t in range(PACK - 1):
+                nc.tensor.transpose(again[:, t, :], flat[:, b, t, :], ident[:])
+            for i in range(2):
+                turn(again[:, PACK - 1, :], flat[:, b, PACK - 1 + i, :], i == 0, i == 1)
             nc.scalar.copy(out=qd_late[:, :, b * P : (b + 1) * P], in_=again[:])
 
         out_rows = out_0.rearrange("(p t) j -> p t j", t=PACK)
         code_rows = out_1[0].rearrange("p n t -> p (n t)").bitcast(I32)
 
-        def finish(j0, n, z_b, first_bank, interleave):
-            cols = slice(j0, j0 + n)
+        def quantise_z(j0, n, z_b):
             z_c = sb([P, n], U32, "z_c%d" % j0)
             z_s = sb([P, n], U8, "z_s%d" % j0)
             nc.vector.quantize_mx(out=z_c[:].bitcast(FP8X4), scales=z_s[:], in_=z_b[:])
+            return z_c, z_s
+
+        def multiply(j0, n, z_q, first_bank):
+            cols = slice(j0, j0 + n)
+            z_c, z_s = z_q
             o_f = sb([P, PACK, n], F32, "o_f%d" % j0)
             for u in range(2):
                 acc = bank(first_bank + u, [P, 2, n], "o%d_%d" % (j0, u))
@@ -227,26 +257,34 @@ def tile_picked_painn8_none_po_kernel(
                         stop=True,
                     )
                 nc.scalar.copy(out=o_f[:, 2 * u : 2 * u + 2, :], in_=acc[:])
-            nc.sync.dma_start(out=out_rows[:, :, cols], in_=o_f[:])
-            o_b = sb([P, PACK * n], BF16, "o_b%d" % j0)
+                if n == HALF:
+                    nc.sync.dma_start(out=out_rows[:, 2 * u : 2 * u + 2, cols], in_=o_f[:, 2 * u : 2 * u + 2, :])
+            if n != HALF:
+                nc.sync.dma_start(out=out_rows[:, :, cols], in_=o_f[:])
+            return o_f
+
+        def planes(j0, o_f, interleave, tag=None):
+            n = P
+            cols = slice(j0, j0 + n)
+            o_b = sb([P, PACK * n], BF16, "o_b%d" % j0, tag=tag)
             interleave(
                 out=o_b[:].rearrange("p (c a t) -> p c t a", a=4, t=PACK),
-                in_=o_f[:].rearrange("p t (c a) -> p c t a", a=4),
+                in_=o_f.rearrange("p t (c a) -> p c t a", a=4),
             )
             nc.vector.quantize_mx(out=o_codes[:, cols].bitcast(FP8X4), scales=o_scales[:, cols], in_=o_b[:])
             nc.sync.dma_start(out=code_rows[:, cols], in_=o_codes[:, cols])
 
-        early = sb([P, PACK, 2, HALF], F32, "early")
-        back = [bank(free, [P, 2, P], "back%d" % free) for free in (0, 3)]
+        early = [sb([P, 2, HALF], F32, "early%d" % t, tag="flat" if t == PACK - 1 else None) for t in range(PACK)]
+        back = [bank(free, [P, 2, P], "back%d" % free) for free in (3, 0)]
         for t in range(PACK):
             for i, lists in enumerate((p1_sb, p2_sb)):
-                nc.vector.tensor_copy(early[:, t, i, :], ye[t][:].indirect(lists[:, : HALF // PER_COLUMN]))
+                nc.vector.tensor_copy(early[t][:, i, :], ye[t][:].indirect(lists[:, : HALF // PER_COLUMN]))
                 for b in range(2):
-                    turn(turned[t // 2][:, b, t % 2, :], early[:, t, i, b * P : (b + 1) * P], False, t % 2 == 1 and i == 1 and b == 1)
+                    turn(turned[t // 2][:, b, t % 2, :], early[t][:, i, b * P : (b + 1) * P], False, t % 2 == 1 and i == 1 and b == 1)
             if t % 2 == 1:
                 u = t // 2
                 for b in range(2):
-                    pairs = sb([P, 2 * P], BF16, "pairs%d_%d" % (u, b))
+                    pairs = sb([P, 2 * P], BF16, "pairs%d_%d" % (u, b), tag="z_b2" if u and b else None)
                     nc.scalar.copy(
                         out=pairs[:].rearrange("a (p odd) -> a p odd", odd=2), in_=turned[u][:, b].rearrange("a odd p -> a p odd")
                     )
@@ -257,25 +295,39 @@ def tile_picked_painn8_none_po_kernel(
                 out=z_early[:].bitcast(F32)[:, 2 * b * P : 2 * (b + 1) * P].rearrange("p (a u) -> p a u", u=2),
                 in_=back[b][:].rearrange("p u a -> p a u"),
             )
-        finish(0, HALF, z_early, 1, nc.scalar.copy)
 
-        with_p1 = sb([P, PACK, HALF], F32, "with_p1")
+        with_p1 = sb([P, PACK, HALF], F32, "with_p1", tag="last")
         for t in range(PACK):
             nc.vector.tensor_tensor(with_p1[:, t, :], ye[t][:].indirect(p1_sb[:, HALF // PER_COLUMN :]), qd_late[:, t, :], ADD)
-        z_late = sb([P, 2, PACK, P], F32, "z_late", tag="z_early")
-        for b in range(2):
+
+        def with_p2(b, t, dst):
             j0 = HALF + b * P
-            z_f = z_late[:, b]
-            for t in range(PACK):
-                nc.vector.tensor_tensor(
-                    z_f[:, t, :], ye[t][:].indirect(p2_sb[:, j0 // PER_COLUMN : (j0 + P) // PER_COLUMN]), with_p1[:, t, b * P : (b + 1) * P], ADD
-                )
-            z_b = sb([P, PACK * P], BF16, "z_b%d" % b)
-            nc.vector.tensor_copy(
-                out=z_b[:].rearrange("p (c a t) -> p c t a", a=4, t=PACK),
-                in_=z_f.rearrange("p t (c a) -> p c t a", a=4),
-            )
-            finish(j0, P, z_b, 4 + 2 * b, nc.vector.tensor_copy)
+            nc.vector.tensor_tensor(dst, ye[t][:].indirect(p2_sb[:, j0 // PER_COLUMN : (j0 + P) // PER_COLUMN]), with_p1[:, t, b * P : (b + 1) * P], ADD)
+
+        def round_z(copy, z_b, z_f):
+            copy(out=z_b[:].rearrange("p (c a t) -> p c t a", a=4, t=PACK), in_=z_f.rearrange("p t (c a) -> p c t a", a=4))
+
+        z_f2 = sb([P, PACK, P], F32, "z_f2")
+        for t in range(PACK):
+            with_p2(0, t, z_f2[:, t, :])
+        z_b2 = sb([P, PACK * P], BF16, "z_b2")
+        round_z(nc.scalar.copy, z_b2, z_f2[:])
+        q_early = quantise_z(0, HALF, z_early)
+        z_f3 = sb([P, PACK, P], F32, "z_f3", tag="z_early")
+        for t in range(PACK):
+            with_p2(1, t, z_f3[:, t, :])
+            if t == 1:
+                q_2 = quantise_z(HALF, P, z_b2)
+        z_b3 = sb([P, PACK * P], BF16, "z_b3")
+        round_z(nc.vector.tensor_copy, z_b3, z_f3[:])
+        q_3 = quantise_z(HALF + P, P, z_b3)
+        o_early = multiply(0, HALF, q_early, 1)
+        o_2 = multiply(HALF, P, q_2, 4)
+        planes(0, o_early[:, :, :P], nc.scalar.copy)
+        o_3 = multiply(HALF + P, P, q_3, 6)
+        planes(HALF, o_2[:], nc.vector.tensor_copy)
+        planes(P, o_early[:, :, P:], nc.scalar.copy, "z_c%d" % (HALF + P))
+        planes(HALF + P, o_3[:], nc.vector.tensor_copy)
         for r in range(PACK):
             queue = nc.scalar if r % 2 else nc.sync
             queue.dma_start(out=out_2[0, r:BLOCKS:PACK, :].bitcast(I32), in_=o_scales[r:P:QUADRANT, :].bitcast(I32))

@@ -32,6 +32,7 @@ def tile_picked_painn8_none_po_kernel(
     nc = tc.nc
     with ExitStack() as ctx:
         keep = ctx.enter_context(tc.tile_pool(name="keep", bufs=1))
+        placed = ctx.enter_context(tc.tile_pool(name="placed", bufs=1))
         psum = ctx.enter_context(tc.psum_pool(name="psum", bufs=1))
 
         def bank(number, shape, name):
@@ -39,6 +40,9 @@ def tile_picked_painn8_none_po_kernel(
 
         def sb(shape, dtype, name, tag=None):
             return keep.tile(shape, dtype, name=name, tag=tag or name, align_bytes=64)
+
+        def at(offset, shape, dtype, name):
+            return placed.tile(shape, dtype, name=name, offset=offset, align_bytes=64)
 
         def load_scale_rows(plane, rows, first=0):
             for r in range(PACK):
@@ -51,8 +55,8 @@ def tile_picked_painn8_none_po_kernel(
         xs = sb([P, T], U8, "xs")
         w1w = sb([P, 2 * H], U8, "w1w")
         w4w = sb([P, 2 * N], U8, "w4w")
-        ws = sb([P, H], U8, "ws")
-        w4s_d = sb([P, N], U8, "w4s_d")
+        w1s = sb([P, H], U8, "w1s")
+        w4s = sb([P, N], U8, "w4s")
         o_scales = sb([P, S], U8, "o_scales")
         o_codes = sb([P, S], I32, "o_codes")
         d1 = sb([P, S], F32, "d1")
@@ -61,8 +65,8 @@ def tile_picked_painn8_none_po_kernel(
         w2_raw = sb([P, PACK, H], F32, "w2_raw")
 
         nc.vector.memset(xs[:].bitcast(I32), 0)
-        nc.gpsimd.memset(ws[:].bitcast(I32), 0)
-        nc.gpsimd.memset(w4s_d[:].bitcast(I32), 0)
+        nc.gpsimd.memset(w1s[:].bitcast(I32), 0)
+        nc.gpsimd.memset(w4s[:].bitcast(I32), 0)
         q_sb = [sb([P, 2 * S if t < PACK - 1 else S], F32, "q_sb%d" % t) for t in range(PACK)]
         for t in range(PACK - 1):
             nc.gpsimd.memset(q_sb[t][:, S:], 0.0)
@@ -76,14 +80,14 @@ def tile_picked_painn8_none_po_kernel(
         nc.sync.dma_start(out=xw[:], in_=x_words[0].rearrange("p n t -> p (n t)").bitcast(I32))
         nc.sync.dma_start(out=w3_raw[1][:], in_=w3_rows[:, :, HALF:])
         nc.sync.dma_start(p1_sb[:], p1)
+        load_scale_rows(w1s, w1_scales[0])
         nc.sync.dma_start(out=w1w[:].bitcast(I32), in_=w1_words[0].bitcast(I32))
-        nc.sync.dma_start(out=w4w[:].bitcast(I32), in_=w4_words[0].bitcast(I32))
         nc.sync.dma_start(out=d1[:], in_=dir1)
-        load_scale_rows(ws, w1_scales[0])
-        load_scale_rows(ws, w4_scales[0], PACK)
+        nc.sync.dma_start(out=w4w[:].bitcast(I32), in_=w4_words[0].bitcast(I32))
         nc.sync.dma_start(p2_sb[:], p2)
         nc.sync.dma_start(out=d2[:], in_=dir2)
         nc.sync.dma_start(out=w2_raw[:], in_=w2.rearrange("(p j) c -> p j c", j=PACK))
+        load_scale_rows(w4s, w4_scales[0])
         d_late = [sb([P, 2], F32, "d_late%d" % i) for i in range(2)]
         with nc.allow_non_contiguous_dma(reason="one direction a partition"):
             for i, direction in enumerate((dir1, dir2)):
@@ -129,9 +133,7 @@ def tile_picked_painn8_none_po_kernel(
             )
         w1w_d = deal_words(w1w, "w1w_d")
         w4w_d = deal_words(w4w, "w4w_d")
-        w1s_d = deal_scales(ws, "ws_d")
-        for r in range(PACK):
-            nc.sync.dma_start(out=w4s_d[r:P:QUADRANT, :].bitcast(I32), in_=w1s_d[PACK + r : P : QUADRANT, :].bitcast(I32))
+        w1s_d = deal_scales(w1s, "w1s_d")
 
         def product(lhsT, lhsT_scale, name, number):
             acc = bank(number, [P, S], name)
@@ -157,7 +159,7 @@ def tile_picked_painn8_none_po_kernel(
             cols = slice(t * P, (t + 1) * P)
             acc = product(w3_c[:, cols].bitcast(FP8X4), w3_s[:, cols], "q%d" % t, t)
             nc.scalar.copy(out=q_sb[t][:, :S], in_=acc[:])
-        w2_b = sb([P, PACK * H], BF16, "w2_b")
+        w2_b = at(4 * S - 64, [P, PACK * H], BF16, "w2_b")
         for h in range(2):
             round_and_deal(nc.scalar.copy, w2_b, w2_raw[:, :, h * HALF : (h + 1) * HALF], h)
         y_first = sb([P, PACK - 1, S], F32, "y_first", tag="w2_raw")
@@ -169,10 +171,9 @@ def tile_picked_painn8_none_po_kernel(
         w2_c = sb([P, H], U32, "w2_c")
         w2_s = sb([P, H], U8, "w2_s")
 
-        def directed(t, n, both):
-            nc.vector.tensor_tensor(both[:, 0, :], q_sb[t][:].indirect(p1_sb[:, : n // PER_COLUMN]), d1[:, :n], MULT)
-            nc.vector.tensor_tensor(both[:, 1, :], q_sb[t][:].indirect(p2_sb[:, : n // PER_COLUMN]), d2[:, :n], MULT)
-            return both
+        def directed(t, i, term):
+            n = term.shape[1]
+            nc.vector.tensor_tensor(term, q_sb[t][:].indirect((p1_sb, p2_sb)[i][:, : n // PER_COLUMN]), (d1, d2)[i][:, :n], MULT)
 
         turned = [bank(4 + u, [P, 2, 2, P], "turned%d" % u) for u in range(2)]
         late = [bank(6 + b, [P, PACK - 1, P], "late%d" % b) for b in range(2)]
@@ -180,26 +181,43 @@ def tile_picked_painn8_none_po_kernel(
         def turn(dst, src, start, stop):
             nc.tensor.matmul(dst, src, ident[:], start=start, stop=stop, is_transpose=True)
 
-        for t in range(PACK - 1):
-            both = directed(t, S, sb([P, 2, S], F32, "qd%d" % t))
-            for i in range(2):
-                for b in range(2):
-                    turn(late[b][:, t, :], both[:, i, (2 + b) * P : (3 + b) * P], t == 0 and i == 0, t == PACK - 2 and i == 1)
-                for b in range(2):
-                    turn(turned[t // 2][:, b, t % 2, :], both[:, i, b * P : (b + 1) * P], t % 2 == 0 and i == 0 and b == 0, False)
-        flat = sb([P, 2, PACK + 1, P], F32, "flat")
-        for b in range(2):
-            nc.scalar.copy(out=flat[:, b, : PACK - 1, :], in_=late[b][:])
+        def whole_term(t, i, term):
+            directed(t, i, term)
+            for b in range(2):
+                turn(late[b][:, t, :], term[:, (2 + b) * P : (3 + b) * P], t == 0 and i == 0, t == PACK - 2 and i == 1)
+            for b in range(2):
+                turn(turned[t // 2][:, b, t % 2, :], term[:, b * P : (b + 1) * P], t % 2 == 0 and i == 0 and b == 0, False)
+
+        for n in range(5):
+            whole_term(n // 2, n % 2, sb([P, S], F32, "qd%d" % n)[:])
         nc.vector.quantize_mx(out=w2_c[:].bitcast(FP8X4), scales=w2_s[:], in_=w2_b[:])
+        w4s_d = deal_scales(w4s, "w4s_d")
         e_sb = []
-        for t in range(PACK):
+
+        def e_tile(t):
             cols = slice(t * P, (t + 1) * P)
             acc = product(w2_c[:, cols].bitcast(FP8X4), w2_s[:, cols], "e%d" % t, t)
             e_t = sb([P, S], F32, "e_sb%d" % t)[:] if t < PACK - 1 else last[:, 1, :]
             nc.scalar.copy(out=e_t, in_=acc[:])
             e_sb.append(e_t)
-        qd3 = sb([P, 2, 2, HALF], F32, "qd3", tag="w2_b")
-        directed(3, HALF, qd3[:, 0])
+
+        e_tile(0)
+        e_tile(1)
+        whole_term(2, 1, at(0, [P, S], F32, "qd5")[:])
+        flat = sb([P, 2, PACK - 1, P], F32, "flat")
+        qd_late = sb([P, PACK, HALF], F32, "qd_late")
+        for b in range(2):
+            nc.scalar.copy(out=flat[:, b], in_=late[b][:])
+        e_tile(2)
+        e_tile(3)
+        for b in range(2):
+            again = bank(3 - 3 * b, [P, PACK - 1, P], "again%d" % b)
+            for t in range(PACK - 1):
+                nc.tensor.transpose(again[:, t, :], flat[:, b, t, :], ident[:])
+            nc.scalar.copy(out=qd_late[:, : PACK - 1, b * P : (b + 1) * P], in_=again[:])
+        qd3 = at(4 * S, [P, 2, 2, HALF], F32, "qd3")
+        for i in range(2):
+            directed(3, i, qd3[:, 0, i, :])
         q3_late = qd3[:, 1]
         for i, lists in enumerate((p1_sb, p2_sb)):
             nc.vector.tensor_copy(q3_late[:, i, :], q_sb[3][:].indirect(lists[:, HALF // PER_COLUMN :]))
@@ -213,22 +231,19 @@ def tile_picked_painn8_none_po_kernel(
         for i in range(2):
             for b in range(2):
                 turn(turned[1][:, b, 1, :], qd3[:, 0, i, b * P : (b + 1) * P], False, False)
-        late3 = bank(0, [P, 2, 2, P], "late3")
+        late3 = bank(1, [P, 2, 2, P], "late3")
         for i in range(2):
             for b in range(2):
                 nc.tensor.transpose(late3[:, i, b, :], q3_late[:, i, b * P : (b + 1) * P], ident[:])
 
-        qd_late = sb([P, PACK, HALF], F32, "qd_late")
+        flat3 = sb([P, 2, 2, P], F32, "flat3")
+        again3 = bank(2, [P, 2, P], "again3")
         for b in range(2):
             for i in range(2):
-                nc.scalar.activation(flat[:, b, PACK - 1 + i, :], late3[:, i, b, :], COPY, scale=d_late[i][:, b : b + 1])
-        for b in range(2):
-            again = bank(3 - 3 * b, [P, PACK, P], "again%d" % b)
-            for t in range(PACK - 1):
-                nc.tensor.transpose(again[:, t, :], flat[:, b, t, :], ident[:])
+                nc.scalar.activation(flat3[:, b, i, :], late3[:, i, b, :], COPY, scale=d_late[i][:, b : b + 1])
             for i in range(2):
-                turn(again[:, PACK - 1, :], flat[:, b, PACK - 1 + i, :], i == 0, i == 1)
-            nc.scalar.copy(out=qd_late[:, :, b * P : (b + 1) * P], in_=again[:])
+                turn(again3[:, b, :], flat3[:, b, i, :], i == 0, i == 1)
+        nc.scalar.copy(out=qd_late[:, PACK - 1, :], in_=again3[:].rearrange("p b a -> p (b a)"))
 
         out_rows = out_0.rearrange("(p t) j -> p t j", t=PACK)
         code_rows = out_1[0].rearrange("p n t -> p (n t)").bitcast(I32)

@@ -59,7 +59,7 @@ def tile_picked_painn8_none_po_kernel(
         w4s = sb([P, N], U8, "w4s")
         o_scales = sb([P, S], U8, "o_scales")
         o_codes = sb([P, S], I32, "o_codes")
-        d1 = sb([P, S], F32, "d1")
+        d1 = at(8192 + 512, [P, S], F32, "d1")
         d2 = sb([P, S], F32, "d2")
         w3_raw = [sb([P, PACK, HALF], F32, "w3_raw%d" % h) for h in range(2)]
         w2_raw = sb([P, PACK, H], F32, "w2_raw")
@@ -67,8 +67,8 @@ def tile_picked_painn8_none_po_kernel(
         nc.vector.memset(xs[:].bitcast(I32), 0)
         nc.gpsimd.memset(w1s[:].bitcast(I32), 0)
         nc.gpsimd.memset(w4s[:].bitcast(I32), 0)
-        q_sb = [sb([P, 2 * S if t < PACK - 1 else S], F32, "q_sb%d" % t) for t in range(PACK)]
-        for t in range(PACK - 1):
+        q_sb = [sb([P, 2 * S if t < 2 else S], F32, "q_sb%d" % t) for t in range(PACK)]
+        for t in range(2):
             nc.gpsimd.memset(q_sb[t][:, S:], 0.0)
         ident = sb([P, P], F32, "ident")
         make_identity(nc, ident[:])
@@ -159,39 +159,34 @@ def tile_picked_painn8_none_po_kernel(
             cols = slice(t * P, (t + 1) * P)
             acc = product(w3_c[:, cols].bitcast(FP8X4), w3_s[:, cols], "q%d" % t, t)
             nc.scalar.copy(out=q_sb[t][:, :S], in_=acc[:])
-        w2_b = at(4 * S - 64, [P, PACK * H], BF16, "w2_b")
+        w2_b = at(512, [P, PACK * H], BF16, "w2_b")
         for h in range(2):
             round_and_deal(nc.scalar.copy, w2_b, w2_raw[:, :, h * HALF : (h + 1) * HALF], h)
-        y_first = sb([P, PACK - 1, S], F32, "y_first", tag="w2_raw")
+        y_first = sb([P, PACK, S], F32, "y_first", tag="w2_raw")
         last = sb([P, 2, S], F32, "last")
         y_sb = [y_first[:, t, :] for t in range(PACK - 1)] + [last[:, 0, :]]
-        for t in range(PACK):
-            acc = product(w1w_d[:, 2 * t * P : 2 * (t + 1) * P].bitcast(FP4X4), w1s_d[:, t * P : (t + 1) * P], "y%d" % t, t)
-            nc.scalar.copy(out=y_sb[t], in_=acc[:])
         w2_c = sb([P, H], U32, "w2_c")
         w2_s = sb([P, H], U8, "w2_s")
+        lists = (p1_sb, p2_sb)
 
         def directed(t, i, term):
             n = term.shape[1]
-            nc.vector.tensor_tensor(term, q_sb[t][:].indirect((p1_sb, p2_sb)[i][:, : n // PER_COLUMN]), (d1, d2)[i][:, :n], MULT)
+            nc.vector.tensor_tensor(term, q_sb[t][:].indirect(lists[i][:, : n // PER_COLUMN]), (d1, d2)[i][:, :n], MULT)
 
         turned = [bank(4 + u, [P, 2, 2, P], "turned%d" % u) for u in range(2)]
-        late = [bank(6 + b, [P, PACK - 1, P], "late%d" % b) for b in range(2)]
+        late01 = bank(6, [P, 2, 2, P], "late01")
 
         def turn(dst, src, start, stop):
             nc.tensor.matmul(dst, src, ident[:], start=start, stop=stop, is_transpose=True)
 
-        def whole_term(t, i, term):
-            directed(t, i, term)
-            for b in range(2):
-                turn(late[b][:, t, :], term[:, (2 + b) * P : (3 + b) * P], t == 0 and i == 0, t == PACK - 2 and i == 1)
+        def turn_early(t, i, term):
             for b in range(2):
                 turn(turned[t // 2][:, b, t % 2, :], term[:, b * P : (b + 1) * P], t % 2 == 0 and i == 0 and b == 0, False)
 
-        for n in range(5):
-            whole_term(n // 2, n % 2, sb([P, S], F32, "qd%d" % n)[:])
-        nc.vector.quantize_mx(out=w2_c[:].bitcast(FP8X4), scales=w2_s[:], in_=w2_b[:])
-        w4s_d = deal_scales(w4s, "w4s_d")
+        def y_tile(t):
+            acc = product(w1w_d[:, 2 * t * P : 2 * (t + 1) * P].bitcast(FP4X4), w1s_d[:, t * P : (t + 1) * P], "y%d" % t, t)
+            nc.scalar.copy(out=y_sb[t], in_=acc[:])
+
         e_sb = []
 
         def e_tile(t):
@@ -201,26 +196,39 @@ def tile_picked_painn8_none_po_kernel(
             nc.scalar.copy(out=e_t, in_=acc[:])
             e_sb.append(e_t)
 
+        y_tile(0)
+        y_tile(1)
+        for t in range(2):
+            for i in range(2):
+                term = sb([P, S], F32, "qd%d_%d" % (t, i))[:]
+                directed(t, i, term)
+                for b in range(2):
+                    turn(late01[:, t, b, :], term[:, (2 + b) * P : (3 + b) * P], t == 0 and i == 0 and b == 0, t == 1 and i == 1 and b == 1)
+                turn_early(t, i, term)
+        nc.vector.quantize_mx(out=w2_c[:].bitcast(FP8X4), scales=w2_s[:], in_=w2_b[:])
+        w4s_d = deal_scales(w4s, "w4s_d")
         e_tile(0)
+        y_tile(2)
         e_tile(1)
-        whole_term(2, 1, at(0, [P, S], F32, "qd5")[:])
-        flat = sb([P, 2, PACK - 1, P], F32, "flat")
-        qd_late = sb([P, PACK, HALF], F32, "qd_late")
-        for b in range(2):
-            nc.scalar.copy(out=flat[:, b], in_=late[b][:])
+        y_tile(3)
         e_tile(2)
         e_tile(3)
-        for b in range(2):
-            again = bank(3 - 3 * b, [P, PACK - 1, P], "again%d" % b)
-            for t in range(PACK - 1):
-                nc.tensor.transpose(again[:, t, :], flat[:, b, t, :], ident[:])
-            nc.scalar.copy(out=qd_late[:, : PACK - 1, b * P : (b + 1) * P], in_=again[:])
-        qd3 = at(4 * S, [P, 2, 2, HALF], F32, "qd3")
-        for i in range(2):
-            directed(3, i, qd3[:, 0, i, :])
-        q3_late = qd3[:, 1]
-        for i, lists in enumerate((p1_sb, p2_sb)):
-            nc.vector.tensor_copy(q3_late[:, i, :], q_sb[3][:].indirect(lists[:, HALF // PER_COLUMN :]))
+        flat = y_first[:, PACK - 1, :].rearrange("p (t b a) -> p t b a", t=2, b=2)
+        qd_late = sb([P, PACK, HALF], F32, "qd_late")
+        nc.scalar.copy(out=flat, in_=late01[:])
+        again01 = bank(6, [P, 2, 2, P], "again01")
+        for t in range(2):
+            for b in range(2):
+                nc.tensor.transpose(again01[:, t, b, :], flat[:, t, b, :], ident[:])
+        nc.scalar.copy(out=qd_late[:, :2, :], in_=again01[:].rearrange("p t b a -> p t (b a)"))
+        terms = []
+        for n in range(PACK):
+            terms.append(at(1024 * n, [P, HALF], F32, "qe%d" % n)[:])
+            directed(2 + n // 2, n % 2, terms[n])
+        plain = []
+        for n in range(PACK):
+            plain.append(at((8192, 9216, 10240, 4096)[n], [P, HALF], F32, "ql%d" % n)[:])
+            nc.vector.tensor_copy(plain[n], q_sb[2 + n // 2][:].indirect(lists[n % 2][:, HALF // PER_COLUMN :]))
 
         ye = []
         for t in range(PACK):
@@ -228,22 +236,23 @@ def tile_picked_painn8_none_po_kernel(
             nc.gpsimd.tensor_tensor(ye_t[:], e_sb[t], y_sb[t], MULT)
             ye.append(ye_t)
 
-        for i in range(2):
-            for b in range(2):
-                turn(turned[1][:, b, 1, :], qd3[:, 0, i, b * P : (b + 1) * P], False, False)
-        late3 = bank(1, [P, 2, 2, P], "late3")
-        for i in range(2):
-            for b in range(2):
-                nc.tensor.transpose(late3[:, i, b, :], q3_late[:, i, b * P : (b + 1) * P], ident[:])
-
-        flat3 = sb([P, 2, 2, P], F32, "flat3")
-        again3 = bank(2, [P, 2, P], "again3")
-        for b in range(2):
+        for n in range(PACK):
+            turn_early(2 + n // 2, n % 2, terms[n])
+        flat23 = sb([P, 2, 2, 2, P], F32, "flat23")
+        for odd in range(2):
+            unscaled = bank(0 if odd else 7, [P, 2, 2, P], "unscaled%d" % odd)
             for i in range(2):
-                nc.scalar.activation(flat3[:, b, i, :], late3[:, i, b, :], COPY, scale=d_late[i][:, b : b + 1])
-            for i in range(2):
-                turn(again3[:, b, :], flat3[:, b, i, :], i == 0, i == 1)
-        nc.scalar.copy(out=qd_late[:, PACK - 1, :], in_=again3[:].rearrange("p b a -> p (b a)"))
+                for b in range(2):
+                    nc.tensor.transpose(unscaled[:, i, b, :], plain[2 * odd + i][:, b * P : (b + 1) * P], ident[:])
+            for b in range(2):
+                for i in range(2):
+                    nc.scalar.activation(flat23[:, odd, b, i, :], unscaled[:, i, b, :], COPY, scale=d_late[i][:, b : b + 1])
+        again23 = bank(7, [P, 2, 2, P], "again23")
+        for odd in range(2):
+            for b in range(2):
+                for i in range(2):
+                    turn(again23[:, odd, b, :], flat23[:, odd, b, i, :], i == 0, i == 1)
+        nc.scalar.copy(out=qd_late[:, 2:, :], in_=again23[:].rearrange("p t b a -> p t (b a)"))
 
         out_rows = out_0.rearrange("(p t) j -> p t j", t=PACK)
         code_rows = out_1[0].rearrange("p n t -> p (n t)").bitcast(I32)
@@ -289,11 +298,11 @@ def tile_picked_painn8_none_po_kernel(
             nc.vector.quantize_mx(out=o_codes[:, cols].bitcast(FP8X4), scales=o_scales[:, cols], in_=o_b[:])
             nc.sync.dma_start(out=code_rows[:, cols], in_=o_codes[:, cols])
 
-        early = [sb([P, 2, HALF], F32, "early%d" % t, tag="flat" if t == PACK - 1 else None) for t in range(PACK)]
-        back = [bank(free, [P, 2, P], "back%d" % free) for free in (3, 0)]
+        early = [sb([P, 2, HALF], F32, "early%d" % t) for t in range(PACK)]
+        back = [bank(free, [P, 2, P], "back%d" % free) for free in (2, 3)]
         for t in range(PACK):
-            for i, lists in enumerate((p1_sb, p2_sb)):
-                nc.vector.tensor_copy(early[t][:, i, :], ye[t][:].indirect(lists[:, : HALF // PER_COLUMN]))
+            for i in range(2):
+                nc.vector.tensor_copy(early[t][:, i, :], ye[t][:].indirect(lists[i][:, : HALF // PER_COLUMN]))
                 for b in range(2):
                     turn(turned[t // 2][:, b, t % 2, :], early[t][:, i, b * P : (b + 1) * P], False, t % 2 == 1 and i == 1 and b == 1)
             if t % 2 == 1:
@@ -336,7 +345,7 @@ def tile_picked_painn8_none_po_kernel(
         z_b3 = sb([P, PACK * P], BF16, "z_b3")
         round_z(nc.vector.tensor_copy, z_b3, z_f3[:])
         q_3 = quantise_z(HALF + P, P, z_b3)
-        o_early = multiply(0, HALF, q_early, 1)
+        o_early = multiply(0, HALF, q_early, 0)
         o_2 = multiply(HALF, P, q_2, 4)
         planes(0, o_early[:, :, :P], nc.scalar.copy)
         o_3 = multiply(HALF + P, P, q_3, 6)

@@ -61,7 +61,7 @@ def tile_picked_painn8_none_po_kernel(
         o_codes = sb([P, S], I32, "o_codes")
         d1 = at(8192 + 512, [P, S], F32, "d1")
         d2 = sb([P, S], F32, "d2")
-        w3_raw = [sb([P, PACK, HALF], F32, "w3_raw%d" % h) for h in range(2)]
+        w3_raw = [sb([P, 2, H], F32, "w3_raw%d" % h) for h in range(2)]
         w2_raw = sb([P, PACK, H], F32, "w2_raw")
 
         nc.vector.memset(xs[:].bitcast(I32), 0)
@@ -74,11 +74,11 @@ def tile_picked_painn8_none_po_kernel(
         make_identity(nc, ident[:])
 
         w3_rows = w3.rearrange("(p j) c -> p j c", j=PACK)
+        nc.sync.dma_start(out=w3_raw[0][:], in_=w3_rows[:, :2, :])
         nc.sync.dma_start(offs_sb[:], offs)
-        nc.sync.dma_start(out=w3_raw[0][:], in_=w3_rows[:, :, :HALF])
         load_scale_rows(xs, x_scales[0])
         nc.sync.dma_start(out=xw[:], in_=x_words[0].rearrange("p n t -> p (n t)").bitcast(I32))
-        nc.sync.dma_start(out=w3_raw[1][:], in_=w3_rows[:, :, HALF:])
+        nc.sync.dma_start(out=w3_raw[1][:], in_=w3_rows[:, 2:, :])
         nc.sync.dma_start(p1_sb[:], p1)
         load_scale_rows(w1s, w1_scales[0])
         nc.sync.dma_start(out=w1w[:].bitcast(I32), in_=w1_words[0].bitcast(I32))
@@ -121,9 +121,17 @@ def tile_picked_painn8_none_po_kernel(
             )
 
         w3_b = sb([P, PACK * H], BF16, "w3_b")
-        round_and_deal(nc.scalar.copy, w3_b, w3_raw[0][:], 0)
-        round_and_deal(nc.vector.tensor_copy, w3_b, w3_raw[1][:], 1, 0, 1)
-        round_and_deal(nc.scalar.copy, w3_b, w3_raw[1][:], 1, 1, PACK)
+
+        def round_rows(copy, h, t0, t1):
+            copy(
+                out=w3_b[:].rearrange("p (t m j) -> p m t j", t=PACK, j=PACK)[:, :, t0:t1, 2 * h : 2 * h + 2],
+                in_=w3_raw[h][:].rearrange("p j (m t) -> p m t j", t=PACK)[:, :, t0:t1],
+            )
+
+        round_rows(nc.scalar.copy, 0, 0, PACK)
+        round_rows(nc.vector.tensor_copy, 1, 0, 1)
+        round_rows(nc.vector.tensor_copy, 1, 1, 2)
+        round_rows(nc.scalar.copy, 1, 2, PACK)
         w3_c = sb([P, H], U32, "w3_c")
         w3_s = sb([P, H], U8, "w3_s")
         for t in range(PACK):

@@ -24,6 +24,9 @@ HALF = 256
 PER_COLUMN = 16
 QUADRANT = 32
 BLOCKS = K // 32
+TERM = 4 * HALF
+ON_W2 = 0
+ON_DIR1 = 8 * TERM
 
 
 def tile_picked_painn8_none_po_kernel(
@@ -44,9 +47,9 @@ def tile_picked_painn8_none_po_kernel(
         def at(offset, shape, dtype, name):
             return placed.tile(shape, dtype, name=name, offset=offset, align_bytes=64)
 
-        def load_scale_rows(plane, rows, first=0):
+        def place_scale_rows(plane, rows):
             for r in range(PACK):
-                nc.sync.dma_start(out=plane[first + r : P : QUADRANT, :].bitcast(I32), in_=rows[r:BLOCKS:PACK, :].bitcast(I32))
+                nc.sync.dma_start(out=plane[r:P:QUADRANT, :].bitcast(I32), in_=rows[r:BLOCKS:PACK, :].bitcast(I32))
 
         offs_sb = keep.tile([P, S // PER_COLUMN], U16, name="offs_sb")
         p1_sb = keep.tile([P, S // PER_COLUMN], U16, name="p1_sb")
@@ -59,7 +62,7 @@ def tile_picked_painn8_none_po_kernel(
         w4s = sb([P, N], U8, "w4s")
         o_scales = sb([P, S], U8, "o_scales")
         o_codes = sb([P, S], I32, "o_codes")
-        d1 = at(8192 + 512, [P, S], F32, "d1")
+        d1 = at(ON_DIR1 + TERM // 2, [P, S], F32, "d1")
         d2 = sb([P, S], F32, "d2")
         w3_raw = [sb([P, 2, H], F32, "w3_raw%d" % h) for h in range(2)]
         w2_raw = sb([P, PACK, H], F32, "w2_raw")
@@ -76,18 +79,18 @@ def tile_picked_painn8_none_po_kernel(
         w3_rows = w3.rearrange("(p j) c -> p j c", j=PACK)
         nc.sync.dma_start(out=w3_raw[0][:], in_=w3_rows[:, :2, :])
         nc.sync.dma_start(offs_sb[:], offs)
-        load_scale_rows(xs, x_scales[0])
+        place_scale_rows(xs, x_scales[0])
+        nc.sync.dma_start(out=w4s[:BLOCKS, :].bitcast(I32), in_=w4_scales[0].bitcast(I32))
         nc.sync.dma_start(out=xw[:], in_=x_words[0].rearrange("p n t -> p (n t)").bitcast(I32))
         nc.sync.dma_start(out=w3_raw[1][:], in_=w3_rows[:, 2:, :])
         nc.sync.dma_start(p1_sb[:], p1)
-        load_scale_rows(w1s, w1_scales[0])
+        place_scale_rows(w1s, w1_scales[0])
         nc.sync.dma_start(out=w1w[:].bitcast(I32), in_=w1_words[0].bitcast(I32))
         nc.sync.dma_start(out=d1[:], in_=dir1)
         nc.sync.dma_start(out=w4w[:].bitcast(I32), in_=w4_words[0].bitcast(I32))
         nc.sync.dma_start(p2_sb[:], p2)
         nc.sync.dma_start(out=d2[:], in_=dir2)
         nc.sync.dma_start(out=w2_raw[:], in_=w2.rearrange("(p j) c -> p j c", j=PACK))
-        load_scale_rows(w4s, w4_scales[0])
         d_late = [sb([P, 2], F32, "d_late%d" % i) for i in range(2)]
         with nc.allow_non_contiguous_dma(reason="one direction a partition"):
             for i, direction in enumerate((dir1, dir2)):
@@ -112,26 +115,24 @@ def tile_picked_painn8_none_po_kernel(
         xq_s = sb([P, S], U8, "xq_s")
         xq = sb([P, S], U32, "xq")
         nc.vector.tensor_copy(xq_s[:], xs[:].indirect(offs_sb[:]))
+        w4s_rows = deal_scales(w4s, "w4s_rows")
+        w4s_d = sb([P, N], U8, "w4s_d")
+        nc.gpsimd.memset(w4s_d[:].bitcast(I32), 0)
+        place_scale_rows(w4s_d, w4s_rows[:BLOCKS, :])
         nc.vector.tensor_copy(xq[:], xw[:].bitcast(U32).indirect(offs_sb[:]))
-
-        def round_and_deal(copy, grouped, raw, h, t0=0, t1=PACK):
-            copy(
-                out=grouped[:].rearrange("p (t m j) -> p m t j", t=PACK, j=PACK)[:, h * P // 2 : (h + 1) * P // 2, t0:t1],
-                in_=raw.rearrange("p j (m t) -> p m t j", t=PACK)[:, :, t0:t1],
-            )
 
         w3_b = sb([P, PACK * H], BF16, "w3_b")
 
-        def round_rows(copy, h, t0, t1):
+        def round_w3(copy, h, t0, t1):
             copy(
                 out=w3_b[:].rearrange("p (t m j) -> p m t j", t=PACK, j=PACK)[:, :, t0:t1, 2 * h : 2 * h + 2],
                 in_=w3_raw[h][:].rearrange("p j (m t) -> p m t j", t=PACK)[:, :, t0:t1],
             )
 
-        round_rows(nc.scalar.copy, 0, 0, PACK)
-        round_rows(nc.vector.tensor_copy, 1, 0, 1)
-        round_rows(nc.vector.tensor_copy, 1, 1, 2)
-        round_rows(nc.scalar.copy, 1, 2, PACK)
+        round_w3(nc.scalar.copy, 0, 0, PACK)
+        round_w3(nc.vector.tensor_copy, 1, 0, 1)
+        round_w3(nc.vector.tensor_copy, 1, 1, 2)
+        round_w3(nc.scalar.copy, 1, 2, PACK)
         w3_c = sb([P, H], U32, "w3_c")
         w3_s = sb([P, H], U8, "w3_s")
         for t in range(PACK):
@@ -167,12 +168,15 @@ def tile_picked_painn8_none_po_kernel(
             cols = slice(t * P, (t + 1) * P)
             acc = product(w3_c[:, cols].bitcast(FP8X4), w3_s[:, cols], "q%d" % t, t)
             nc.scalar.copy(out=q_sb[t][:, :S], in_=acc[:])
-        w2_b = at(512, [P, PACK * H], BF16, "w2_b")
+        w2_b = at(ON_W2 + TERM // 2, [P, PACK * H], BF16, "w2_b")
         for h in range(2):
-            round_and_deal(nc.scalar.copy, w2_b, w2_raw[:, :, h * HALF : (h + 1) * HALF], h)
-        y_first = sb([P, PACK, S], F32, "y_first", tag="w2_raw")
-        last = sb([P, 2, S], F32, "last")
-        y_sb = [y_first[:, t, :] for t in range(PACK - 1)] + [last[:, 0, :]]
+            nc.scalar.copy(
+                out=w2_b[:].rearrange("p (t m j) -> p m t j", t=PACK, j=PACK)[:, h * P // 2 : (h + 1) * P // 2],
+                in_=w2_raw[:, :, h * HALF : (h + 1) * HALF].rearrange("p j (m t) -> p m t j", t=PACK),
+            )
+        after_w2 = sb([P, PACK, S], F32, "after_w2", tag="w2_raw")
+        y3_e3 = sb([P, 2, S], F32, "y3_e3")
+        y_sb = [after_w2[:, t, :] for t in range(PACK - 1)] + [y3_e3[:, 0, :]]
         w2_c = sb([P, H], U32, "w2_c")
         w2_s = sb([P, H], U8, "w2_s")
         lists = (p1_sb, p2_sb)
@@ -200,7 +204,7 @@ def tile_picked_painn8_none_po_kernel(
         def e_tile(t):
             cols = slice(t * P, (t + 1) * P)
             acc = product(w2_c[:, cols].bitcast(FP8X4), w2_s[:, cols], "e%d" % t, t)
-            e_t = sb([P, S], F32, "e_sb%d" % t)[:] if t < PACK - 1 else last[:, 1, :]
+            e_t = sb([P, S], F32, "e_sb%d" % t)[:] if t < PACK - 1 else y3_e3[:, 1, :]
             nc.scalar.copy(out=e_t, in_=acc[:])
             e_sb.append(e_t)
 
@@ -213,30 +217,32 @@ def tile_picked_painn8_none_po_kernel(
                 for b in range(2):
                     turn(late01[:, t, b, :], term[:, (2 + b) * P : (3 + b) * P], t == 0 and i == 0 and b == 0, t == 1 and i == 1 and b == 1)
                 turn_early(t, i, term)
-        nc.vector.quantize_mx(out=w2_c[:].bitcast(FP8X4), scales=w2_s[:], in_=w2_b[:])
-        w4s_d = deal_scales(w4s, "w4s_d")
+        for u in range(2):
+            cols = slice(u * HALF, (u + 1) * HALF)
+            nc.vector.quantize_mx(out=w2_c[:, cols].bitcast(FP8X4), scales=w2_s[:, cols], in_=w2_b[:, u * PACK * HALF : (u + 1) * PACK * HALF])
         e_tile(0)
         y_tile(2)
         e_tile(1)
         y_tile(3)
         e_tile(2)
         e_tile(3)
-        flat = y_first[:, PACK - 1, :].rearrange("p (t b a) -> p t b a", t=2, b=2)
+        flat01 = after_w2[:, PACK - 1, :].rearrange("p (t b a) -> p t b a", t=2, b=2)
         qd_late = sb([P, PACK, HALF], F32, "qd_late")
-        nc.scalar.copy(out=flat, in_=late01[:])
+        nc.scalar.copy(out=flat01, in_=late01[:])
         again01 = bank(6, [P, 2, 2, P], "again01")
         for t in range(2):
             for b in range(2):
-                nc.tensor.transpose(again01[:, t, b, :], flat[:, t, b, :], ident[:])
+                nc.tensor.transpose(again01[:, t, b, :], flat01[:, t, b, :], ident[:])
         nc.scalar.copy(out=qd_late[:, :2, :], in_=again01[:].rearrange("p t b a -> p t (b a)"))
-        terms = []
+        early_terms = []
         for n in range(PACK):
-            terms.append(at(1024 * n, [P, HALF], F32, "qe%d" % n)[:])
-            directed(2 + n // 2, n % 2, terms[n])
-        plain = []
+            early_terms.append(at(ON_W2 + n * TERM, [P, HALF], F32, "early_term%d" % n)[:])
+            directed(2 + n // 2, n % 2, early_terms[n])
+        late_q = []
         for n in range(PACK):
-            plain.append(at((8192, 9216, 10240, 4096)[n], [P, HALF], F32, "ql%d" % n)[:])
-            nc.vector.tensor_copy(plain[n], q_sb[2 + n // 2][:].indirect(lists[n % 2][:, HALF // PER_COLUMN :]))
+            offset = ON_DIR1 + n * TERM if n < PACK - 1 else ON_W2 + PACK * TERM
+            late_q.append(at(offset, [P, HALF], F32, "late_q%d" % n)[:])
+            nc.vector.tensor_copy(late_q[n], q_sb[2 + n // 2][:].indirect(lists[n % 2][:, HALF // PER_COLUMN :]))
 
         ye = []
         for t in range(PACK):
@@ -245,13 +251,13 @@ def tile_picked_painn8_none_po_kernel(
             ye.append(ye_t)
 
         for n in range(PACK):
-            turn_early(2 + n // 2, n % 2, terms[n])
+            turn_early(2 + n // 2, n % 2, early_terms[n])
         flat23 = sb([P, 2, 2, 2, P], F32, "flat23")
         for odd in range(2):
             unscaled = bank(0 if odd else 7, [P, 2, 2, P], "unscaled%d" % odd)
             for i in range(2):
                 for b in range(2):
-                    nc.tensor.transpose(unscaled[:, i, b, :], plain[2 * odd + i][:, b * P : (b + 1) * P], ident[:])
+                    nc.tensor.transpose(unscaled[:, i, b, :], late_q[2 * odd + i][:, b * P : (b + 1) * P], ident[:])
             for b in range(2):
                 for i in range(2):
                     nc.scalar.activation(flat23[:, odd, b, i, :], unscaled[:, i, b, :], COPY, scale=d_late[i][:, b : b + 1])
@@ -268,7 +274,9 @@ def tile_picked_painn8_none_po_kernel(
         def quantise_z(j0, n, z_b):
             z_c = sb([P, n], U32, "z_c%d" % j0)
             z_s = sb([P, n], U8, "z_s%d" % j0)
-            nc.vector.quantize_mx(out=z_c[:].bitcast(FP8X4), scales=z_s[:], in_=z_b[:])
+            for b in range(n // P):
+                cols = slice(b * P, (b + 1) * P)
+                nc.vector.quantize_mx(out=z_c[:, cols].bitcast(FP8X4), scales=z_s[:, cols], in_=z_b[:, b * PACK * P : (b + 1) * PACK * P])
             return z_c, z_s
 
         def multiply(j0, n, z_q, first_bank):
@@ -295,16 +303,17 @@ def tile_picked_painn8_none_po_kernel(
                 nc.sync.dma_start(out=out_rows[:, :, cols], in_=o_f[:])
             return o_f
 
-        def planes(j0, o_f, interleave, tag=None):
-            n = P
-            cols = slice(j0, j0 + n)
-            o_b = sb([P, PACK * n], BF16, "o_b%d" % j0, tag=tag)
-            interleave(
-                out=o_b[:].rearrange("p (c a t) -> p c t a", a=4, t=PACK),
-                in_=o_f.rearrange("p t (c a) -> p c t a", a=4),
-            )
+        def interleave(copy, name, values):
+            rounded = sb([P, PACK * P], BF16, name)
+            copy(out=rounded[:].rearrange("p (c a t) -> p c t a", a=4, t=PACK), in_=values.rearrange("p t (c a) -> p c t a", a=4))
+            return rounded
+
+        def planes(b, o_b):
+            cols = slice(b * P, (b + 1) * P)
             nc.vector.quantize_mx(out=o_codes[:, cols].bitcast(FP8X4), scales=o_scales[:, cols], in_=o_b[:])
-            nc.sync.dma_start(out=code_rows[:, cols], in_=o_codes[:, cols])
+            if b % 2:
+                both = slice((b - 1) * P, (b + 1) * P)
+                nc.sync.dma_start(out=code_rows[:, both], in_=o_codes[:, both])
 
         early = [sb([P, 2, HALF], F32, "early%d" % t) for t in range(PACK)]
         back = [bank(free, [P, 2, P], "back%d" % free) for free in (2, 3)]
@@ -328,7 +337,7 @@ def tile_picked_painn8_none_po_kernel(
                 in_=back[b][:].rearrange("p u a -> p a u"),
             )
 
-        with_p1 = sb([P, PACK, HALF], F32, "with_p1", tag="last")
+        with_p1 = sb([P, PACK, HALF], F32, "with_p1", tag="y3_e3")
         for t in range(PACK):
             nc.vector.tensor_tensor(with_p1[:, t, :], ye[t][:].indirect(p1_sb[:, HALF // PER_COLUMN :]), qd_late[:, t, :], ADD)
 
@@ -336,30 +345,29 @@ def tile_picked_painn8_none_po_kernel(
             j0 = HALF + b * P
             nc.vector.tensor_tensor(dst, ye[t][:].indirect(p2_sb[:, j0 // PER_COLUMN : (j0 + P) // PER_COLUMN]), with_p1[:, t, b * P : (b + 1) * P], ADD)
 
-        def round_z(copy, z_b, z_f):
-            copy(out=z_b[:].rearrange("p (c a t) -> p c t a", a=4, t=PACK), in_=z_f.rearrange("p t (c a) -> p c t a", a=4))
-
         z_f2 = sb([P, PACK, P], F32, "z_f2")
         for t in range(PACK):
             with_p2(0, t, z_f2[:, t, :])
-        z_b2 = sb([P, PACK * P], BF16, "z_b2")
-        round_z(nc.scalar.copy, z_b2, z_f2[:])
-        q_early = quantise_z(0, HALF, z_early)
+        z_b2 = interleave(nc.scalar.copy, "z_b2", z_f2[:])
+        zq_early = quantise_z(0, HALF, z_early)
         z_f3 = sb([P, PACK, P], F32, "z_f3", tag="z_early")
-        for t in range(PACK):
+        for t in range(2):
             with_p2(1, t, z_f3[:, t, :])
-            if t == 1:
-                q_2 = quantise_z(HALF, P, z_b2)
-        z_b3 = sb([P, PACK * P], BF16, "z_b3")
-        round_z(nc.vector.tensor_copy, z_b3, z_f3[:])
-        q_3 = quantise_z(HALF + P, P, z_b3)
-        o_early = multiply(0, HALF, q_early, 0)
-        o_2 = multiply(HALF, P, q_2, 4)
-        planes(0, o_early[:, :, :P], nc.scalar.copy)
-        o_3 = multiply(HALF + P, P, q_3, 6)
-        planes(HALF, o_2[:], nc.vector.tensor_copy)
-        planes(P, o_early[:, :, P:], nc.scalar.copy, "z_c%d" % (HALF + P))
-        planes(HALF + P, o_3[:], nc.vector.tensor_copy)
+        zq_2 = quantise_z(HALF, P, z_b2)
+        for t in range(2, PACK):
+            with_p2(1, t, z_f3[:, t, :])
+        zq_3 = quantise_z(HALF + P, P, interleave(nc.vector.tensor_copy, "z_b3", z_f3[:]))
+
+        o_early = multiply(0, HALF, zq_early, 0)
+        o_2 = multiply(HALF, P, zq_2, 4)
+        planes(0, interleave(nc.scalar.copy, "o_b0", o_early[:, :, :P]))
+        o_3 = multiply(HALF + P, P, zq_3, 6)
+        o_b1 = interleave(nc.vector.tensor_copy, "o_b1", o_early[:, :, P:])
+        o_b2 = interleave(nc.vector.tensor_copy, "o_b2", o_2[:])
+        planes(1, o_b1)
+        o_b3 = interleave(nc.vector.tensor_copy, "o_b3", o_3[:])
+        planes(2, o_b2)
+        planes(3, o_b3)
         for r in range(PACK):
             queue = nc.scalar if r % 2 else nc.sync
             queue.dma_start(out=out_2[0, r:BLOCKS:PACK, :].bitcast(I32), in_=o_scales[r:P:QUADRANT, :].bitcast(I32))

@@ -67,9 +67,9 @@ def tile_picked_painn8_none_po_kernel(
         w3_raw = [sb([P, 2, H], F32, "w3_raw%d" % h) for h in range(2)]
         w2_raw = sb([P, PACK, H], F32, "w2_raw")
 
-        nc.vector.memset(xs[:].bitcast(I32), 0)
-        nc.gpsimd.memset(w1s[:].bitcast(I32), 0)
+        nc.gpsimd.memset(xs[:].bitcast(I32), 0)
         nc.gpsimd.memset(w4s[:].bitcast(I32), 0)
+        nc.gpsimd.memset(w1s[:].bitcast(I32), 0)
         q_sb = [sb([P, 2 * S if t < 2 else S], F32, "q_sb%d" % t) for t in range(PACK)]
         for t in range(2):
             nc.gpsimd.memset(q_sb[t][:, S:], 0.0)

@@ -15,18 +15,15 @@ U8 = mybir.dt.uint8
 FP8X4 = mybir.dt.float8_e4m3fn_x4
 FP4X4 = mybir.dt.float4_e2m1fn_x4
 MULT = mybir.AluOpType.mult
-ADD = mybir.AluOpType.add
 COPY = mybir.ActivationFunctionType.Copy
 
 P = 128
 PACK = 4
+RUNS = 8
 HALF = 256
 PER_COLUMN = 16
 QUADRANT = 32
 BLOCKS = K // 32
-TERM = 4 * HALF
-ON_W2 = 0
-ON_DIR1 = 8 * TERM
 
 
 def tile_picked_painn8_none_po_kernel(
@@ -62,87 +59,60 @@ def tile_picked_painn8_none_po_kernel(
         w4s = sb([P, N], U8, "w4s")
         o_scales = sb([P, S], U8, "o_scales")
         o_codes = sb([P, S], I32, "o_codes")
-        d1 = at(ON_DIR1 + TERM // 2, [P, S], F32, "d1")
+        d1 = sb([P, S], F32, "d1")
         d2 = sb([P, S], F32, "d2")
+        w2_raw = [sb([P, 2, H], F32, "w2_raw%d" % h) for h in range(2)]
         w3_raw = [sb([P, 2, H], F32, "w3_raw%d" % h) for h in range(2)]
-        w2_raw = sb([P, PACK, H], F32, "w2_raw")
 
         nc.gpsimd.memset(xs[:].bitcast(I32), 0)
         nc.gpsimd.memset(w4s[:].bitcast(I32), 0)
         nc.gpsimd.memset(w1s[:].bitcast(I32), 0)
-        q_sb = [sb([P, 2 * S if t < 2 else S], F32, "q_sb%d" % t) for t in range(PACK)]
-        for t in range(2):
+        w4s_d = sb([P, N], U8, "w4s_d")
+        nc.gpsimd.memset(w4s_d[:].bitcast(I32), 0)
+        q_sb = [sb([P, 2 * S if t < PACK - 1 else S], F32, "q_sb%d" % t) for t in range(PACK)]
+        for t in range(PACK - 1):
             nc.gpsimd.memset(q_sb[t][:, S:], 0.0)
-        ident = sb([P, P], F32, "ident")
-        make_identity(nc, ident[:])
 
+        x_rows = x_words[0].rearrange("p n t -> p (n t)").bitcast(I32)
+        w2_rows = w2.rearrange("(p j) c -> p j c", j=PACK)
         w3_rows = w3.rearrange("(p j) c -> p j c", j=PACK)
-        nc.sync.dma_start(out=w3_raw[0][:], in_=w3_rows[:, :2, :])
+        nc.sync.dma_start(out=xw[:, : T // 2], in_=x_rows[:, : T // 2])
         nc.sync.dma_start(offs_sb[:], offs)
         place_scale_rows(xs, x_scales[0])
         nc.sync.dma_start(out=w4s[:BLOCKS, :].bitcast(I32), in_=w4_scales[0].bitcast(I32))
-        nc.sync.dma_start(out=xw[:], in_=x_words[0].rearrange("p n t -> p (n t)").bitcast(I32))
-        nc.sync.dma_start(out=w3_raw[1][:], in_=w3_rows[:, 2:, :])
-        nc.sync.dma_start(p1_sb[:], p1)
-        place_scale_rows(w1s, w1_scales[0])
+        nc.sync.dma_start(out=xw[:, T // 2 :], in_=x_rows[:, T // 2 :])
         nc.sync.dma_start(out=w1w[:].bitcast(I32), in_=w1_words[0].bitcast(I32))
-        nc.sync.dma_start(out=d1[:], in_=dir1)
-        nc.sync.dma_start(out=w4w[:].bitcast(I32), in_=w4_words[0].bitcast(I32))
+        nc.sync.dma_start(out=w2_raw[0][:], in_=w2_rows[:, :2, :])
+        place_scale_rows(w1s, w1_scales[0])
+        nc.sync.dma_start(out=w2_raw[1][:], in_=w2_rows[:, 2:, :])
+        nc.sync.dma_start(p1_sb[:], p1)
+        nc.sync.dma_start(out=w3_raw[0][:], in_=w3_rows[:, :2, :])
         nc.sync.dma_start(p2_sb[:], p2)
+        nc.sync.dma_start(out=w3_raw[1][:], in_=w3_rows[:, 2:, :])
+        nc.sync.dma_start(out=d1[:], in_=dir1)
         nc.sync.dma_start(out=d2[:], in_=dir2)
-        nc.sync.dma_start(out=w2_raw[:], in_=w2.rearrange("(p j) c -> p j c", j=PACK))
-        d_late = [sb([P, 2], F32, "d_late%d" % i) for i in range(2)]
-        with nc.allow_non_contiguous_dma(reason="one direction a partition"):
-            for i, direction in enumerate((dir1, dir2)):
-                nc.sync.dma_start(out=d_late[i][:], in_=direction[0, HALF:].rearrange("(b a) -> a b", a=P))
-
-        def deal_words(words, name):
-            dealt = sb([P, 2 * H], U8, name)
-            nc.vector.tensor_copy(
-                out=dealt[:].bitcast(U16).rearrange("p (t m) -> p t m", t=PACK),
-                in_=words[:].bitcast(U16).rearrange("p (m t) -> p t m", t=PACK),
-            )
-            return dealt
-
-        def deal_scales(plane, name):
-            dealt = sb([P, H], U8, name)
-            nc.vector.tensor_copy(
-                out=dealt[:].rearrange("p (t m) -> p t m", t=PACK),
-                in_=plane[:].rearrange("p (m t) -> p t m", t=PACK),
-            )
-            return dealt
+        nc.sync.dma_start(out=w4w[:].bitcast(I32), in_=w4_words[0].bitcast(I32))
 
         xq_s = sb([P, S], U8, "xq_s")
         xq = sb([P, S], U32, "xq")
         nc.vector.tensor_copy(xq_s[:], xs[:].indirect(offs_sb[:]))
-        w4s_rows = deal_scales(w4s, "w4s_rows")
-        w4s_d = sb([P, N], U8, "w4s_d")
-        nc.gpsimd.memset(w4s_d[:].bitcast(I32), 0)
+        w4s_rows = sb([P, N], U8, "w4s_rows")
+        nc.vector.tensor_copy(
+            out=w4s_rows[:].rearrange("p (t m) -> p t m", t=PACK), in_=w4s[:].rearrange("p (m t) -> p t m", t=PACK)
+        )
         place_scale_rows(w4s_d, w4s_rows[:BLOCKS, :])
         nc.vector.tensor_copy(xq[:], xw[:].bitcast(U32).indirect(offs_sb[:]))
 
-        w3_b = sb([P, PACK * H], BF16, "w3_b")
-
-        def round_w3(copy, h, t0, t1):
-            copy(
-                out=w3_b[:].rearrange("p (t m j) -> p m t j", t=PACK, j=PACK)[:, :, t0:t1, 2 * h : 2 * h + 2],
-                in_=w3_raw[h][:].rearrange("p j (m t) -> p m t j", t=PACK)[:, :, t0:t1],
+        def deal_runs(packed, width, name):
+            dealt = sb([P, width], U8, name)
+            nc.vector.tensor_copy(
+                out=dealt[:].bitcast(I32).rearrange("p (t r i) -> p t r i", t=PACK, r=RUNS),
+                in_=packed[:].bitcast(I32).rearrange("p (r t i) -> p t r i", t=PACK, r=RUNS),
             )
+            return dealt
 
-        round_w3(nc.scalar.copy, 0, 0, PACK)
-        round_w3(nc.vector.tensor_copy, 1, 0, 1)
-        round_w3(nc.vector.tensor_copy, 1, 1, 2)
-        round_w3(nc.scalar.copy, 1, 2, PACK)
-        w3_c = sb([P, H], U32, "w3_c")
-        w3_s = sb([P, H], U8, "w3_s")
-        for t in range(PACK):
-            cols = slice(t * P, (t + 1) * P)
-            nc.vector.quantize_mx(
-                out=w3_c[:, cols].bitcast(FP8X4), scales=w3_s[:, cols], in_=w3_b[:, t * PACK * P : (t + 1) * PACK * P]
-            )
-        w1w_d = deal_words(w1w, "w1w_d")
-        w4w_d = deal_words(w4w, "w4w_d")
-        w1s_d = deal_scales(w1s, "w1s_d")
+        w1w_d = deal_runs(w1w, 2 * H, "w1w_d")
+        w1s_d = deal_runs(w1s, H, "w1s_d")
 
         def product(lhsT, lhsT_scale, name, number):
             acc = bank(number, [P, S], name)
@@ -151,161 +121,165 @@ def tile_picked_painn8_none_po_kernel(
             )
             return acc
 
-        for h in range(2):
-            cols = slice(h * HALF, (h + 1) * HALF)
-            acc = bank(h, [P, HALF], "q0_%d" % h)
-            nc.tensor.matmul_mx(
-                out=acc[:],
-                lhsT=w3_c[:, :P].bitcast(FP8X4),
-                lhsT_scale=w3_s[:, :P],
-                rhs=xq[:, cols].bitcast(FP8X4),
-                rhs_scale=xq_s[:, cols],
-                start=True,
-                stop=True,
-            )
-            nc.scalar.copy(out=q_sb[0][:, cols], in_=acc[:])
-        for t in range(1, PACK):
-            cols = slice(t * P, (t + 1) * P)
-            acc = product(w3_c[:, cols].bitcast(FP8X4), w3_s[:, cols], "q%d" % t, t)
-            nc.scalar.copy(out=q_sb[t][:, :S], in_=acc[:])
-        w2_b = at(ON_W2 + TERM // 2, [P, PACK * H], BF16, "w2_b")
-        for h in range(2):
-            nc.scalar.copy(
-                out=w2_b[:].rearrange("p (t m j) -> p m t j", t=PACK, j=PACK)[:, h * P // 2 : (h + 1) * P // 2],
-                in_=w2_raw[:, :, h * HALF : (h + 1) * HALF].rearrange("p j (m t) -> p m t j", t=PACK),
-            )
-        after_w2 = sb([P, PACK, S], F32, "after_w2", tag="w2_raw")
-        y3_e3 = sb([P, 2, S], F32, "y3_e3")
-        y_sb = [after_w2[:, t, :] for t in range(PACK - 1)] + [y3_e3[:, 0, :]]
-        w2_c = sb([P, H], U32, "w2_c")
-        w2_s = sb([P, H], U8, "w2_s")
-        lists = (p1_sb, p2_sb)
-
-        def directed(t, i, term):
-            n = term.shape[1]
-            nc.vector.tensor_tensor(term, q_sb[t][:].indirect(lists[i][:, : n // PER_COLUMN]), (d1, d2)[i][:, :n], MULT)
-
-        turned = [bank(4 + u, [P, 2, 2, P], "turned%d" % u) for u in range(2)]
-        late01 = bank(6, [P, 2, 2, P], "late01")
-
-        def turn(dst, src, start, stop):
-            nc.tensor.matmul(dst, src, ident[:], start=start, stop=stop, is_transpose=True)
-
-        def turn_early(t, i, term):
-            for b in range(2):
-                turn(turned[t // 2][:, b, t % 2, :], term[:, b * P : (b + 1) * P], t % 2 == 0 and i == 0 and b == 0, False)
-
-        def y_tile(t):
-            acc = product(w1w_d[:, 2 * t * P : 2 * (t + 1) * P].bitcast(FP4X4), w1s_d[:, t * P : (t + 1) * P], "y%d" % t, t)
-            nc.scalar.copy(out=y_sb[t], in_=acc[:])
-
-        e_sb = []
-
-        def e_tile(t):
-            cols = slice(t * P, (t + 1) * P)
-            acc = product(w2_c[:, cols].bitcast(FP8X4), w2_s[:, cols], "e%d" % t, t)
-            e_t = sb([P, S], F32, "e_sb%d" % t)[:] if t < PACK - 1 else y3_e3[:, 1, :]
-            nc.scalar.copy(out=e_t, in_=acc[:])
-            e_sb.append(e_t)
-
-        y_tile(0)
-        y_tile(1)
-        for t in range(2):
-            for i in range(2):
-                term = sb([P, S], F32, "qd%d_%d" % (t, i))[:]
-                directed(t, i, term)
-                for b in range(2):
-                    turn(late01[:, t, b, :], term[:, (2 + b) * P : (3 + b) * P], t == 0 and i == 0 and b == 0, t == 1 and i == 1 and b == 1)
-                turn_early(t, i, term)
-        for u in range(2):
-            cols = slice(u * HALF, (u + 1) * HALF)
-            nc.vector.quantize_mx(out=w2_c[:, cols].bitcast(FP8X4), scales=w2_s[:, cols], in_=w2_b[:, u * PACK * HALF : (u + 1) * PACK * HALF])
-        e_tile(0)
-        y_tile(2)
-        e_tile(1)
-        y_tile(3)
-        e_tile(2)
-        e_tile(3)
-        flat01 = after_w2[:, PACK - 1, :].rearrange("p (t b a) -> p t b a", t=2, b=2)
-        qd_late = sb([P, PACK, HALF], F32, "qd_late")
-        nc.scalar.copy(out=flat01, in_=late01[:])
-        again01 = bank(6, [P, 2, 2, P], "again01")
-        for t in range(2):
-            for b in range(2):
-                nc.tensor.transpose(again01[:, t, b, :], flat01[:, t, b, :], ident[:])
-        nc.scalar.copy(out=qd_late[:, :2, :], in_=again01[:].rearrange("p t b a -> p t (b a)"))
-        early_terms = []
-        for n in range(PACK):
-            early_terms.append(at(ON_W2 + n * TERM, [P, HALF], F32, "early_term%d" % n)[:])
-            directed(2 + n // 2, n % 2, early_terms[n])
-        late_q = []
-        for n in range(PACK):
-            offset = ON_DIR1 + n * TERM if n < PACK - 1 else ON_W2 + PACK * TERM
-            late_q.append(at(offset, [P, HALF], F32, "late_q%d" % n)[:])
-            nc.vector.tensor_copy(late_q[n], q_sb[2 + n // 2][:].indirect(lists[n % 2][:, HALF // PER_COLUMN :]))
-
-        ye = []
+        ye = [sb([P, 2 * S], F32, "ye%d" % t) for t in range(PACK)]
         for t in range(PACK):
-            ye_t = sb([P, S], F32, "ye%d" % t, tag="d2" if t == 0 else None)
-            nc.gpsimd.tensor_tensor(ye_t[:], e_sb[t], y_sb[t], MULT)
-            ye.append(ye_t)
+            acc = product(w1w_d[:, 2 * t * P : 2 * (t + 1) * P].bitcast(FP4X4), w1s_d[:, t * P : (t + 1) * P], "y%d" % t, t)
+            nc.scalar.copy(out=ye[t][:, S:], in_=acc[:])
 
-        for n in range(PACK):
-            turn_early(2 + n // 2, n % 2, early_terms[n])
-        flat23 = sb([P, 2, 2, 2, P], F32, "flat23")
-        for odd in range(2):
-            unscaled = bank(0 if odd else 7, [P, 2, 2, P], "unscaled%d" % odd)
+        def round_rows(raw, rounded, h, t0, t1):
+            nc.vector.tensor_copy(
+                out=rounded[:].rearrange("p (t r i j) -> p t r i j", t=PACK, r=RUNS, j=PACK)[:, t0:t1, :, :, 2 * h : 2 * h + 2],
+                in_=raw[h][:].rearrange("p j (r t i) -> p t r i j", r=RUNS, t=PACK)[:, t0:t1],
+            )
+
+        def quantise_weight(raw, rounded, name):
+            codes = sb([P, H], U32, name + "_c")
+            scales = sb([P, H], U8, name + "_s")
+
+            def quantise(t0, t1):
+                cols = slice(t0 * P, t1 * P)
+                nc.vector.quantize_mx(
+                    out=codes[:, cols].bitcast(FP8X4), scales=scales[:, cols], in_=rounded[:, t0 * PACK * P : t1 * PACK * P]
+                )
+
+            round_rows(raw, rounded, 0, 0, PACK)
+            round_rows(raw, rounded, 1, 0, 1)
+            round_rows(raw, rounded, 1, 1, 2)
+            quantise(0, 1)
+            round_rows(raw, rounded, 1, 2, PACK)
+            quantise(1, 2)
+            quantise(2, PACK)
+            return codes, scales
+
+        def weight_product(quantised, t, name, number):
+            cols = slice(t * P, (t + 1) * P)
+            return product(quantised[0][:, cols].bitcast(FP8X4), quantised[1][:, cols], name, number)
+
+        w2_q = quantise_weight(w2_raw, sb([P, PACK * H], BF16, "w2_b"), "w2")
+        e_ps = [weight_product(w2_q, t, "e%d" % t, PACK + t) for t in range(PACK)]
+
+        def gate(t):
+            nc.vector.tensor_tensor(ye[t][:, :S], e_ps[t][:], ye[t][:, S:], MULT)
+
+        gate(0)
+        gate(1)
+        w3_b = at(0, [P, PACK * H], BF16, "w3_b")
+        w3_q = quantise_weight(w3_raw, w3_b, "w3")
+        q_ps = [weight_product(w3_q, t, "q%d" % t, t) for t in range(PACK)]
+        gate(2)
+        gate(3)
+        ident = at(3 * 2 * H, [P, P], F32, "ident")
+        make_identity(nc, ident[:])
+
+        lists = (p1_sb, p2_sb)
+        dirs = (d1, d2)
+        turned = [bank(PACK + b, [P, PACK, P], "turned%d" % b) for b in range(PACK)]
+        seen = [0] * PACK
+
+        def turn(t, term, j0):
+            for c in range(term.shape[1] // P):
+                b = j0 // P + c
+                nc.tensor.matmul(
+                    turned[b][:, t, :],
+                    term[:, c * P : (c + 1) * P],
+                    ident[:],
+                    start=seen[b] == 0,
+                    stop=seen[b] == 4 * PACK - 1,
+                    is_transpose=True,
+                )
+                seen[b] = seen[b] + 1
+
+        def entries(i, j0, n):
+            return lists[i][:, j0 // PER_COLUMN : (j0 + n) // PER_COLUMN]
+
+        def fetch_ye(t, i, j0, n, tag=None):
+            term = sb([P, n], F32, "ye_term%d_%d_%d" % (t, i, j0), tag=tag)
+            nc.scalar.activation(term[:], ye[t][:].indirect(entries(i, j0, n)), COPY)
+            turn(t, term[:], j0)
+
+        def fetch_q(t, i, j0, n):
+            term = sb([P, n], F32, "q_term%d_%d_%d" % (t, i, j0))
+            nc.vector.tensor_tensor(term[:], q_sb[t][:].indirect(entries(i, j0, n)), dirs[i][:, j0 : j0 + n], MULT)
+            turn(t, term[:], j0)
+
+        for i in range(2):
+            fetch_ye(0, i, 0, S, "ring%d" % i)
+        for t in range(PACK):
+            nc.scalar.copy(out=q_sb[t][:, :S], in_=q_ps[t][:])
+        for i in range(2):
+            fetch_q(0, i, 0, S)
+        for t in range(1, PACK - 1):
             for i in range(2):
-                for b in range(2):
-                    nc.tensor.transpose(unscaled[:, i, b, :], late_q[2 * odd + i][:, b * P : (b + 1) * P], ident[:])
-            for b in range(2):
-                for i in range(2):
-                    nc.scalar.activation(flat23[:, odd, b, i, :], unscaled[:, i, b, :], COPY, scale=d_late[i][:, b : b + 1])
-        again23 = bank(7, [P, 2, 2, P], "again23")
-        for odd in range(2):
-            for b in range(2):
-                for i in range(2):
-                    turn(again23[:, odd, b, :], flat23[:, odd, b, i, :], i == 0, i == 1)
-        nc.scalar.copy(out=qd_late[:, 2:, :], in_=again23[:].rearrange("p t b a -> p t (b a)"))
+                fetch_ye(t, i, 0, S, "ring%d" % i)
+                fetch_q(t, i, 0, S)
+        for j0 in (0, HALF):
+            for i in range(2):
+                fetch_ye(PACK - 1, i, j0, HALF, "ring%d" % i)
+            for i in range(2):
+                fetch_q(PACK - 1, i, j0, HALF)
+
+        w4w_d = sb([P, 2 * N], U8, "w4w_d")
+        nc.vector.tensor_copy(
+            out=w4w_d[:].bitcast(U16).rearrange("p (t m) -> p t m", t=PACK),
+            in_=w4w[:].bitcast(U16).rearrange("p (m t) -> p t m", t=PACK),
+        )
 
         out_rows = out_0.rearrange("(p t) j -> p t j", t=PACK)
         code_rows = out_1[0].rearrange("p n t -> p (n t)").bitcast(I32)
+        z_c = sb([P, S], U32, "z_c")
+        z_s = sb([P, S], U8, "z_s")
 
-        def quantise_z(j0, n, z_b):
-            z_c = sb([P, n], U32, "z_c%d" % j0)
-            z_s = sb([P, n], U8, "z_s%d" % j0)
-            for b in range(n // P):
-                cols = slice(b * P, (b + 1) * P)
-                nc.vector.quantize_mx(out=z_c[:, cols].bitcast(FP8X4), scales=z_s[:, cols], in_=z_b[:, b * PACK * P : (b + 1) * PACK * P])
-            return z_c, z_s
-
-        def multiply(j0, n, z_q, first_bank):
-            cols = slice(j0, j0 + n)
-            z_c, z_s = z_q
-            o_f = sb([P, PACK, n], F32, "o_f%d" % j0)
+        def round_turned(copy, b):
+            zt = sb([P, H], BF16, "zt%d" % b)
+            copy(
+                out=zt[:].rearrange("a (r t i) -> a t r i", r=RUNS, t=PACK),
+                in_=turned[b][:].rearrange("a t (r i) -> a t r i", r=RUNS),
+            )
+            back = bank(b, [P, 2, P], "back%d" % b)
             for u in range(2):
-                acc = bank(first_bank + u, [P, 2, n], "o%d_%d" % (j0, u))
-                for odd in range(2):
-                    t = 2 * u + odd
-                    nc.tensor.matmul_mx(
-                        out=acc[:, odd, :],
-                        lhsT=w4w_d[:, 2 * t * P : 2 * (t + 1) * P].bitcast(FP4X4),
-                        lhsT_scale=w4s_d[:, t * P : (t + 1) * P],
-                        rhs=z_c[:].bitcast(FP8X4),
-                        rhs_scale=z_s[:],
-                        start=True,
-                        stop=True,
-                    )
-                nc.scalar.copy(out=o_f[:, 2 * u : 2 * u + 2, :], in_=acc[:])
-                if n == HALF:
-                    nc.sync.dma_start(out=out_rows[:, 2 * u : 2 * u + 2, cols], in_=o_f[:, 2 * u : 2 * u + 2, :])
-            if n != HALF:
-                nc.sync.dma_start(out=out_rows[:, :, cols], in_=o_f[:])
-            return o_f
+                nc.tensor.transpose(back[:, u, :], zt[:].bitcast(F32)[:, u : 2 * P : 2], ident[:])
+            return back
 
-        def interleave(copy, name, values):
-            rounded = sb([P, PACK * P], BF16, name)
-            copy(out=rounded[:].rearrange("p (c a t) -> p c t a", a=4, t=PACK), in_=values.rearrange("p t (c a) -> p c t a", a=4))
+        def lay_z(copy, b, back):
+            z_b = sb([P, PACK * P], BF16, "z_b%d" % b)
+            copy(out=z_b[:].bitcast(F32).rearrange("p (a u) -> p a u", u=2), in_=back[:].rearrange("p u a -> p a u"))
+            return z_b
+
+        def quantise_z(b, z_b):
+            cols = slice(b * P, (b + 1) * P)
+            nc.vector.quantize_mx(out=z_c[:, cols].bitcast(FP8X4), scales=z_s[:, cols], in_=z_b[:])
+
+        def multiply(b):
+            cols = slice(b * P, (b + 1) * P)
+            acc = bank(PACK + b, [P, PACK, P], "o%d" % b)
+            for t in range(PACK):
+                nc.tensor.matmul_mx(
+                    out=acc[:, t, :],
+                    lhsT=w4w_d[:, 2 * t * P : 2 * (t + 1) * P].bitcast(FP4X4),
+                    lhsT_scale=w4s_d[:, t * P : (t + 1) * P],
+                    rhs=z_c[:, cols].bitcast(FP8X4),
+                    rhs_scale=z_s[:, cols],
+                    start=True,
+                    stop=True,
+                )
+            return acc
+
+        o_f = [sb([P, PACK, HALF], F32, "o_f%d" % h) for h in range(2)]
+
+        def leave(copy, b, acc):
+            part = o_f[b // 2][:, :, (b % 2) * P : (b % 2 + 1) * P]
+            copy(out=part, in_=acc[:])
+            if b == 1:
+                nc.sync.dma_start(out=out_rows[:, :, :HALF], in_=o_f[0][:])
+            if b > 1:
+                nc.sync.dma_start(out=out_rows[:, :, b * P : (b + 1) * P], in_=part)
+            return part
+
+        def interleave(b, values):
+            rounded = sb([P, PACK * P], BF16, "o_b%d" % b)
+            nc.vector.tensor_copy(
+                out=rounded[:].rearrange("p (c a t) -> p c t a", a=4, t=PACK), in_=values.rearrange("p t (c a) -> p c t a", a=4)
+            )
             return rounded
 
         def planes(b, o_b):
@@ -315,59 +289,35 @@ def tile_picked_painn8_none_po_kernel(
                 both = slice((b - 1) * P, (b + 1) * P)
                 nc.sync.dma_start(out=code_rows[:, both], in_=o_codes[:, both])
 
-        early = [sb([P, 2, HALF], F32, "early%d" % t) for t in range(PACK)]
-        back = [bank(free, [P, 2, P], "back%d" % free) for free in (2, 3)]
-        for t in range(PACK):
-            for i in range(2):
-                nc.vector.tensor_copy(early[t][:, i, :], ye[t][:].indirect(lists[i][:, : HALF // PER_COLUMN]))
-                for b in range(2):
-                    turn(turned[t // 2][:, b, t % 2, :], early[t][:, i, b * P : (b + 1) * P], False, t % 2 == 1 and i == 1 and b == 1)
-            if t % 2 == 1:
-                u = t // 2
-                for b in range(2):
-                    pairs = sb([P, 2 * P], BF16, "pairs%d_%d" % (u, b), tag="z_b2" if u and b else None)
-                    nc.scalar.copy(
-                        out=pairs[:].rearrange("a (p odd) -> a p odd", odd=2), in_=turned[u][:, b].rearrange("a odd p -> a p odd")
-                    )
-                    nc.tensor.transpose(back[b][:, u, :], pairs[:].bitcast(F32), ident[:])
-        z_early = sb([P, PACK * HALF], BF16, "z_early")
-        for b in range(2):
-            nc.scalar.copy(
-                out=z_early[:].bitcast(F32)[:, 2 * b * P : 2 * (b + 1) * P].rearrange("p (a u) -> p a u", u=2),
-                in_=back[b][:].rearrange("p u a -> p a u"),
-            )
-
-        with_p1 = sb([P, PACK, HALF], F32, "with_p1", tag="y3_e3")
-        for t in range(PACK):
-            nc.vector.tensor_tensor(with_p1[:, t, :], ye[t][:].indirect(p1_sb[:, HALF // PER_COLUMN :]), qd_late[:, t, :], ADD)
-
-        def with_p2(b, t, dst):
-            j0 = HALF + b * P
-            nc.vector.tensor_tensor(dst, ye[t][:].indirect(p2_sb[:, j0 // PER_COLUMN : (j0 + P) // PER_COLUMN]), with_p1[:, t, b * P : (b + 1) * P], ADD)
-
-        z_f2 = sb([P, PACK, P], F32, "z_f2")
-        for t in range(PACK):
-            with_p2(0, t, z_f2[:, t, :])
-        z_b2 = interleave(nc.scalar.copy, "z_b2", z_f2[:])
-        zq_early = quantise_z(0, HALF, z_early)
-        z_f3 = sb([P, PACK, P], F32, "z_f3", tag="z_early")
-        for t in range(2):
-            with_p2(1, t, z_f3[:, t, :])
-        zq_2 = quantise_z(HALF, P, z_b2)
-        for t in range(2, PACK):
-            with_p2(1, t, z_f3[:, t, :])
-        zq_3 = quantise_z(HALF + P, P, interleave(nc.vector.tensor_copy, "z_b3", z_f3[:]))
-
-        o_early = multiply(0, HALF, zq_early, 0)
-        o_2 = multiply(HALF, P, zq_2, 4)
-        planes(0, interleave(nc.scalar.copy, "o_b0", o_early[:, :, :P]))
-        o_3 = multiply(HALF + P, P, zq_3, 6)
-        o_b1 = interleave(nc.vector.tensor_copy, "o_b1", o_early[:, :, P:])
-        o_b2 = interleave(nc.vector.tensor_copy, "o_b2", o_2[:])
-        planes(1, o_b1)
-        o_b3 = interleave(nc.vector.tensor_copy, "o_b3", o_3[:])
-        planes(2, o_b2)
-        planes(3, o_b3)
+        on_s, on_v = nc.scalar.copy, nc.vector.tensor_copy
+        back0 = round_turned(on_s, 0)
+        back1 = round_turned(on_s, 1)
+        z0 = lay_z(on_s, 0, back0)
+        z1 = lay_z(on_s, 1, back1)
+        back2 = round_turned(on_v, 2)
+        back3 = round_turned(on_s, 3)
+        quantise_z(0, z0)
+        quantise_z(1, z1)
+        acc0 = multiply(0)
+        acc1 = multiply(1)
+        z2 = lay_z(on_v, 2, back2)
+        o0 = leave(on_s, 0, acc0)
+        z3 = lay_z(on_s, 3, back3)
+        o1 = leave(on_v, 1, acc1)
+        quantise_z(2, z2)
+        acc2 = multiply(2)
+        b0 = interleave(0, o0)
+        quantise_z(3, z3)
+        acc3 = multiply(3)
+        o2 = leave(on_s, 2, acc2)
+        b1 = interleave(1, o1)
+        planes(0, b0)
+        o3 = leave(on_s, 3, acc3)
+        b2 = interleave(2, o2)
+        planes(1, b1)
+        b3 = interleave(3, o3)
+        planes(2, b2)
+        planes(3, b3)
         for r in range(PACK):
             queue = nc.scalar if r % 2 else nc.sync
             queue.dma_start(out=out_2[0, r:BLOCKS:PACK, :].bitcast(I32), in_=o_scales[r:P:QUADRANT, :].bitcast(I32))

@@ -15,6 +15,7 @@ U8 = mybir.dt.uint8
 FP8X4 = mybir.dt.float8_e4m3fn_x4
 FP4X4 = mybir.dt.float4_e2m1fn_x4
 MULT = mybir.AluOpType.mult
+ADD = mybir.AluOpType.add
 COPY = mybir.ActivationFunctionType.Copy
 
 P = 128
@@ -24,6 +25,7 @@ HALF = 256
 PER_COLUMN = 16
 QUADRANT = 32
 BLOCKS = K // 32
+RING = 2 * PACK * H
 
 
 def tile_picked_painn8_none_po_kernel(
@@ -61,58 +63,50 @@ def tile_picked_painn8_none_po_kernel(
         o_codes = sb([P, S], I32, "o_codes")
         d1 = sb([P, S], F32, "d1")
         d2 = sb([P, S], F32, "d2")
-        w2_raw = [sb([P, 2, H], F32, "w2_raw%d" % h) for h in range(2)]
-        w3_raw = [sb([P, 2, H], F32, "w3_raw%d" % h) for h in range(2)]
+        w2_raw = [sb([P, PACK, HALF], F32, "w2_raw%d" % h) for h in range(2)]
+        w3_raw = [sb([P, PACK, HALF], F32, "w3_raw%d" % h) for h in range(2)]
 
         nc.gpsimd.memset(xs[:].bitcast(I32), 0)
         nc.gpsimd.memset(w4s[:].bitcast(I32), 0)
         nc.gpsimd.memset(w1s[:].bitcast(I32), 0)
-        w4s_d = sb([P, N], U8, "w4s_d")
-        nc.gpsimd.memset(w4s_d[:].bitcast(I32), 0)
-        q_sb = [sb([P, 2 * S if t < PACK - 1 else S], F32, "q_sb%d" % t) for t in range(PACK)]
-        for t in range(PACK - 1):
+        q_sb = [sb([P, 2 * S if t < 2 else S], F32, "q_sb%d" % t) for t in range(PACK)]
+        for t in range(2):
             nc.gpsimd.memset(q_sb[t][:, S:], 0.0)
 
         x_rows = x_words[0].rearrange("p n t -> p (n t)").bitcast(I32)
         w2_rows = w2.rearrange("(p j) c -> p j c", j=PACK)
         w3_rows = w3.rearrange("(p j) c -> p j c", j=PACK)
-        nc.sync.dma_start(out=xw[:, : T // 2], in_=x_rows[:, : T // 2])
+        nc.sync.dma_start(out=xw[:, : T // 4], in_=x_rows[:, : T // 4])
         nc.sync.dma_start(offs_sb[:], offs)
         place_scale_rows(xs, x_scales[0])
-        nc.sync.dma_start(out=w4s[:BLOCKS, :].bitcast(I32), in_=w4_scales[0].bitcast(I32))
-        nc.sync.dma_start(out=xw[:, T // 2 :], in_=x_rows[:, T // 2 :])
+        nc.sync.dma_start(out=xw[:, T // 4 :], in_=x_rows[:, T // 4 :])
+        nc.sync.dma_start(out=w2_raw[0][:], in_=w2_rows[:, :, :HALF])
         nc.sync.dma_start(out=w1w[:].bitcast(I32), in_=w1_words[0].bitcast(I32))
-        nc.sync.dma_start(out=w2_raw[0][:], in_=w2_rows[:, :2, :])
         place_scale_rows(w1s, w1_scales[0])
-        nc.sync.dma_start(out=w2_raw[1][:], in_=w2_rows[:, 2:, :])
+        nc.sync.dma_start(out=w2_raw[1][:], in_=w2_rows[:, :, HALF:])
+        nc.sync.dma_start(out=w3_raw[0][:], in_=w3_rows[:, :, :HALF])
         nc.sync.dma_start(p1_sb[:], p1)
-        nc.sync.dma_start(out=w3_raw[0][:], in_=w3_rows[:, :2, :])
         nc.sync.dma_start(p2_sb[:], p2)
-        nc.sync.dma_start(out=w3_raw[1][:], in_=w3_rows[:, 2:, :])
+        nc.sync.dma_start(out=w3_raw[1][:], in_=w3_rows[:, :, HALF:])
         nc.sync.dma_start(out=d1[:], in_=dir1)
         nc.sync.dma_start(out=d2[:], in_=dir2)
+        nc.sync.dma_start(out=w4s[0:P:8, :].bitcast(I32), in_=w4_scales[0].bitcast(I32))
         nc.sync.dma_start(out=w4w[:].bitcast(I32), in_=w4_words[0].bitcast(I32))
 
         xq_s = sb([P, S], U8, "xq_s")
         xq = sb([P, S], U32, "xq")
         nc.vector.tensor_copy(xq_s[:], xs[:].indirect(offs_sb[:]))
-        w4s_rows = sb([P, N], U8, "w4s_rows")
-        nc.vector.tensor_copy(
-            out=w4s_rows[:].rearrange("p (t m) -> p t m", t=PACK), in_=w4s[:].rearrange("p (m t) -> p t m", t=PACK)
-        )
-        place_scale_rows(w4s_d, w4s_rows[:BLOCKS, :])
         nc.vector.tensor_copy(xq[:], xw[:].bitcast(U32).indirect(offs_sb[:]))
 
-        def deal_runs(packed, width, name):
-            dealt = sb([P, width], U8, name)
+        def deal_runs(packed, dealt):
             nc.vector.tensor_copy(
                 out=dealt[:].bitcast(I32).rearrange("p (t r i) -> p t r i", t=PACK, r=RUNS),
                 in_=packed[:].bitcast(I32).rearrange("p (r t i) -> p t r i", t=PACK, r=RUNS),
             )
             return dealt
 
-        w1w_d = deal_runs(w1w, 2 * H, "w1w_d")
-        w1s_d = deal_runs(w1s, H, "w1s_d")
+        w1w_d = deal_runs(w1w, sb([P, 2 * H], U8, "w1w_d"))
+        w1s_d = deal_runs(w1s, sb([P, H], U8, "w1s_d"))
 
         def product(lhsT, lhsT_scale, name, number):
             acc = bank(number, [P, S], name)
@@ -122,78 +116,113 @@ def tile_picked_painn8_none_po_kernel(
             return acc
 
         ye = [sb([P, 2 * S], F32, "ye%d" % t) for t in range(PACK)]
-        for t in range(PACK):
-            acc = product(w1w_d[:, 2 * t * P : 2 * (t + 1) * P].bitcast(FP4X4), w1s_d[:, t * P : (t + 1) * P], "y%d" % t, t)
+
+        def y_tile(t, number):
+            acc = product(w1w_d[:, 2 * t * P : 2 * (t + 1) * P].bitcast(FP4X4), w1s_d[:, t * P : (t + 1) * P], "y%d" % t, number)
             nc.scalar.copy(out=ye[t][:, S:], in_=acc[:])
 
-        def round_rows(raw, rounded, h, t0, t1):
-            nc.vector.tensor_copy(
-                out=rounded[:].rearrange("p (t r i j) -> p t r i j", t=PACK, r=RUNS, j=PACK)[:, t0:t1, :, :, 2 * h : 2 * h + 2],
-                in_=raw[h][:].rearrange("p j (r t i) -> p t r i j", r=RUNS, t=PACK)[:, t0:t1],
+        def dealt_views(raw, rounded, h):
+            runs = slice(h * RUNS // 2, (h + 1) * RUNS // 2)
+            return (
+                rounded[:].rearrange("p (t r i j) -> p t r i j", t=PACK, r=RUNS, j=PACK)[:, :, runs],
+                raw[h][:].rearrange("p j (r t i) -> p t r i j", r=RUNS // 2, t=PACK),
             )
 
-        def quantise_weight(raw, rounded, name):
-            codes = sb([P, H], U32, name + "_c")
-            scales = sb([P, H], U8, name + "_s")
+        def round_rows(copy, raw, rounded, h, t0, t1):
+            out, in_ = dealt_views(raw, rounded, h)
+            copy(out=out[:, t0:t1], in_=in_[:, t0:t1])
 
-            def quantise(t0, t1):
-                cols = slice(t0 * P, t1 * P)
-                nc.vector.quantize_mx(
-                    out=codes[:, cols].bitcast(FP8X4), scales=scales[:, cols], in_=rounded[:, t0 * PACK * P : t1 * PACK * P]
-                )
+        def quantise(rounded, t0, t1, codes, scales):
+            nc.vector.quantize_mx(out=codes[:].bitcast(FP8X4), scales=scales[:], in_=rounded[:, t0 * PACK * P : t1 * PACK * P])
+            return [(codes[:, c * P : (c + 1) * P], scales[:, c * P : (c + 1) * P]) for c in range(t1 - t0)]
 
-            round_rows(raw, rounded, 0, 0, PACK)
-            round_rows(raw, rounded, 1, 0, 1)
-            round_rows(raw, rounded, 1, 1, 2)
-            quantise(0, 1)
-            round_rows(raw, rounded, 1, 2, PACK)
-            quantise(1, 2)
-            quantise(2, PACK)
-            return codes, scales
+        def quantise_tile(rounded, t, name):
+            return quantise(rounded, t, t + 1, sb([P, P], U32, "%s_c%d" % (name, t)), sb([P, P], U8, "%s_s%d" % (name, t)))
 
-        def weight_product(quantised, t, name, number):
-            cols = slice(t * P, (t + 1) * P)
-            return product(quantised[0][:, cols].bitcast(FP8X4), quantised[1][:, cols], name, number)
+        def weight_product(quantised, name, number):
+            return product(quantised[0].bitcast(FP8X4), quantised[1], name, number)
 
-        w2_q = quantise_weight(w2_raw, sb([P, PACK * H], BF16, "w2_b"), "w2")
-        e_ps = [weight_product(w2_q, t, "e%d" % t, PACK + t) for t in range(PACK)]
+        on_s, on_v = nc.scalar.copy, nc.vector.tensor_copy
+        w2_b = sb([P, PACK * H], BF16, "w2_b")
+        round_rows(on_s, w2_raw, w2_b, 0, 0, PACK)
+        round_rows(on_v, w2_raw, w2_b, 1, 0, 1)
+        round_rows(on_v, w2_raw, w2_b, 1, 1, 2)
+        w2_q = quantise(w2_b, 0, 1, at(2 * H - 2 * P, [P, P], U32, "w2_c0"), at(6 * H - P // 2, [P, P], U8, "w2_s0"))
+        round_rows(on_v, w2_raw, w2_b, 1, 2, PACK)
+        w2_q = w2_q + quantise_tile(w2_b, 1, "w2")
+        for t in range(2):
+            y_tile(t, t)
+        e_ps = [weight_product(w2_q[t], "e%d" % t, PACK + t) for t in range(2)]
 
         def gate(t):
             nc.vector.tensor_tensor(ye[t][:, :S], e_ps[t][:], ye[t][:, S:], MULT)
 
         gate(0)
         gate(1)
-        w3_b = at(0, [P, PACK * H], BF16, "w3_b")
-        w3_q = quantise_weight(w3_raw, w3_b, "w3")
-        q_ps = [weight_product(w3_q, t, "q%d" % t, t) for t in range(PACK)]
+        w3_b = [at(t * 2 * H, [P, H], BF16, "w3_b%d" % t) for t in range(PACK)]
+
+        def w3_views(t, h):
+            return (
+                w3_b[t][:, h * HALF : (h + 1) * HALF].rearrange("p (r i j) -> p r i j", r=RUNS // 2, j=PACK),
+                w3_raw[h][:].rearrange("p j (r t i) -> p t r i j", r=RUNS // 2, t=PACK)[:, t],
+            )
+
+        for t in range(PACK):
+            out, in_ = w3_views(t, 0)
+            nc.gpsimd.tensor_scalar(out, in_, 1.0, 0.0, op0=MULT, op1=ADD)
+        w3_q = []
+        for t in range(PACK + 1):
+            if t < PACK:
+                out, in_ = w3_views(t, 1)
+                on_v(out=out, in_=in_)
+            if t == PACK:
+                w2_q = w2_q + quantise(w2_b, 2, PACK, sb([P, HALF], U32, "w2_c23", tag="w3_raw1"), sb([P, HALF], U8, "w2_s23"))
+            if t > 0:
+                codes, scales = sb([P, P], U32, "w3_c%d" % (t - 1)), sb([P, P], U8, "w3_s%d" % (t - 1))
+                w3_q = w3_q + quantise(w3_b[t - 1], 0, 1, codes, scales)
+        y_tile(2, PACK)
+        y_tile(3, PACK + 1)
+        q_ps = [weight_product(w3_q[0], "q0", 2)]
+        e_ps = e_ps + [weight_product(w2_q[t], "e%d" % t, PACK + t) for t in (2, 3)]
+        q_ps = q_ps + [weight_product(w3_q[t], "q%d" % t, (t + 2) % PACK) for t in range(1, PACK)]
         gate(2)
         gate(3)
-        ident = at(3 * 2 * H, [P, P], F32, "ident")
+        ident = at(2 * H, [P, P], F32, "ident")
         make_identity(nc, ident[:])
 
         lists = (p1_sb, p2_sb)
         dirs = (d1, d2)
         turned = [bank(PACK + b, [P, PACK, P], "turned%d" % b) for b in range(PACK)]
-        seen = [0] * PACK
+        last = bank(3, [P, P], "last")
+        left = [4 * PACK] * (PACK - 1) + [4 * (PACK - 1), 4]
+        total = list(left)
 
         def turn(t, term, j0):
             for c in range(term.shape[1] // P):
                 b = j0 // P + c
+                apart = b == PACK - 1 and t == PACK - 1
+                g = PACK if apart else b
                 nc.tensor.matmul(
-                    turned[b][:, t, :],
+                    last[:] if apart else turned[b][:, t, :],
                     term[:, c * P : (c + 1) * P],
                     ident[:],
-                    start=seen[b] == 0,
-                    stop=seen[b] == 4 * PACK - 1,
+                    start=left[g] == total[g],
+                    stop=left[g] == 1,
                     is_transpose=True,
                 )
-                seen[b] = seen[b] + 1
+                left[g] = left[g] - 1
 
         def entries(i, j0, n):
             return lists[i][:, j0 // PER_COLUMN : (j0 + n) // PER_COLUMN]
 
-        def fetch_ye(t, i, j0, n, tag=None):
-            term = sb([P, n], F32, "ye_term%d_%d_%d" % (t, i, j0), tag=tag)
+        def fetch_ye(t, i, j0, n):
+            name = "ye_term%d_%d_%d" % (t, i, j0)
+            if n == S:
+                term = at(RING + i * 4 * S, [P, n], F32, name)
+            elif j0 == 0:
+                term = sb([P, n], F32, name, tag="w3_%s%d" % (("c", "s")[i], t))
+            else:
+                term = at(RING + (2 * (t - 2) + i) * 4 * HALF, [P, n], F32, name)
             nc.scalar.activation(term[:], ye[t][:].indirect(entries(i, j0, n)), COPY)
             turn(t, term[:], j0)
 
@@ -203,41 +232,54 @@ def tile_picked_painn8_none_po_kernel(
             turn(t, term[:], j0)
 
         for i in range(2):
-            fetch_ye(0, i, 0, S, "ring%d" % i)
+            fetch_ye(0, i, 0, S)
         for t in range(PACK):
-            nc.scalar.copy(out=q_sb[t][:, :S], in_=q_ps[t][:])
-        for i in range(2):
-            fetch_q(0, i, 0, S)
-        for t in range(1, PACK - 1):
-            for i in range(2):
-                fetch_ye(t, i, 0, S, "ring%d" % i)
-                fetch_q(t, i, 0, S)
-        for j0 in (0, HALF):
-            for i in range(2):
-                fetch_ye(PACK - 1, i, j0, HALF, "ring%d" % i)
-            for i in range(2):
-                fetch_q(PACK - 1, i, j0, HALF)
-
-        w4w_d = sb([P, 2 * N], U8, "w4w_d")
+            (on_s if t else on_v)(out=q_sb[t][:, :S], in_=q_ps[t][:])
+        fetch_q(0, 0, 0, S)
+        fetch_q(0, 1, 0, S)
+        w4s_d = at(4 * N, [P, N], U8, "w4s_d")
+        nc.vector.tensor_copy(
+            out=w4s_d[:].rearrange("p (t m) -> p t m", t=PACK), in_=w4s[:].rearrange("p (m t) -> p t m", t=PACK)
+        )
+        for r in range(1, PACK):
+            nc.sync.dma_start(out=w4s_d[r:P:QUADRANT, :].bitcast(I32), in_=w4s_d[8 * r : P : QUADRANT, :].bitcast(I32))
+        w4w_d = at(6 * N, [P, 2 * N], U8, "w4w_d")
         nc.vector.tensor_copy(
             out=w4w_d[:].bitcast(U16).rearrange("p (t m) -> p t m", t=PACK),
             in_=w4w[:].bitcast(U16).rearrange("p (m t) -> p t m", t=PACK),
         )
+        for t in (2, 3):
+            for i in range(2):
+                fetch_ye(t, i, 0, HALF)
+            fetch_q(1, t - 2, 0, S)
+        for i in range(2):
+            fetch_ye(1, i, 0, S)
+            fetch_q(2, i, 0, HALF)
+        for i in range(2):
+            fetch_q(3, i, 0, HALF)
+        for t in (2, 3):
+            for i in range(2):
+                fetch_ye(t, i, HALF, HALF)
+        for j0 in (HALF, HALF + P):
+            for t in (2, 3):
+                for i in range(2):
+                    fetch_q(t, i, j0, P)
+
 
         out_rows = out_0.rearrange("(p t) j -> p t j", t=PACK)
         code_rows = out_1[0].rearrange("p n t -> p (n t)").bitcast(I32)
         z_c = sb([P, S], U32, "z_c")
         z_s = sb([P, S], U8, "z_s")
 
-        def round_turned(copy, b):
-            zt = sb([P, H], BF16, "zt%d" % b)
-            copy(
-                out=zt[:].rearrange("a (r t i) -> a t r i", r=RUNS, t=PACK),
-                in_=turned[b][:].rearrange("a t (r i) -> a t r i", r=RUNS),
-            )
-            back = bank(b, [P, 2, P], "back%d" % b)
+        zt = [sb([P, H], BF16, "zt%d" % b) for b in range(PACK)]
+
+        def round_turned(copy, b, t0, t1, sums):
+            copy(out=zt[b][:].rearrange("a (r t i) -> a t r i", r=RUNS, t=PACK)[:, t0:t1], in_=sums.rearrange("a t (r i) -> a t r i", r=RUNS))
+
+        def turn_back(b):
+            back = bank(b % 3, [P, 2, P], "back%d" % b)
             for u in range(2):
-                nc.tensor.transpose(back[:, u, :], zt[:].bitcast(F32)[:, u : 2 * P : 2], ident[:])
+                nc.tensor.transpose(back[:, u, :], zt[b][:].bitcast(F32)[:, u : 2 * P : 2], ident[:])
             return back
 
         def lay_z(copy, b, back):
@@ -249,12 +291,12 @@ def tile_picked_painn8_none_po_kernel(
             cols = slice(b * P, (b + 1) * P)
             nc.vector.quantize_mx(out=z_c[:, cols].bitcast(FP8X4), scales=z_s[:, cols], in_=z_b[:])
 
-        def multiply(b):
+        def multiply(b, t0, t1, number):
             cols = slice(b * P, (b + 1) * P)
-            acc = bank(PACK + b, [P, PACK, P], "o%d" % b)
-            for t in range(PACK):
+            acc = bank(number, [P, t1 - t0, P], "o%d_%d" % (b, t0))
+            for t in range(t0, t1):
                 nc.tensor.matmul_mx(
-                    out=acc[:, t, :],
+                    out=acc[:, t - t0, :],
                     lhsT=w4w_d[:, 2 * t * P : 2 * (t + 1) * P].bitcast(FP4X4),
                     lhsT_scale=w4s_d[:, t * P : (t + 1) * P],
                     rhs=z_c[:, cols].bitcast(FP8X4),
@@ -271,7 +313,7 @@ def tile_picked_painn8_none_po_kernel(
             copy(out=part, in_=acc[:])
             if b == 1:
                 nc.sync.dma_start(out=out_rows[:, :, :HALF], in_=o_f[0][:])
-            if b > 1:
+            if b == 2:
                 nc.sync.dma_start(out=out_rows[:, :, b * P : (b + 1) * P], in_=part)
             return part
 
@@ -289,35 +331,46 @@ def tile_picked_painn8_none_po_kernel(
                 both = slice((b - 1) * P, (b + 1) * P)
                 nc.sync.dma_start(out=code_rows[:, both], in_=o_codes[:, both])
 
-        on_s, on_v = nc.scalar.copy, nc.vector.tensor_copy
-        back0 = round_turned(on_s, 0)
-        back1 = round_turned(on_s, 1)
+        def early(b):
+            round_turned(on_s, b, 0, PACK, turned[b][:])
+            return turn_back(b)
+
+        back0 = early(0)
+        back1 = early(1)
         z0 = lay_z(on_s, 0, back0)
+        back2 = early(2)
         z1 = lay_z(on_s, 1, back1)
-        back2 = round_turned(on_v, 2)
-        back3 = round_turned(on_s, 3)
         quantise_z(0, z0)
+        acc0 = multiply(0, 0, PACK, 4)
+        round_turned(on_s, 3, 0, PACK - 1, turned[3][:, : PACK - 1, :])
+        round_turned(on_v, 3, PACK - 1, PACK, last[:].unsqueeze(1))
+        back3 = turn_back(3)
         quantise_z(1, z1)
-        acc0 = multiply(0)
-        acc1 = multiply(1)
+        acc1 = multiply(1, 0, PACK, 5)
         z2 = lay_z(on_v, 2, back2)
-        o0 = leave(on_s, 0, acc0)
         z3 = lay_z(on_s, 3, back3)
-        o1 = leave(on_v, 1, acc1)
+        o0 = leave(on_v, 0, acc0)
         quantise_z(2, z2)
-        acc2 = multiply(2)
-        b0 = interleave(0, o0)
         quantise_z(3, z3)
-        acc3 = multiply(3)
+        acc2 = multiply(2, 0, PACK, 6)
+        acc3 = [multiply(3, 0, 2, 7), multiply(3, 2, PACK, 1)]
+        o1 = leave(on_s, 1, acc1)
+        b0 = interleave(0, o0)
         o2 = leave(on_s, 2, acc2)
         b1 = interleave(1, o1)
         planes(0, b0)
-        o3 = leave(on_s, 3, acc3)
         b2 = interleave(2, o2)
         planes(1, b1)
-        b3 = interleave(3, o3)
+        o_b3 = sb([P, PACK * P], BF16, "o_b3")
+        pairs = o_b3[:].rearrange("p (a t) -> p a t", t=PACK)
+        o3 = o_f[1][:, :, P:]
+        on_s(out=pairs[:, :, :2], in_=acc3[0][:].rearrange("p t a -> p a t"))
+        on_v(out=o3[:, 2:, :], in_=acc3[1][:])
+        on_s(out=pairs[:, :, 2:], in_=acc3[1][:].rearrange("p t a -> p a t"))
+        on_v(out=o3[:, :2, :], in_=acc3[0][:])
+        nc.sync.dma_start(out=out_rows[:, :, 3 * P :], in_=o3)
         planes(2, b2)
-        planes(3, b3)
+        planes(3, o_b3)
         for r in range(PACK):
             queue = nc.scalar if r % 2 else nc.sync
             queue.dma_start(out=out_2[0, r:BLOCKS:PACK, :].bitcast(I32), in_=o_scales[r:P:QUADRANT, :].bitcast(I32))

@@ -69,8 +69,8 @@ def tile_picked_painn8_none_po_kernel(
         nc.gpsimd.memset(xs[:].bitcast(I32), 0)
         nc.gpsimd.memset(w4s[:].bitcast(I32), 0)
         nc.gpsimd.memset(w1s[:].bitcast(I32), 0)
-        q_sb = [sb([P, 2 * S if t < 2 else S], F32, "q_sb%d" % t) for t in range(PACK)]
-        for t in range(2):
+        q_sb = [sb([P, 2 * S], F32, "q_sb%d" % t) for t in range(PACK)]
+        for t in range(PACK):
             nc.gpsimd.memset(q_sb[t][:, S:], 0.0)
 
         x_rows = x_words[0].rearrange("p n t -> p (n t)").bitcast(I32)
@@ -105,7 +105,7 @@ def tile_picked_painn8_none_po_kernel(
             )
             return dealt
 
-        w1w_d = deal_runs(w1w, sb([P, 2 * H], U8, "w1w_d"))
+        w1w_d = deal_runs(w1w, at(RING + 8 * S, [P, 2 * H], U8, "w1w_d"))
         w1s_d = deal_runs(w1s, sb([P, H], U8, "w1s_d"))
 
         def product(lhsT, lhsT_scale, name, number):
@@ -178,7 +178,8 @@ def tile_picked_painn8_none_po_kernel(
             if t == PACK:
                 w2_q = w2_q + quantise(w2_b, 2, PACK, sb([P, HALF], U32, "w2_c23", tag="w3_raw1"), sb([P, HALF], U8, "w2_s23"))
             if t > 0:
-                codes, scales = sb([P, P], U32, "w3_c%d" % (t - 1)), sb([P, P], U8, "w3_s%d" % (t - 1))
+                name = "w3_c%d" % (t - 1)
+                codes, scales = at(RING + 12 * S, [P, P], U32, name) if t == 2 else sb([P, P], U32, name), sb([P, P], U8, "w3_s%d" % (t - 1))
                 w3_q = w3_q + quantise(w3_b[t - 1], 0, 1, codes, scales)
         y_tile(2, PACK)
         y_tile(3, PACK + 1)
@@ -192,18 +193,18 @@ def tile_picked_painn8_none_po_kernel(
 
         lists = (p1_sb, p2_sb)
         dirs = (d1, d2)
-        turned = [bank(PACK + b, [P, PACK, P], "turned%d" % b) for b in range(PACK)]
-        last = bank(3, [P, P], "last")
-        left = [4 * PACK] * (PACK - 1) + [4 * (PACK - 1), 4]
+        turned = [bank(PACK + b, [P, PACK - 1, P], "turned%d" % b) for b in range(PACK)]
+        last = [bank(3 - h, [P, 2, P], "last%d" % h) for h in range(2)]
+        left = [4 * (PACK - 1)] * PACK + [8, 8]
         total = list(left)
 
         def turn(t, term, j0):
             for c in range(term.shape[1] // P):
                 b = j0 // P + c
-                apart = b == PACK - 1 and t == PACK - 1
-                g = PACK if apart else b
+                apart = t == PACK - 1
+                g = PACK + b // 2 if apart else b
                 nc.tensor.matmul(
-                    last[:] if apart else turned[b][:, t, :],
+                    last[b // 2][:, b % 2, :] if apart else turned[b][:, t, :],
                     term[:, c * P : (c + 1) * P],
                     ident[:],
                     start=left[g] == total[g],
@@ -217,12 +218,7 @@ def tile_picked_painn8_none_po_kernel(
 
         def fetch_ye(t, i, j0, n):
             name = "ye_term%d_%d_%d" % (t, i, j0)
-            if n == S:
-                term = at(RING + i * 4 * S, [P, n], F32, name)
-            elif j0 == 0:
-                term = sb([P, n], F32, name, tag="w3_%s%d" % (("c", "s")[i], t))
-            else:
-                term = at(RING + (2 * (t - 2) + i) * 4 * HALF, [P, n], F32, name)
+            term = at(RING + (2 * t + i) % PACK * 4 * S, [P, n], F32, name)
             nc.scalar.activation(term[:], ye[t][:].indirect(entries(i, j0, n)), COPY)
             turn(t, term[:], j0)
 
@@ -236,6 +232,8 @@ def tile_picked_painn8_none_po_kernel(
         for t in range(PACK):
             (on_s if t else on_v)(out=q_sb[t][:, :S], in_=q_ps[t][:])
         fetch_q(0, 0, 0, S)
+        for i in range(2):
+            fetch_ye(1, i, 0, S)
         fetch_q(0, 1, 0, S)
         w4s_d = at(4 * N, [P, N], U8, "w4s_d")
         nc.vector.tensor_copy(
@@ -248,38 +246,36 @@ def tile_picked_painn8_none_po_kernel(
             out=w4w_d[:].bitcast(U16).rearrange("p (t m) -> p t m", t=PACK),
             in_=w4w[:].bitcast(U16).rearrange("p (m t) -> p t m", t=PACK),
         )
-        for t in (2, 3):
-            for i in range(2):
-                fetch_ye(t, i, 0, HALF)
-            fetch_q(1, t - 2, 0, S)
         for i in range(2):
-            fetch_ye(1, i, 0, S)
-            fetch_q(2, i, 0, HALF)
+            fetch_ye(2, i, 0, S)
+            fetch_q(1, i, 0, S)
         for i in range(2):
-            fetch_q(3, i, 0, HALF)
-        for t in (2, 3):
-            for i in range(2):
-                fetch_ye(t, i, HALF, HALF)
-        for j0 in (HALF, HALF + P):
-            for t in (2, 3):
-                for i in range(2):
-                    fetch_q(t, i, j0, P)
-
+            fetch_ye(3, i, 0, S)
+            fetch_q(2, i, 0, S)
+        fetch_q(3, 0, 0, S)
+        for j0 in (0, HALF):
+            fetch_q(3, 1, j0, HALF)
 
         out_rows = out_0.rearrange("(p t) j -> p t j", t=PACK)
         code_rows = out_1[0].rearrange("p n t -> p (n t)").bitcast(I32)
         z_c = sb([P, S], U32, "z_c")
         z_s = sb([P, S], U8, "z_s")
 
-        zt = [sb([P, H], BF16, "zt%d" % b) for b in range(PACK)]
+        zt = [sb([P, 2, H], BF16, "zt%d" % h) for h in range(2)]
 
-        def round_turned(copy, b, t0, t1, sums):
-            copy(out=zt[b][:].rearrange("a (r t i) -> a t r i", r=RUNS, t=PACK)[:, t0:t1], in_=sums.rearrange("a t (r i) -> a t r i", r=RUNS))
+        def features(h):
+            return zt[h][:].rearrange("a b (r t i) -> a b t r i", r=RUNS, t=PACK)
+
+        def round_turned(b):
+            on_s(out=features(b // 2)[:, b % 2, : PACK - 1], in_=turned[b][:].rearrange("a t (r i) -> a t r i", r=RUNS))
+
+        def round_last(copy, h):
+            copy(out=features(h)[:, :, PACK - 1], in_=last[h][:].rearrange("a b (r i) -> a b r i", r=RUNS))
 
         def turn_back(b):
-            back = bank(b % 3, [P, 2, P], "back%d" % b)
+            back = bank(PACK + b, [P, 2, P], "back%d" % b)
             for u in range(2):
-                nc.tensor.transpose(back[:, u, :], zt[b][:].bitcast(F32)[:, u : 2 * P : 2], ident[:])
+                nc.tensor.transpose(back[:, u, :], zt[b // 2][:, b % 2, :].bitcast(F32)[:, u : 2 * P : 2], ident[:])
             return back
 
         def lay_z(copy, b, back):
@@ -311,10 +307,7 @@ def tile_picked_painn8_none_po_kernel(
         def leave(copy, b, acc):
             part = o_f[b // 2][:, :, (b % 2) * P : (b % 2 + 1) * P]
             copy(out=part, in_=acc[:])
-            if b == 1:
-                nc.sync.dma_start(out=out_rows[:, :, :HALF], in_=o_f[0][:])
-            if b == 2:
-                nc.sync.dma_start(out=out_rows[:, :, b * P : (b + 1) * P], in_=part)
+            nc.sync.dma_start(out=out_rows[:, :, b * P : (b + 1) * P], in_=part)
             return part
 
         def interleave(b, values):
@@ -331,46 +324,30 @@ def tile_picked_painn8_none_po_kernel(
                 both = slice((b - 1) * P, (b + 1) * P)
                 nc.sync.dma_start(out=code_rows[:, both], in_=o_codes[:, both])
 
-        def early(b):
-            round_turned(on_s, b, 0, PACK, turned[b][:])
-            return turn_back(b)
-
-        back0 = early(0)
-        back1 = early(1)
-        z0 = lay_z(on_s, 0, back0)
-        back2 = early(2)
-        z1 = lay_z(on_s, 1, back1)
-        quantise_z(0, z0)
-        acc0 = multiply(0, 0, PACK, 4)
-        round_turned(on_s, 3, 0, PACK - 1, turned[3][:, : PACK - 1, :])
-        round_turned(on_v, 3, PACK - 1, PACK, last[:].unsqueeze(1))
-        back3 = turn_back(3)
-        quantise_z(1, z1)
-        acc1 = multiply(1, 0, PACK, 5)
-        z2 = lay_z(on_v, 2, back2)
-        z3 = lay_z(on_s, 3, back3)
-        o0 = leave(on_v, 0, acc0)
-        quantise_z(2, z2)
-        quantise_z(3, z3)
-        acc2 = multiply(2, 0, PACK, 6)
-        acc3 = [multiply(3, 0, 2, 7), multiply(3, 2, PACK, 1)]
-        o1 = leave(on_s, 1, acc1)
+        for b in range(PACK):
+            round_turned(b)
+        round_last(on_s, 0)
+        round_last(on_v, 1)
+        back = [turn_back(b) for b in range(PACK)]
+        z = [lay_z(on_v if b == 2 else on_s, b, back[b]) for b in range(PACK)]
+        for b in range(PACK):
+            quantise_z(b, z[b])
+        acc0 = multiply(0, 0, PACK, 0)
+        acc1 = multiply(1, 0, PACK, 1)
+        acc2 = multiply(2, 0, PACK, 2)
+        acc3 = multiply(3, 0, PACK, 3)
+        o0 = leave(on_s, 0, acc0)
+        o1 = leave(on_v, 1, acc1)
         b0 = interleave(0, o0)
         o2 = leave(on_s, 2, acc2)
         b1 = interleave(1, o1)
         planes(0, b0)
+        o3 = leave(on_s, 3, acc3)
         b2 = interleave(2, o2)
         planes(1, b1)
-        o_b3 = sb([P, PACK * P], BF16, "o_b3")
-        pairs = o_b3[:].rearrange("p (a t) -> p a t", t=PACK)
-        o3 = o_f[1][:, :, P:]
-        on_s(out=pairs[:, :, :2], in_=acc3[0][:].rearrange("p t a -> p a t"))
-        on_v(out=o3[:, 2:, :], in_=acc3[1][:])
-        on_s(out=pairs[:, :, 2:], in_=acc3[1][:].rearrange("p t a -> p a t"))
-        on_v(out=o3[:, :2, :], in_=acc3[0][:])
-        nc.sync.dma_start(out=out_rows[:, :, 3 * P :], in_=o3)
+        b3 = interleave(3, o3)
         planes(2, b2)
-        planes(3, o_b3)
+        planes(3, b3)
         for r in range(PACK):
             queue = nc.scalar if r % 2 else nc.sync
             queue.dma_start(out=out_2[0, r:BLOCKS:PACK, :].bitcast(I32), in_=o_scales[r:P:QUADRANT, :].bitcast(I32))

@@ -263,19 +263,24 @@ def tile_picked_painn8_none_po_kernel(
 
         zt = [sb([P, 2, H], BF16, "zt%d" % h) for h in range(2)]
 
-        def features(h):
-            return zt[h][:].rearrange("a b (r t i) -> a b t r i", r=RUNS, t=PACK)
+        def words(h, u):
+            return zt[h][:].rearrange("a b (u r t c e) -> a u b t r c e", u=2, r=RUNS, t=PACK, e=2)[:, u]
 
         def round_turned(b):
-            on_s(out=features(b // 2)[:, b % 2, : PACK - 1], in_=turned[b][:].rearrange("a t (r i) -> a t r i", r=RUNS))
+            for u in range(2):
+                on_s(
+                    out=words(b // 2, u)[:, b % 2, : PACK - 1],
+                    in_=turned[b][:].rearrange("a t (r c u e) -> a u t r c e", r=RUNS, u=2, e=2)[:, u],
+                )
 
         def round_last(copy, h):
-            copy(out=features(h)[:, :, PACK - 1], in_=last[h][:].rearrange("a b (r i) -> a b r i", r=RUNS))
+            for u in range(2):
+                copy(out=words(h, u)[:, :, PACK - 1], in_=last[h][:].rearrange("a b (r c u e) -> a u b r c e", r=RUNS, u=2, e=2)[:, u])
 
         def turn_back(b):
             back = bank(PACK + b, [P, 2, P], "back%d" % b)
             for u in range(2):
-                nc.tensor.transpose(back[:, u, :], zt[b // 2][:, b % 2, :].bitcast(F32)[:, u : 2 * P : 2], ident[:])
+                nc.tensor.transpose(back[:, u, :], zt[b // 2][:, b % 2, :].bitcast(F32)[:, u * P : (u + 1) * P], ident[:])
             return back
 
         def lay_z(copy, b, back):

@@ -337,11 +337,14 @@ def tile_picked_painn8_none_po_kernel(
         z = [lay_z(on_v if b == 2 else on_s, b, back[b]) for b in range(PACK)]
         for b in range(PACK):
             quantise_z(b, z[b])
-        acc0 = multiply(0, 0, PACK, 0)
+        first = [multiply(0, 0, 2, 0), multiply(0, 2, PACK, PACK)]
         acc1 = multiply(1, 0, PACK, 1)
         acc2 = multiply(2, 0, PACK, 2)
         acc3 = multiply(3, 0, PACK, 3)
-        o0 = leave(on_s, 0, acc0)
+        o0 = o_f[0][:, :, :P]
+        for u in range(2):
+            on_s(out=o0[:, 2 * u : 2 * u + 2, :], in_=first[u][:])
+            nc.sync.dma_start(out=out_rows[:, 2 * u : 2 * u + 2, :P], in_=o0[:, 2 * u : 2 * u + 2, :])
         o1 = leave(on_v, 1, acc1)
         b0 = interleave(0, o0)
         o2 = leave(on_s, 2, acc2)

@@ -76,10 +76,10 @@ def tile_picked_painn8_none_po_kernel(
         x_rows = x_words[0].rearrange("p n t -> p (n t)").bitcast(I32)
         w2_rows = w2.rearrange("(p j) c -> p j c", j=PACK)
         w3_rows = w3.rearrange("(p j) c -> p j c", j=PACK)
-        nc.sync.dma_start(out=xw[:, : T // 4], in_=x_rows[:, : T // 4])
+        nc.sync.dma_start(out=xw[:, : T // 2], in_=x_rows[:, : T // 2])
         nc.sync.dma_start(offs_sb[:], offs)
         place_scale_rows(xs, x_scales[0])
-        nc.sync.dma_start(out=xw[:, T // 4 :], in_=x_rows[:, T // 4 :])
+        nc.sync.dma_start(out=xw[:, T // 2 :], in_=x_rows[:, T // 2 :])
         nc.sync.dma_start(out=w2_raw[0][:], in_=w2_rows[:, :, :HALF])
         nc.sync.dma_start(out=w1w[:].bitcast(I32), in_=w1_words[0].bitcast(I32))
         place_scale_rows(w1s, w1_scales[0])

@@ -20,12 +20,11 @@ COPY = mybir.ActivationFunctionType.Copy
 
 P = 128
 PACK = 4
-RUNS = 8
 HALF = 256
 PER_COLUMN = 16
 QUADRANT = 32
 BLOCKS = K // 32
-RING = 2 * PACK * H
+KB = 1024
 
 
 def tile_picked_painn8_none_po_kernel(
@@ -40,8 +39,8 @@ def tile_picked_painn8_none_po_kernel(
         def bank(number, shape, name):
             return psum.tile(shape, F32, name=name, tag="bank%d" % number)
 
-        def sb(shape, dtype, name, tag=None):
-            return keep.tile(shape, dtype, name=name, tag=tag or name, align_bytes=64)
+        def sb(shape, dtype, name):
+            return keep.tile(shape, dtype, name=name, align_bytes=64)
 
         def at(offset, shape, dtype, name):
             return placed.tile(shape, dtype, name=name, offset=offset, align_bytes=64)
@@ -61,10 +60,10 @@ def tile_picked_painn8_none_po_kernel(
         w4s = sb([P, N], U8, "w4s")
         o_scales = sb([P, S], U8, "o_scales")
         o_codes = sb([P, S], I32, "o_codes")
-        d1 = sb([P, S], F32, "d1")
+        d1 = at(32 * KB, [P, S], F32, "d1")
         d2 = sb([P, S], F32, "d2")
-        w2_raw = [sb([P, PACK, HALF], F32, "w2_raw%d" % h) for h in range(2)]
-        w3_raw = [sb([P, PACK, HALF], F32, "w3_raw%d" % h) for h in range(2)]
+        w2_raw = [sb([P, PACK, HALF], F32, "w2_raw0"), at(24 * KB, [P, PACK, HALF], F32, "w2_raw1")]
+        w3_raw = [sb([P, PACK, HALF], F32, "w3_raw0"), at(28 * KB, [P, PACK, HALF], F32, "w3_raw1")]
 
         nc.gpsimd.memset(xs[:].bitcast(I32), 0)
         nc.gpsimd.memset(w4s[:].bitcast(I32), 0)
@@ -93,20 +92,25 @@ def tile_picked_painn8_none_po_kernel(
         nc.sync.dma_start(out=w4s[0:P:8, :].bitcast(I32), in_=w4_scales[0].bitcast(I32))
         nc.sync.dma_start(out=w4w[:].bitcast(I32), in_=w4_words[0].bitcast(I32))
 
+        on_s, on_v = nc.scalar.copy, nc.vector.tensor_copy
         xq_s = sb([P, S], U8, "xq_s")
         xq = sb([P, S], U32, "xq")
-        nc.vector.tensor_copy(xq_s[:], xs[:].indirect(offs_sb[:]))
-        nc.vector.tensor_copy(xq[:], xw[:].bitcast(U32).indirect(offs_sb[:]))
+        on_v(xq_s[:], xs[:].indirect(offs_sb[:]))
+        on_v(xq[:], xw[:].bitcast(U32).indirect(offs_sb[:]))
 
-        def deal_runs(packed, dealt):
-            nc.vector.tensor_copy(
-                out=dealt[:].bitcast(I32).rearrange("p (t r i) -> p t r i", t=PACK, r=RUNS),
-                in_=packed[:].bitcast(I32).rearrange("p (r t i) -> p t r i", t=PACK, r=RUNS),
+        def deal_words(u, dealt):
+            on_v(
+                out=dealt[:].bitcast(I32).rearrange("p (s n) -> p s n", s=2),
+                in_=w1w[:].bitcast(I32).rearrange("p (n s u) -> p u s n", s=2, u=2)[:, u],
             )
             return dealt
 
-        w1w_d = deal_runs(w1w, at(RING + 8 * S, [P, 2 * H], U8, "w1w_d"))
-        w1s_d = deal_runs(w1s, sb([P, H], U8, "w1s_d"))
+        w1w_d = [deal_words(0, sb([P, H], U8, "w1w_d0"))]
+        w1s_d = sb([P, H], U8, "w1s_d")
+        on_v(
+            out=w1s_d[:].bitcast(U16).rearrange("p (u s n) -> p u s n", u=2, s=2),
+            in_=w1s[:].bitcast(U16).rearrange("p (n s u) -> p u s n", s=2, u=2),
+        )
 
         def product(lhsT, lhsT_scale, name, number):
             acc = bank(number, [P, S], name)
@@ -117,175 +121,165 @@ def tile_picked_painn8_none_po_kernel(
 
         ye = [sb([P, 2 * S], F32, "ye%d" % t) for t in range(PACK)]
 
-        def y_tile(t, number):
-            acc = product(w1w_d[:, 2 * t * P : 2 * (t + 1) * P].bitcast(FP4X4), w1s_d[:, t * P : (t + 1) * P], "y%d" % t, number)
-            nc.scalar.copy(out=ye[t][:, S:], in_=acc[:])
+        def y_tile(t):
+            words = w1w_d[t // 2][:, (t % 2) * 2 * P : (t % 2 + 1) * 2 * P]
+            acc = product(words.bitcast(FP4X4), w1s_d[:, t * P : (t + 1) * P], "y%d" % t, t)
+            on_s(out=ye[t][:, S:], in_=acc[:])
 
-        def dealt_views(raw, rounded, h):
-            runs = slice(h * RUNS // 2, (h + 1) * RUNS // 2)
-            return (
-                rounded[:].rearrange("p (t r i j) -> p t r i j", t=PACK, r=RUNS, j=PACK)[:, :, runs],
-                raw[h][:].rearrange("p j (r t i) -> p t r i j", r=RUNS // 2, t=PACK),
+        def round_views(raw, rounded, h, s):
+            return dict(
+                out=rounded[:].rearrange("p (u s h n e j) -> p h s n j u e", u=2, s=2, h=2, e=2, j=PACK)[:, h, s],
+                in_=raw[h][:].rearrange("p j (n s u e) -> p s n j u e", s=2, u=2, e=2)[:, s],
             )
 
-        def round_rows(copy, raw, rounded, h, t0, t1):
-            out, in_ = dealt_views(raw, rounded, h)
-            copy(out=out[:, t0:t1], in_=in_[:, t0:t1])
-
-        def quantise(rounded, t0, t1, codes, scales):
-            nc.vector.quantize_mx(out=codes[:].bitcast(FP8X4), scales=scales[:], in_=rounded[:, t0 * PACK * P : t1 * PACK * P])
-            return [(codes[:, c * P : (c + 1) * P], scales[:, c * P : (c + 1) * P]) for c in range(t1 - t0)]
-
-        def quantise_tile(rounded, t, name):
-            return quantise(rounded, t, t + 1, sb([P, P], U32, "%s_c%d" % (name, t)), sb([P, P], U8, "%s_s%d" % (name, t)))
+        def quantise(rounded, codes, scales):
+            nc.vector.quantize_mx(out=codes[:].bitcast(FP8X4), scales=scales[:], in_=rounded)
+            return [(codes[:, c : c + P], scales[:, c : c + P]) for c in range(0, codes.shape[1], P)]
 
         def weight_product(quantised, name, number):
             return product(quantised[0].bitcast(FP8X4), quantised[1], name, number)
 
-        on_s, on_v = nc.scalar.copy, nc.vector.tensor_copy
         w2_b = sb([P, PACK * H], BF16, "w2_b")
-        round_rows(on_s, w2_raw, w2_b, 0, 0, PACK)
-        round_rows(on_v, w2_raw, w2_b, 1, 0, 1)
-        round_rows(on_v, w2_raw, w2_b, 1, 1, 2)
-        w2_q = quantise(w2_b, 0, 1, at(2 * H - 2 * P, [P, P], U32, "w2_c0"), at(6 * H - P // 2, [P, P], U8, "w2_s0"))
-        round_rows(on_v, w2_raw, w2_b, 1, 2, PACK)
-        w2_q = w2_q + quantise_tile(w2_b, 1, "w2")
-        for t in range(2):
-            y_tile(t, t)
-        e_ps = [weight_product(w2_q[t], "e%d" % t, PACK + t) for t in range(2)]
+        on_s(**round_views(w2_raw, w2_b, 0, 0))
+        on_s(**round_views(w2_raw, w2_b, 0, 1))
+        y_tile(0)
+        y_tile(1)
+        on_v(**round_views(w2_raw, w2_b, 1, 0))
+        on_v(**round_views(w2_raw, w2_b, 1, 1))
+        w2_q = quantise(w2_b[:, :H], at(KB - 256, [P, P], U32, "w2_c0"), at(3 * KB - 64, [P, P], U8, "w2_s0"))
+        w2_q = w2_q + quantise(w2_b[:, H : 2 * H], sb([P, P], U32, "w2_c1"), sb([P, P], U8, "w2_s1"))
+        w1w_d.append(deal_words(1, at(24 * KB, [P, H], U8, "w1w_d1")))
+        w2_q = w2_q + quantise(w2_b[:, 2 * H :], sb([P, HALF], U32, "w2_c23"), sb([P, HALF], U8, "w2_s23"))
+        e_ps = [weight_product(w2_q[0], "e0", PACK)]
+        y_tile(2)
+        e_ps.append(weight_product(w2_q[1], "e1", PACK + 1))
+        y_tile(3)
+        e_ps = e_ps + [weight_product(w2_q[t], "e%d" % t, PACK + t) for t in (2, 3)]
 
         def gate(t):
             nc.vector.tensor_tensor(ye[t][:, :S], e_ps[t][:], ye[t][:, S:], MULT)
+            product(w1w_d[0][:, : 2 * P].bitcast(FP4X4), w1s_d[:, :P], "warm%d" % t, PACK + t)
 
         gate(0)
         gate(1)
-        w3_b = [at(t * 2 * H, [P, H], BF16, "w3_b%d" % t) for t in range(PACK)]
-
-        def w3_views(t, h):
-            return (
-                w3_b[t][:, h * HALF : (h + 1) * HALF].rearrange("p (r i j) -> p r i j", r=RUNS // 2, j=PACK),
-                w3_raw[h][:].rearrange("p j (r t i) -> p t r i j", r=RUNS // 2, t=PACK)[:, t],
-            )
-
+        w3_b = at(0, [P, PACK * H], BF16, "w3_b")
         for t in range(PACK):
-            out, in_ = w3_views(t, 0)
+            views = round_views(w3_raw, w3_b, 0, t % 2)
+            out, in_ = (views[side][:, :, :, t // 2].rearrange("p n j e -> p n e j") for side in ("out", "in_"))
             nc.gpsimd.tensor_scalar(out, in_, 1.0, 0.0, op0=MULT, op1=ADD)
-        w3_q = []
-        for t in range(PACK + 1):
-            if t < PACK:
-                out, in_ = w3_views(t, 1)
-                on_v(out=out, in_=in_)
-            if t == PACK:
-                w2_q = w2_q + quantise(w2_b, 2, PACK, sb([P, HALF], U32, "w2_c23", tag="w3_raw1"), sb([P, HALF], U8, "w2_s23"))
-            if t > 0:
-                name = "w3_c%d" % (t - 1)
-                codes, scales = at(RING + 12 * S, [P, P], U32, name) if t == 2 else sb([P, P], U32, name), sb([P, P], U8, "w3_s%d" % (t - 1))
-                w3_q = w3_q + quantise(w3_b[t - 1], 0, 1, codes, scales)
-        y_tile(2, PACK)
-        y_tile(3, PACK + 1)
-        q_ps = [weight_product(w3_q[0], "q0", 2)]
-        e_ps = e_ps + [weight_product(w2_q[t], "e%d" % t, PACK + t) for t in (2, 3)]
-        q_ps = q_ps + [weight_product(w3_q[t], "q%d" % t, (t + 2) % PACK) for t in range(1, PACK)]
+        on_v(**round_views(w3_raw, w3_b, 1, 0))
+        on_v(**round_views(w3_raw, w3_b, 1, 1))
+        w3_q = quantise(w3_b[:, :H], sb([P, P], U32, "w3_c0"), sb([P, P], U8, "w3_s0"))
+        w3_q = w3_q + quantise(w3_b[:, H : 2 * H], at(9 * KB, [P, P], U32, "w3_c1"), sb([P, P], U8, "w3_s1"))
+        w3_q = w3_q + quantise(w3_b[:, 2 * H :], at(19 * KB - 512, [P, HALF], U32, "w3_c23"), at(13 * KB - 128, [P, HALF], U8, "w3_s23"))
+        q_ps = [weight_product(w3_q[t], "q%d" % t, t) for t in range(PACK)]
         gate(2)
         gate(3)
-        ident = at(2 * H, [P, P], F32, "ident")
+        ident = at(28 * KB, [P, P], F32, "ident")
         make_identity(nc, ident[:])
+
+        w4s_d = at(2 * KB + 512, [P, N], U8, "w4s_d")
+        on_v(out=w4s_d[:].rearrange("p (t m) -> p t m", t=PACK), in_=w4s[:].rearrange("p (m t) -> p t m", t=PACK))
+        for r in range(1, PACK):
+            nc.sync.dma_start(out=w4s_d[r:P:QUADRANT, :].bitcast(I32), in_=w4s_d[8 * r : P : QUADRANT, :].bitcast(I32))
 
         lists = (p1_sb, p2_sb)
         dirs = (d1, d2)
-        turned = [bank(PACK + b, [P, PACK - 1, P], "turned%d" % b) for b in range(PACK)]
-        last = [bank(3 - h, [P, 2, P], "last%d" % h) for h in range(2)]
-        left = [4 * (PACK - 1)] * PACK + [8, 8]
-        total = list(left)
+        turned = [[bank(PACK + 2 * u + h, [P, 2, 2, P], "turned%d_%d" % (u, h)) for h in range(2)] for u in range(2)]
+        left = [[16, 16], [16, 16]]
 
         def turn(t, term, j0):
+            u, s = divmod(t, 2)
             for c in range(term.shape[1] // P):
-                b = j0 // P + c
-                apart = t == PACK - 1
-                g = PACK + b // 2 if apart else b
+                h, b = divmod(j0 // P + c, 2)
                 nc.tensor.matmul(
-                    last[b // 2][:, b % 2, :] if apart else turned[b][:, t, :],
+                    turned[u][h][:, b, s, :],
                     term[:, c * P : (c + 1) * P],
                     ident[:],
-                    start=left[g] == total[g],
-                    stop=left[g] == 1,
+                    start=left[u][h] == 16,
+                    stop=left[u][h] == 1,
                     is_transpose=True,
                 )
-                left[g] = left[g] - 1
+                left[u][h] = left[u][h] - 1
 
         def entries(i, j0, n):
             return lists[i][:, j0 // PER_COLUMN : (j0 + n) // PER_COLUMN]
 
-        def fetch_ye(t, i, j0, n):
-            name = "ye_term%d_%d_%d" % (t, i, j0)
-            term = at(RING + (2 * t + i) % PACK * 4 * S, [P, n], F32, name)
+        def term_tile(kind, t, i, j0, n, offset):
+            name = "%s_term%d_%d_%d" % (kind, t, i, j0)
+            return sb([P, n], F32, name) if offset is None else at(offset, [P, n], F32, name)
+
+        def fetch_ye(t, i, offset=None, j0=0, n=S):
+            term = term_tile("ye", t, i, j0, n, offset)
             nc.scalar.activation(term[:], ye[t][:].indirect(entries(i, j0, n)), COPY)
             turn(t, term[:], j0)
 
-        def fetch_q(t, i, j0, n):
-            term = sb([P, n], F32, "q_term%d_%d_%d" % (t, i, j0))
+        def fetch_q(t, i, offset=None, j0=0, n=S):
+            term = term_tile("q", t, i, j0, n, offset)
             nc.vector.tensor_tensor(term[:], q_sb[t][:].indirect(entries(i, j0, n)), dirs[i][:, j0 : j0 + n], MULT)
             turn(t, term[:], j0)
 
-        for i in range(2):
-            fetch_ye(0, i, 0, S)
-        for t in range(PACK):
+        zt = [[None] * PACK, [None] * PACK]
+        back = [bank(b, [P, 2, P], "back%d" % b) for b in range(PACK)]
+
+        def round_turned(copy, u, h, b0, b1, offset=None):
+            name = "zt%d_%d_%d" % (u, h, b0)
+            shape = [P, b1 - b0, 2 * P]
+            words = sb(shape, BF16, name) if offset is None else at(offset, shape, BF16, name)
+            copy(
+                out=words[:].rearrange("a b (n s e) -> a b n s e", s=2, e=2),
+                in_=turned[u][h][:, b0:b1].rearrange("a b s (n e) -> a b n s e", e=2),
+            )
+            for b in range(b0, b1):
+                zt[u][2 * h + b] = words[:, b - b0, :].bitcast(F32)
+
+        def turn_back(u, b):
+            nc.tensor.transpose(back[b][:, u, :], zt[u][b], ident[:])
+
+        def leave_q(t):
             (on_s if t else on_v)(out=q_sb[t][:, :S], in_=q_ps[t][:])
-        fetch_q(0, 0, 0, S)
+
+        fetch_ye(0, 0)
+        fetch_ye(0, 1)
+        leave_q(0)
+        fetch_ye(1, 0)
+        fetch_q(0, 0)
+        leave_q(1)
+        fetch_ye(1, 1, 9 * KB)
+        fetch_q(0, 1)
+        fetch_ye(2, 0, 17 * KB)
+        fetch_q(1, 0)
+        leave_q(2)
+        fetch_ye(2, 1, 19 * KB)
+        fetch_q(1, 1)
+        fetch_ye(3, 0, 11 * KB)
+        fetch_q(2, 0)
+        leave_q(3)
+        fetch_ye(3, 1, 13 * KB)
+        fetch_q(2, 1)
+        fetch_q(3, 0, None, 0, HALF)
+        fetch_q(3, 1, None, 0, HALF)
+        for h in range(2):
+            round_turned(on_s, 0, h, 0, 2)
+        for b in range(PACK):
+            turn_back(0, b)
         for i in range(2):
-            fetch_ye(1, i, 0, S)
-        fetch_q(0, 1, 0, S)
-        w4s_d = at(4 * N, [P, N], U8, "w4s_d")
-        nc.vector.tensor_copy(
-            out=w4s_d[:].rearrange("p (t m) -> p t m", t=PACK), in_=w4s[:].rearrange("p (m t) -> p t m", t=PACK)
-        )
-        for r in range(1, PACK):
-            nc.sync.dma_start(out=w4s_d[r:P:QUADRANT, :].bitcast(I32), in_=w4s_d[8 * r : P : QUADRANT, :].bitcast(I32))
-        w4w_d = at(6 * N, [P, 2 * N], U8, "w4w_d")
-        nc.vector.tensor_copy(
+            fetch_q(3, i, None, HALF, HALF)
+
+        w4w_d = at(32 * KB, [P, 2 * N], U8, "w4w_d")
+        on_v(
             out=w4w_d[:].bitcast(U16).rearrange("p (t m) -> p t m", t=PACK),
             in_=w4w[:].bitcast(U16).rearrange("p (m t) -> p t m", t=PACK),
         )
-        for i in range(2):
-            fetch_ye(2, i, 0, S)
-            fetch_q(1, i, 0, S)
-        for i in range(2):
-            fetch_ye(3, i, 0, S)
-            fetch_q(2, i, 0, S)
-        fetch_q(3, 0, 0, S)
-        for j0 in (0, HALF):
-            fetch_q(3, 1, j0, HALF)
 
         out_rows = out_0.rearrange("(p t) j -> p t j", t=PACK)
         code_rows = out_1[0].rearrange("p n t -> p (n t)").bitcast(I32)
         z_c = sb([P, S], U32, "z_c")
         z_s = sb([P, S], U8, "z_s")
 
-        zt = [sb([P, 2, H], BF16, "zt%d" % h) for h in range(2)]
-
-        def words(h, u):
-            return zt[h][:].rearrange("a b (u r t c e) -> a u b t r c e", u=2, r=RUNS, t=PACK, e=2)[:, u]
-
-        def round_turned(b):
-            for u in range(2):
-                on_s(
-                    out=words(b // 2, u)[:, b % 2, : PACK - 1],
-                    in_=turned[b][:].rearrange("a t (r c u e) -> a u t r c e", r=RUNS, u=2, e=2)[:, u],
-                )
-
-        def round_last(copy, h):
-            for u in range(2):
-                copy(out=words(h, u)[:, :, PACK - 1], in_=last[h][:].rearrange("a b (r c u e) -> a u b r c e", r=RUNS, u=2, e=2)[:, u])
-
-        def turn_back(b):
-            back = bank(PACK + b, [P, 2, P], "back%d" % b)
-            for u in range(2):
-                nc.tensor.transpose(back[:, u, :], zt[b // 2][:, b % 2, :].bitcast(F32)[:, u * P : (u + 1) * P], ident[:])
-            return back
-
-        def lay_z(copy, b, back):
+        def lay_z(copy, b):
             z_b = sb([P, PACK * P], BF16, "z_b%d" % b)
-            copy(out=z_b[:].bitcast(F32).rearrange("p (a u) -> p a u", u=2), in_=back[:].rearrange("p u a -> p a u"))
+            copy(out=z_b[:].bitcast(F32).rearrange("p (a u) -> p a u", u=2), in_=back[b][:].rearrange("p u a -> p a u"))
             return z_b
 
         def quantise_z(b, z_b):
@@ -307,18 +301,18 @@ def tile_picked_painn8_none_po_kernel(
                 )
             return acc
 
-        o_f = [sb([P, PACK, HALF], F32, "o_f%d" % h) for h in range(2)]
+        o_f = [sb([P, PACK, P], F32, "o_f%d" % b) for b in range(PACK)]
 
-        def leave(copy, b, acc):
-            part = o_f[b // 2][:, :, (b % 2) * P : (b % 2 + 1) * P]
+        def leave(copy, b, t0, acc):
+            part = o_f[b][:, t0 : t0 + acc.shape[1], :]
             copy(out=part, in_=acc[:])
-            nc.sync.dma_start(out=out_rows[:, :, b * P : (b + 1) * P], in_=part)
-            return part
+            nc.sync.dma_start(out=out_rows[:, t0 : t0 + acc.shape[1], b * P : (b + 1) * P], in_=part)
 
-        def interleave(b, values):
+        def interleave(b):
             rounded = sb([P, PACK * P], BF16, "o_b%d" % b)
-            nc.vector.tensor_copy(
-                out=rounded[:].rearrange("p (c a t) -> p c t a", a=4, t=PACK), in_=values.rearrange("p t (c a) -> p c t a", a=4)
+            on_v(
+                out=rounded[:].rearrange("p (c a t) -> p c t a", a=4, t=PACK),
+                in_=o_f[b][:].rearrange("p t (c a) -> p c t a", a=4),
             )
             return rounded
 
@@ -329,31 +323,29 @@ def tile_picked_painn8_none_po_kernel(
                 both = slice((b - 1) * P, (b + 1) * P)
                 nc.sync.dma_start(out=code_rows[:, both], in_=o_codes[:, both])
 
+        for h in range(2):
+            for b in range(2):
+                round_turned(on_v if h else on_s, 1, h, b, b + 1)
         for b in range(PACK):
-            round_turned(b)
-        round_last(on_s, 0)
-        round_last(on_v, 1)
-        back = [turn_back(b) for b in range(PACK)]
-        z = [lay_z(on_v if b == 2 else on_s, b, back[b]) for b in range(PACK)]
+            turn_back(1, b)
+        z = [lay_z(on_s, b) for b in range(PACK)]
         for b in range(PACK):
             quantise_z(b, z[b])
-        first = [multiply(0, 0, 2, 0), multiply(0, 2, PACK, PACK)]
-        acc1 = multiply(1, 0, PACK, 1)
-        acc2 = multiply(2, 0, PACK, 2)
-        acc3 = multiply(3, 0, PACK, 3)
-        o0 = o_f[0][:, :, :P]
-        for u in range(2):
-            on_s(out=o0[:, 2 * u : 2 * u + 2, :], in_=first[u][:])
-            nc.sync.dma_start(out=out_rows[:, 2 * u : 2 * u + 2, :P], in_=o0[:, 2 * u : 2 * u + 2, :])
-        o1 = leave(on_v, 1, acc1)
-        b0 = interleave(0, o0)
-        o2 = leave(on_s, 2, acc2)
-        b1 = interleave(1, o1)
+        first = [multiply(0, 0, 2, 4), multiply(0, 2, PACK, 5)]
+        acc1 = multiply(1, 0, PACK, 6)
+        acc2 = multiply(2, 0, PACK, 7)
+        acc3 = multiply(3, 0, PACK, 0)
+        leave(on_s, 0, 0, first[0])
+        leave(on_s, 0, 2, first[1])
+        leave(on_v, 1, 0, acc1)
+        b0 = interleave(0)
+        leave(on_s, 2, 0, acc2)
+        b1 = interleave(1)
         planes(0, b0)
-        o3 = leave(on_s, 3, acc3)
-        b2 = interleave(2, o2)
+        leave(on_s, 3, 0, acc3)
+        b2 = interleave(2)
         planes(1, b1)
-        b3 = interleave(3, o3)
+        b3 = interleave(3)
         planes(2, b2)
         planes(3, b3)
         for r in range(PACK):

@@ -158,7 +158,6 @@ def tile_picked_painn8_none_po_kernel(
 
         def gate(t):
             nc.vector.tensor_tensor(ye[t][:, :S], e_ps[t][:], ye[t][:, S:], MULT)
-            product(w1w_d[0][:, : 2 * P].bitcast(FP4X4), w1s_d[:, :P], "warm%d" % t, PACK + t)
 
         gate(0)
         gate(1)
@@ -255,9 +254,9 @@ def tile_picked_painn8_none_po_kernel(
         fetch_ye(3, 0, 11 * KB)
         fetch_q(2, 0)
         leave_q(3)
-        fetch_ye(3, 1, 13 * KB)
         fetch_q(2, 1)
         fetch_q(3, 0, None, 0, HALF)
+        fetch_ye(3, 1, 13 * KB)
         fetch_q(3, 1, None, 0, HALF)
         for h in range(2):
             round_turned(on_s, 0, h, 0, 2)
@@ -304,9 +303,10 @@ def tile_picked_painn8_none_po_kernel(
         o_f = [sb([P, PACK, P], F32, "o_f%d" % b) for b in range(PACK)]
 
         def leave(copy, b, t0, acc):
-            part = o_f[b][:, t0 : t0 + acc.shape[1], :]
-            copy(out=part, in_=acc[:])
-            nc.sync.dma_start(out=out_rows[:, t0 : t0 + acc.shape[1], b * P : (b + 1) * P], in_=part)
+            copy(out=o_f[b][:, t0 : t0 + acc.shape[1], :], in_=acc[:])
+
+        def store(b, t0, t1):
+            nc.sync.dma_start(out=out_rows[:, t0:t1, b * P : (b + 1) * P], in_=o_f[b][:, t0:t1, :])
 
         def interleave(b):
             rounded = sb([P, PACK * P], BF16, "o_b%d" % b)
@@ -334,15 +334,21 @@ def tile_picked_painn8_none_po_kernel(
         first = [multiply(0, 0, 2, 4), multiply(0, 2, PACK, 5)]
         acc1 = multiply(1, 0, PACK, 6)
         acc2 = multiply(2, 0, PACK, 7)
-        acc3 = multiply(3, 0, PACK, 0)
+        last = [multiply(3, 0, 2, 0), multiply(3, 2, PACK, 1)]
         leave(on_s, 0, 0, first[0])
+        store(0, 0, 2)
         leave(on_s, 0, 2, first[1])
+        store(0, 2, PACK)
         leave(on_v, 1, 0, acc1)
+        store(1, 0, PACK)
         b0 = interleave(0)
         leave(on_s, 2, 0, acc2)
+        store(2, 0, PACK)
         b1 = interleave(1)
         planes(0, b0)
-        leave(on_s, 3, 0, acc3)
+        leave(on_s, 3, 0, last[0])
+        leave(on_s, 3, 2, last[1])
+        store(3, 0, PACK)
         b2 = interleave(2)
         planes(1, b1)
         b3 = interleave(3)

@@ -171,7 +171,7 @@ def tile_picked_painn8_none_po_kernel(
         w3_q = quantise(w3_b[:, :H], sb([P, P], U32, "w3_c0"), sb([P, P], U8, "w3_s0"))
         w3_q = w3_q + quantise(w3_b[:, H : 2 * H], at(9 * KB, [P, P], U32, "w3_c1"), sb([P, P], U8, "w3_s1"))
         w3_q = w3_q + quantise(w3_b[:, 2 * H :], at(19 * KB - 512, [P, HALF], U32, "w3_c23"), at(13 * KB - 128, [P, HALF], U8, "w3_s23"))
-        q_ps = [weight_product(w3_q[t], "q%d" % t, t) for t in range(PACK)]
+        q_ps = [weight_product(w3_q[t], "q%d" % t, t % 2) for t in range(PACK)]
         gate(2)
         gate(3)
         ident = at(28 * KB, [P, P], F32, "ident")

@@ -62,7 +62,7 @@ def tile_picked_painn8_none_po_kernel(
         o_codes = sb([P, S], I32, "o_codes")
         d1 = at(32 * KB, [P, S], F32, "d1")
         d2 = sb([P, S], F32, "d2")
-        w2_raw = [sb([P, PACK, HALF], F32, "w2_raw0"), at(24 * KB, [P, PACK, HALF], F32, "w2_raw1")]
+        w2_raw = [sb([P, PACK, HALF], F32, "w2_raw0"), at(52 * KB, [P, PACK, HALF], F32, "w2_raw1")]
         w3_raw = [sb([P, PACK, HALF], F32, "w3_raw0"), at(28 * KB, [P, PACK, HALF], F32, "w3_raw1")]
 
         nc.gpsimd.memset(xs[:].bitcast(I32), 0)
@@ -119,17 +119,19 @@ def tile_picked_painn8_none_po_kernel(
             )
             return acc
 
-        ye = [sb([P, 2 * S], F32, "ye%d" % t) for t in range(PACK)]
+        ye = [at(53 * KB, [P, 2 * S], F32, "ye0"), at(48 * KB + 256, [P, 2 * S], F32, "ye1")]
+        ye = ye + [sb([P, 2 * S], F32, "ye2"), at(68 * KB + 512, [P, 2 * S], F32, "ye3")]
+        y_sb = [ye[t][:, S:] for t in range(3)] + [sb([P, S], F32, "y3")[:]]
 
         def y_tile(t):
             words = w1w_d[t // 2][:, (t % 2) * 2 * P : (t % 2 + 1) * 2 * P]
             acc = product(words.bitcast(FP4X4), w1s_d[:, t * P : (t + 1) * P], "y%d" % t, t)
-            on_s(out=ye[t][:, S:], in_=acc[:])
+            on_s(out=y_sb[t], in_=acc[:])
 
-        def round_views(raw, rounded, h, s):
+        def round_views(raw, rounded, h, u):
             return dict(
-                out=rounded[:].rearrange("p (u s h n e j) -> p h s n j u e", u=2, s=2, h=2, e=2, j=PACK)[:, h, s],
-                in_=raw[h][:].rearrange("p j (n s u e) -> p s n j u e", s=2, u=2, e=2)[:, s],
+                out=rounded[u][:].rearrange("p (s h n e j) -> p h n j s e", s=2, h=2, e=2, j=PACK)[:, h],
+                in_=raw[h][:].rearrange("p j (n s u e) -> p u n j s e", s=2, u=2, e=2)[:, u],
             )
 
         def quantise(rounded, codes, scales):
@@ -139,45 +141,56 @@ def tile_picked_painn8_none_po_kernel(
         def weight_product(quantised, name, number):
             return product(quantised[0].bitcast(FP8X4), quantised[1], name, number)
 
-        w2_b = sb([P, PACK * H], BF16, "w2_b")
+        w2_b = [sb([P, 2 * H], BF16, "w2_b%d" % u) for u in range(2)]
         on_s(**round_views(w2_raw, w2_b, 0, 0))
         on_s(**round_views(w2_raw, w2_b, 0, 1))
+        on_v(**round_views(w2_raw, w2_b, 1, 0))
+        on_s(**round_views(w2_raw, w2_b, 1, 1))
         y_tile(0)
         y_tile(1)
-        on_v(**round_views(w2_raw, w2_b, 1, 0))
-        on_v(**round_views(w2_raw, w2_b, 1, 1))
-        w2_q = quantise(w2_b[:, :H], at(KB - 256, [P, P], U32, "w2_c0"), at(3 * KB - 64, [P, P], U8, "w2_s0"))
-        w2_q = w2_q + quantise(w2_b[:, H : 2 * H], sb([P, P], U32, "w2_c1"), sb([P, P], U8, "w2_s1"))
-        w1w_d.append(deal_words(1, at(24 * KB, [P, H], U8, "w1w_d1")))
-        w2_q = w2_q + quantise(w2_b[:, 2 * H :], sb([P, HALF], U32, "w2_c23"), sb([P, HALF], U8, "w2_s23"))
+        w2_q = quantise(w2_b[0][:, :H], at(73 * KB - 256, [P, P], U32, "w2_c0"), at(3 * KB - 64, [P, P], U8, "w2_s0"))
+        w2_q = w2_q + quantise(w2_b[0][:, H:], sb([P, P], U32, "w2_c1"), sb([P, P], U8, "w2_s1"))
+        w1w_d.append(deal_words(1, at(52 * KB + 512, [P, H], U8, "w1w_d1")))
+        w2_q = w2_q + quantise(w2_b[1][:], sb([P, HALF], U32, "w2_c23"), sb([P, HALF], U8, "w2_s23"))
         e_ps = [weight_product(w2_q[0], "e0", PACK)]
         y_tile(2)
         e_ps.append(weight_product(w2_q[1], "e1", PACK + 1))
         y_tile(3)
-        e_ps = e_ps + [weight_product(w2_q[t], "e%d" % t, PACK + t) for t in (2, 3)]
+        e_ps = e_ps + [weight_product(w2_q[2], "e2", PACK + 2), weight_product(w2_q[3], "e3", PACK + 3)]
 
         def gate(t):
-            nc.vector.tensor_tensor(ye[t][:, :S], e_ps[t][:], ye[t][:, S:], MULT)
+            nc.vector.tensor_tensor(ye[t][:, :S], e_ps[t][:], y_sb[t], MULT)
 
         gate(0)
         gate(1)
-        w3_b = at(0, [P, PACK * H], BF16, "w3_b")
-        for t in range(PACK):
-            views = round_views(w3_raw, w3_b, 0, t % 2)
-            out, in_ = (views[side][:, :, :, t // 2].rearrange("p n j e -> p n e j") for side in ("out", "in_"))
-            nc.gpsimd.tensor_scalar(out, in_, 1.0, 0.0, op0=MULT, op1=ADD)
-        on_v(**round_views(w3_raw, w3_b, 1, 0))
-        on_v(**round_views(w3_raw, w3_b, 1, 1))
-        w3_q = quantise(w3_b[:, :H], sb([P, P], U32, "w3_c0"), sb([P, P], U8, "w3_s0"))
-        w3_q = w3_q + quantise(w3_b[:, H : 2 * H], at(9 * KB, [P, P], U32, "w3_c1"), sb([P, P], U8, "w3_s1"))
-        w3_q = w3_q + quantise(w3_b[:, 2 * H :], at(19 * KB - 512, [P, HALF], U32, "w3_c23"), at(13 * KB - 128, [P, HALF], U8, "w3_s23"))
-        q_ps = [weight_product(w3_q[t], "q%d" % t, t % 2) for t in range(PACK)]
         gate(2)
+        w3_b01 = [at((72 + t) * KB, [P, H], BF16, "w3_b%d" % t) for t in range(2)]
+        w3_b23 = at(2 * KB, [P, 2 * H], BF16, "w3_b23")
+        w3_b = [w3_b01[0][:], w3_b01[1][:], w3_b23[:, :H], w3_b23[:, H:]]
+
+        def tile_views(t, h, order):
+            u, s = divmod(t, 2)
+            return dict(
+                out=w3_b[t].rearrange("p (h n e j) -> p h %s" % order, h=2, e=2, j=PACK)[:, h],
+                in_=w3_raw[h][:].rearrange("p j (n s u e) -> p s u %s" % order, s=2, u=2, e=2)[:, s, u],
+            )
+
+        for t, h in [(t, 0) for t in range(PACK)] + [(2, 1), (3, 1)]:
+            views = tile_views(t, h, "n e j")
+            nc.gpsimd.tensor_scalar(views["out"], views["in_"], 1.0, 0.0, op0=MULT, op1=ADD)
+        on_v(**tile_views(0, 1, "n j e"))
+        on_v(**tile_views(1, 1, "n j e"))
+        w3_q = quantise(w3_b[0], sb([P, P], U32, "w3_c0"), sb([P, P], U8, "w3_s0"))
+        w3_q = w3_q + quantise(w3_b[1], at(9 * KB, [P, P], U32, "w3_c1"), sb([P, P], U8, "w3_s1"))
+        q_ps = [weight_product(w3_q[t], "q%d" % t, t) for t in range(2)]
         gate(3)
+        on_v(out=q_sb[0][:, :S], in_=q_ps[0][:])
+        w3_q = w3_q + quantise(w3_b23[:], at(19 * KB - 512, [P, HALF], U32, "w3_c23"), at(13 * KB - 128, [P, HALF], U8, "w3_s23"))
+        q_ps = q_ps + [weight_product(w3_q[t], "q%d" % t, t % 2) for t in (2, 3)]
         ident = at(28 * KB, [P, P], F32, "ident")
         make_identity(nc, ident[:])
 
-        w4s_d = at(2 * KB + 512, [P, N], U8, "w4s_d")
+        w4s_d = at(73 * KB + 512, [P, N], U8, "w4s_d")
         on_v(out=w4s_d[:].rearrange("p (t m) -> p t m", t=PACK), in_=w4s[:].rearrange("p (m t) -> p t m", t=PACK))
         for r in range(1, PACK):
             nc.sync.dma_start(out=w4s_d[r:P:QUADRANT, :].bitcast(I32), in_=w4s_d[8 * r : P : QUADRANT, :].bitcast(I32))
@@ -214,7 +227,7 @@ def tile_picked_painn8_none_po_kernel(
             turn(t, term[:], j0)
 
         def fetch_q(t, i, offset=None, j0=0, n=S):
-            term = term_tile("q", t, i, j0, n, offset)
+            term = ye[3][:, S:] if (t, i) == (0, 0) else term_tile("q", t, i, j0, n, offset)
             nc.vector.tensor_tensor(term[:], q_sb[t][:].indirect(entries(i, j0, n)), dirs[i][:, j0 : j0 + n], MULT)
             turn(t, term[:], j0)
 
@@ -236,11 +249,10 @@ def tile_picked_painn8_none_po_kernel(
             nc.tensor.transpose(back[b][:, u, :], zt[u][b], ident[:])
 
         def leave_q(t):
-            (on_s if t else on_v)(out=q_sb[t][:, :S], in_=q_ps[t][:])
+            on_s(out=q_sb[t][:, :S], in_=q_ps[t][:])
 
         fetch_ye(0, 0)
         fetch_ye(0, 1)
-        leave_q(0)
         fetch_ye(1, 0)
         fetch_q(0, 0)
         leave_q(1)
@@ -251,19 +263,21 @@ def tile_picked_painn8_none_po_kernel(
         leave_q(2)
         fetch_ye(2, 1, 19 * KB)
         fetch_q(1, 1)
+        leave_q(3)
         fetch_ye(3, 0, 11 * KB)
         fetch_q(2, 0)
-        leave_q(3)
         fetch_q(2, 1)
         fetch_q(3, 0, None, 0, HALF)
         fetch_ye(3, 1, 13 * KB)
         fetch_q(3, 1, None, 0, HALF)
-        for h in range(2):
-            round_turned(on_s, 0, h, 0, 2)
-        for b in range(PACK):
+        round_turned(on_s, 0, 0, 0, 2)
+        round_turned(on_s, 0, 1, 0, 1)
+        for b in range(3):
             turn_back(0, b)
         for i in range(2):
             fetch_q(3, i, None, HALF, HALF)
+        round_turned(on_v, 0, 1, 1, 2)
+        turn_back(0, 3)
 
         w4w_d = at(32 * KB, [P, 2 * N], U8, "w4w_d")
         on_v(

@@ -175,14 +175,15 @@ def tile_picked_painn8_none_po_kernel(
                 in_=w3_raw[h][:].rearrange("p j (n s u e) -> p s u %s" % order, s=2, u=2, e=2)[:, s, u],
             )
 
-        for t, h in [(t, 0) for t in range(PACK)] + [(2, 1), (3, 1)]:
-            views = tile_views(t, h, "n e j")
+        for t in range(PACK):
+            views = tile_views(t, 0, "n e j")
             nc.gpsimd.tensor_scalar(views["out"], views["in_"], 1.0, 0.0, op0=MULT, op1=ADD)
         on_v(**tile_views(0, 1, "n j e"))
         on_v(**tile_views(1, 1, "n j e"))
         w3_q = quantise(w3_b[0], sb([P, P], U32, "w3_c0"), sb([P, P], U8, "w3_s0"))
         w3_q = w3_q + quantise(w3_b[1], at(9 * KB, [P, P], U32, "w3_c1"), sb([P, P], U8, "w3_s1"))
         q_ps = [weight_product(w3_q[t], "q%d" % t, t) for t in range(2)]
+        on_v(**round_views(w3_raw, [None, w3_b23], 1, 1))
         gate(3)
         on_v(out=q_sb[0][:, :S], in_=q_ps[0][:])
         w3_q = w3_q + quantise(w3_b23[:], at(19 * KB - 512, [P, HALF], U32, "w3_c23"), at(13 * KB - 128, [P, HALF], U8, "w3_s23"))

from contextlib import ExitStack

import concourse.mybir as mybir
from concourse.masks import make_identity

K, T, S, H, N = 512, 2048, 512, 512, 512
FLOPS = 3 * 2 * K * H * S + 2 * H * N * S

F32 = mybir.dt.float32
BF16 = mybir.dt.bfloat16
I32 = mybir.dt.int32
U32 = mybir.dt.uint32
U16 = mybir.dt.uint16
U8 = mybir.dt.uint8
FP8X4 = mybir.dt.float8_e4m3fn_x4
FP4X4 = mybir.dt.float4_e2m1fn_x4
MULT = mybir.AluOpType.mult
ADD = mybir.AluOpType.add
COPY = mybir.ActivationFunctionType.Copy

P = 128
PACK = 4
HALF = 256
PER_COLUMN = 16
QUADRANT = 32
BLOCKS = K // 32
KB = 1024


def tile_picked_painn8_none_po_kernel(
    tc, x_words, x_scales, w1_words, w1_scales, w2, w3, dir1, dir2, w4_words, w4_scales, offs, p1, p2, out_0, out_1, out_2
):
    nc = tc.nc
    with ExitStack() as ctx:
        keep = ctx.enter_context(tc.tile_pool(name="keep", bufs=1))
        placed = ctx.enter_context(tc.tile_pool(name="placed", bufs=1))
        psum = ctx.enter_context(tc.psum_pool(name="psum", bufs=1))

        def bank(number, shape, name):
            return psum.tile(shape, F32, name=name, tag="bank%d" % number)

        def sb(shape, dtype, name):
            return keep.tile(shape, dtype, name=name, align_bytes=64)

        def at(offset, shape, dtype, name):
            return placed.tile(shape, dtype, name=name, offset=offset, align_bytes=64)

        def place_scale_rows(plane, rows):
            for r in range(PACK):
                nc.sync.dma_start(out=plane[r:P:QUADRANT, :].bitcast(I32), in_=rows[r:BLOCKS:PACK, :].bitcast(I32))

        offs_sb = keep.tile([P, S // PER_COLUMN], U16, name="offs_sb")
        p1_sb = keep.tile([P, S // PER_COLUMN], U16, name="p1_sb")
        p2_sb = keep.tile([P, S // PER_COLUMN], U16, name="p2_sb")
        xw = sb([P, T], I32, "xw")
        xs = sb([P, T], U8, "xs")
        w1w = sb([P, 2 * H], U8, "w1w")
        w4w = sb([P, 2 * N], U8, "w4w")
        w1s = sb([P, H], U8, "w1s")
        w4s = sb([P, N], U8, "w4s")
        o_scales = sb([P, S], U8, "o_scales")
        o_codes = sb([P, S], I32, "o_codes")
        d1 = at(32 * KB, [P, S], F32, "d1")
        d2 = sb([P, S], F32, "d2")
        w2_raw = [sb([P, PACK, HALF], F32, "w2_raw0"), at(52 * KB, [P, PACK, HALF], F32, "w2_raw1")]
        w3_raw = [sb([P, PACK, HALF], F32, "w3_raw0"), at(28 * KB, [P, PACK, HALF], F32, "w3_raw1")]

        nc.gpsimd.memset(xs[:].bitcast(I32), 0)
        nc.gpsimd.memset(w4s[:].bitcast(I32), 0)
        nc.gpsimd.memset(w1s[:].bitcast(I32), 0)
        q_sb = [sb([P, 2 * S], F32, "q_sb%d" % t) for t in range(PACK)]
        for t in range(PACK):
            nc.gpsimd.memset(q_sb[t][:, S:], 0.0)

        x_rows = x_words[0].rearrange("p n t -> p (n t)").bitcast(I32)
        w2_rows = w2.rearrange("(p j) c -> p j c", j=PACK)
        w3_rows = w3.rearrange("(p j) c -> p j c", j=PACK)
        nc.sync.dma_start(out=xw[:, : T // 2], in_=x_rows[:, : T // 2])
        nc.sync.dma_start(offs_sb[:], offs)
        place_scale_rows(xs, x_scales[0])
        nc.sync.dma_start(out=xw[:, T // 2 :], in_=x_rows[:, T // 2 :])
        nc.sync.dma_start(out=w2_raw[0][:], in_=w2_rows[:, :, :HALF])
        nc.sync.dma_start(out=w1w[:].bitcast(I32), in_=w1_words[0].bitcast(I32))
        place_scale_rows(w1s, w1_scales[0])
        nc.sync.dma_start(out=w2_raw[1][:], in_=w2_rows[:, :, HALF:])
        nc.sync.dma_start(out=w3_raw[0][:], in_=w3_rows[:, :, :HALF])
        nc.sync.dma_start(p1_sb[:], p1)
        nc.sync.dma_start(p2_sb[:], p2)
        nc.sync.dma_start(out=w3_raw[1][:], in_=w3_rows[:, :, HALF:])
        nc.sync.dma_start(out=d1[:], in_=dir1)
        nc.sync.dma_start(out=d2[:], in_=dir2)
        nc.sync.dma_start(out=w4s[0:P:8, :].bitcast(I32), in_=w4_scales[0].bitcast(I32))
        nc.sync.dma_start(out=w4w[:].bitcast(I32), in_=w4_words[0].bitcast(I32))

        on_s, on_v = nc.scalar.copy, nc.vector.tensor_copy
        xq_s = sb([P, S], U8, "xq_s")
        xq = sb([P, S], U32, "xq")
        on_v(xq_s[:], xs[:].indirect(offs_sb[:]))
        on_v(xq[:], xw[:].bitcast(U32).indirect(offs_sb[:]))

        def deal_words(u, dealt):
            on_v(
                out=dealt[:].bitcast(I32).rearrange("p (s n) -> p s n", s=2),
                in_=w1w[:].bitcast(I32).rearrange("p (n s u) -> p u s n", s=2, u=2)[:, u],
            )
            return dealt

        w1w_d = [deal_words(0, sb([P, H], U8, "w1w_d0"))]
        w1s_d = sb([P, H], U8, "w1s_d")
        on_v(
            out=w1s_d[:].bitcast(U16).rearrange("p (u s n) -> p u s n", u=2, s=2),
            in_=w1s[:].bitcast(U16).rearrange("p (n s u) -> p u s n", s=2, u=2),
        )

        def product(lhsT, lhsT_scale, name, number):
            acc = bank(number, [P, S], name)
            nc.tensor.matmul_mx(
                out=acc[:], lhsT=lhsT, lhsT_scale=lhsT_scale, rhs=xq[:].bitcast(FP8X4), rhs_scale=xq_s[:], start=True, stop=True
            )
            return acc

        ye = [at(53 * KB, [P, 2 * S], F32, "ye0"), at(48 * KB + 256, [P, 2 * S], F32, "ye1")]
        ye = ye + [sb([P, 2 * S], F32, "ye2"), at(68 * KB + 512, [P, 2 * S], F32, "ye3")]
        y_sb = [ye[t][:, S:] for t in range(3)] + [sb([P, S], F32, "y3")[:]]

        def y_tile(t):
            words = w1w_d[t // 2][:, (t % 2) * 2 * P : (t % 2 + 1) * 2 * P]
            acc = product(words.bitcast(FP4X4), w1s_d[:, t * P : (t + 1) * P], "y%d" % t, t)
            on_s(out=y_sb[t], in_=acc[:])

        def round_views(raw, rounded, h, u):
            return dict(
                out=rounded[u][:].rearrange("p (s h n e j) -> p h n j s e", s=2, h=2, e=2, j=PACK)[:, h],
                in_=raw[h][:].rearrange("p j (n s u e) -> p u n j s e", s=2, u=2, e=2)[:, u],
            )

        def quantise(rounded, codes, scales):
            nc.vector.quantize_mx(out=codes[:].bitcast(FP8X4), scales=scales[:], in_=rounded)
            return [(codes[:, c : c + P], scales[:, c : c + P]) for c in range(0, codes.shape[1], P)]

        def weight_product(quantised, name, number):
            return product(quantised[0].bitcast(FP8X4), quantised[1], name, number)

        w2_b = [sb([P, 2 * H], BF16, "w2_b%d" % u) for u in range(2)]
        on_s(**round_views(w2_raw, w2_b, 0, 0))
        on_s(**round_views(w2_raw, w2_b, 0, 1))
        on_v(**round_views(w2_raw, w2_b, 1, 0))
        on_s(**round_views(w2_raw, w2_b, 1, 1))
        y_tile(0)
        y_tile(1)
        w2_q = quantise(w2_b[0][:, :H], at(73 * KB - 256, [P, P], U32, "w2_c0"), at(3 * KB - 64, [P, P], U8, "w2_s0"))
        w2_q = w2_q + quantise(w2_b[0][:, H:], sb([P, P], U32, "w2_c1"), sb([P, P], U8, "w2_s1"))
        w1w_d.append(deal_words(1, at(52 * KB + 512, [P, H], U8, "w1w_d1")))
        w2_q = w2_q + quantise(w2_b[1][:], sb([P, HALF], U32, "w2_c23"), sb([P, HALF], U8, "w2_s23"))
        e_ps = [weight_product(w2_q[0], "e0", PACK)]
        y_tile(2)
        e_ps.append(weight_product(w2_q[1], "e1", PACK + 1))
        y_tile(3)
        e_ps = e_ps + [weight_product(w2_q[2], "e2", PACK + 2), weight_product(w2_q[3], "e3", PACK + 3)]

        def gate(t):
            nc.vector.tensor_tensor(ye[t][:, :S], e_ps[t][:], y_sb[t], MULT)

        gate(0)
        gate(1)
        gate(2)
        w3_b01 = [at((72 + t) * KB, [P, H], BF16, "w3_b%d" % t) for t in range(2)]
        w3_b23 = at(2 * KB, [P, 2 * H], BF16, "w3_b23")
        w3_b = [w3_b01[0][:], w3_b01[1][:], w3_b23[:, :H], w3_b23[:, H:]]

        def tile_views(t, h, order):
            u, s = divmod(t, 2)
            return dict(
                out=w3_b[t].rearrange("p (h n e j) -> p h %s" % order, h=2, e=2, j=PACK)[:, h],
                in_=w3_raw[h][:].rearrange("p j (n s u e) -> p s u %s" % order, s=2, u=2, e=2)[:, s, u],
            )

        for t in range(PACK):
            views = tile_views(t, 0, "n e j")
            nc.gpsimd.tensor_scalar(views["out"], views["in_"], 1.0, 0.0, op0=MULT, op1=ADD)
        on_v(**tile_views(0, 1, "n j e"))
        on_v(**tile_views(1, 1, "n j e"))
        w3_q = quantise(w3_b[0], sb([P, P], U32, "w3_c0"), sb([P, P], U8, "w3_s0"))
        w3_q = w3_q + quantise(w3_b[1], at(9 * KB, [P, P], U32, "w3_c1"), sb([P, P], U8, "w3_s1"))
        q_ps = [weight_product(w3_q[t], "q%d" % t, t) for t in range(2)]
        on_v(**round_views(w3_raw, [None, w3_b23], 1, 1))
        gate(3)
        on_v(out=q_sb[0][:, :S], in_=q_ps[0][:])
        w3_q = w3_q + quantise(w3_b23[:], at(19 * KB - 512, [P, HALF], U32, "w3_c23"), at(13 * KB - 128, [P, HALF], U8, "w3_s23"))
        q_ps = q_ps + [weight_product(w3_q[t], "q%d" % t, t % 2) for t in (2, 3)]
        ident = at(28 * KB, [P, P], F32, "ident")
        make_identity(nc, ident[:])

        w4s_d = at(73 * KB + 512, [P, N], U8, "w4s_d")
        on_v(out=w4s_d[:].rearrange("p (t m) -> p t m", t=PACK), in_=w4s[:].rearrange("p (m t) -> p t m", t=PACK))
        for r in range(1, PACK):
            nc.sync.dma_start(out=w4s_d[r:P:QUADRANT, :].bitcast(I32), in_=w4s_d[8 * r : P : QUADRANT, :].bitcast(I32))

        lists = (p1_sb, p2_sb)
        dirs = (d1, d2)
        turned = [[bank(PACK + 2 * u + h, [P, 2, 2, P], "turned%d_%d" % (u, h)) for h in range(2)] for u in range(2)]
        left = [[16, 16], [16, 16]]

        def turn(t, term, j0):
            u, s = divmod(t, 2)
            for c in range(term.shape[1] // P):
                h, b = divmod(j0 // P + c, 2)
                nc.tensor.matmul(
                    turned[u][h][:, b, s, :],
                    term[:, c * P : (c + 1) * P],
                    ident[:],
                    start=left[u][h] == 16,
                    stop=left[u][h] == 1,
                    is_transpose=True,
                )
                left[u][h] = left[u][h] - 1

        def entries(i, j0, n):
            return lists[i][:, j0 // PER_COLUMN : (j0 + n) // PER_COLUMN]

        def term_tile(kind, t, i, j0, n, offset):
            name = "%s_term%d_%d_%d" % (kind, t, i, j0)
            return sb([P, n], F32, name) if offset is None else at(offset, [P, n], F32, name)

        def fetch_ye(t, i, offset=None, j0=0, n=S):
            term = term_tile("ye", t, i, j0, n, offset)
            nc.scalar.activation(term[:], ye[t][:].indirect(entries(i, j0, n)), COPY)
            turn(t, term[:], j0)

        def fetch_q(t, i, offset=None, j0=0, n=S):
            term = ye[3][:, S:] if (t, i) == (0, 0) else term_tile("q", t, i, j0, n, offset)
            nc.vector.tensor_tensor(term[:], q_sb[t][:].indirect(entries(i, j0, n)), dirs[i][:, j0 : j0 + n], MULT)
            turn(t, term[:], j0)

        zt = [[None] * PACK, [None] * PACK]
        back = [bank(b, [P, 2, P], "back%d" % b) for b in range(PACK)]

        def round_turned(copy, u, h, b0, b1, offset=None):
            name = "zt%d_%d_%d" % (u, h, b0)
            shape = [P, b1 - b0, 2 * P]
            words = sb(shape, BF16, name) if offset is None else at(offset, shape, BF16, name)
            copy(
                out=words[:].rearrange("a b (n s e) -> a b n s e", s=2, e=2),
                in_=turned[u][h][:, b0:b1].rearrange("a b s (n e) -> a b n s e", e=2),
            )
            for b in range(b0, b1):
                zt[u][2 * h + b] = words[:, b - b0, :].bitcast(F32)

        def turn_back(u, b):
            nc.tensor.transpose(back[b][:, u, :], zt[u][b], ident[:])

        def leave_q(t):
            on_s(out=q_sb[t][:, :S], in_=q_ps[t][:])

        fetch_ye(0, 0)
        fetch_ye(0, 1)
        fetch_ye(1, 0)
        fetch_q(0, 0)
        leave_q(1)
        fetch_ye(1, 1, 9 * KB)
        fetch_q(0, 1)
        fetch_ye(2, 0, 17 * KB)
        fetch_q(1, 0)
        leave_q(2)
        fetch_ye(2, 1, 19 * KB)
        fetch_q(1, 1)
        leave_q(3)
        fetch_ye(3, 0, 11 * KB)
        fetch_q(2, 0)
        fetch_q(2, 1)
        fetch_q(3, 0, None, 0, HALF)
        fetch_ye(3, 1, 13 * KB)
        fetch_q(3, 1, None, 0, HALF)
        round_turned(on_s, 0, 0, 0, 2)
        round_turned(on_s, 0, 1, 0, 1)
        for b in range(3):
            turn_back(0, b)
        for i in range(2):
            fetch_q(3, i, None, HALF, HALF)
        round_turned(on_v, 0, 1, 1, 2)
        turn_back(0, 3)

        w4w_d = at(32 * KB, [P, 2 * N], U8, "w4w_d")
        on_v(
            out=w4w_d[:].bitcast(U16).rearrange("p (t m) -> p t m", t=PACK),
            in_=w4w[:].bitcast(U16).rearrange("p (m t) -> p t m", t=PACK),
        )

        out_rows = out_0.rearrange("(p t) j -> p t j", t=PACK)
        code_rows = out_1[0].rearrange("p n t -> p (n t)").bitcast(I32)
        z_c = sb([P, S], U32, "z_c")
        z_s = sb([P, S], U8, "z_s")

        def lay_z(copy, b):
            z_b = sb([P, PACK * P], BF16, "z_b%d" % b)
            copy(out=z_b[:].bitcast(F32).rearrange("p (a u) -> p a u", u=2), in_=back[b][:].rearrange("p u a -> p a u"))
            return z_b

        def quantise_z(b, z_b):
            cols = slice(b * P, (b + 1) * P)
            nc.vector.quantize_mx(out=z_c[:, cols].bitcast(FP8X4), scales=z_s[:, cols], in_=z_b[:])

        def multiply(b, t0, t1, number):
            cols = slice(b * P, (b + 1) * P)
            acc = bank(number, [P, t1 - t0, P], "o%d_%d" % (b, t0))
            for t in range(t0, t1):
                nc.tensor.matmul_mx(
                    out=acc[:, t - t0, :],
                    lhsT=w4w_d[:, 2 * t * P : 2 * (t + 1) * P].bitcast(FP4X4),
                    lhsT_scale=w4s_d[:, t * P : (t + 1) * P],
                    rhs=z_c[:, cols].bitcast(FP8X4),
                    rhs_scale=z_s[:, cols],
                    start=True,
                    stop=True,
                )
            return acc

        o_f = [sb([P, PACK, P], F32, "o_f%d" % b) for b in range(PACK)]

        def leave(copy, b, t0, acc):
            copy(out=o_f[b][:, t0 : t0 + acc.shape[1], :], in_=acc[:])

        def store(b, t0, t1):
            nc.sync.dma_start(out=out_rows[:, t0:t1, b * P : (b + 1) * P], in_=o_f[b][:, t0:t1, :])

        def interleave(b):
            rounded = sb([P, PACK * P], BF16, "o_b%d" % b)
            on_v(
                out=rounded[:].rearrange("p (c a t) -> p c t a", a=4, t=PACK),
                in_=o_f[b][:].rearrange("p t (c a) -> p c t a", a=4),
            )
            return rounded

        def planes(b, o_b):
            cols = slice(b * P, (b + 1) * P)
            nc.vector.quantize_mx(out=o_codes[:, cols].bitcast(FP8X4), scales=o_scales[:, cols], in_=o_b[:])
            if b % 2:
                both = slice((b - 1) * P, (b + 1) * P)
                nc.sync.dma_start(out=code_rows[:, both], in_=o_codes[:, both])

        for h in range(2):
            for b in range(2):
                round_turned(on_v if h else on_s, 1, h, b, b + 1)
        for b in range(PACK):
            turn_back(1, b)
        z = [lay_z(on_s, b) for b in range(PACK)]
        for b in range(PACK):
            quantise_z(b, z[b])
        first = [multiply(0, 0, 2, 4), multiply(0, 2, PACK, 5)]
        acc1 = multiply(1, 0, PACK, 6)
        acc2 = multiply(2, 0, PACK, 7)
        last = [multiply(3, 0, 2, 0), multiply(3, 2, PACK, 1)]
        leave(on_s, 0, 0, first[0])
        store(0, 0, 2)
        leave(on_s, 0, 2, first[1])
        store(0, 2, PACK)
        leave(on_v, 1, 0, acc1)
        store(1, 0, PACK)
        b0 = interleave(0)
        leave(on_s, 2, 0, acc2)
        store(2, 0, PACK)
        b1 = interleave(1)
        planes(0, b0)
        leave(on_s, 3, 0, last[0])
        leave(on_s, 3, 2, last[1])
        store(3, 0, PACK)
        b2 = interleave(2)
        planes(1, b1)
        b3 = interleave(3)
        planes(2, b2)
        planes(3, b3)
        for r in range(PACK):
            queue = nc.scalar if r % 2 else nc.sync
            queue.dma_start(out=out_2[0, r:BLOCKS:PACK, :].bitcast(I32), in_=o_scales[r:P:QUADRANT, :].bitcast(I32))
